import numpy as np, ml_dtypes
CORES = [40,64,80,88,96,104,120,144]
N = 8
BF = ml_dtypes.bfloat16
def gentries(a):
    return np.ascontiguousarray(a.reshape(8, 16, -1).transpose(0, 2, 1)).reshape(8, -1)
def gtable(e):
    e = np.asarray(e); return np.ascontiguousarray(e.reshape(8, -1, 16).transpose(0, 2, 1)).reshape(128, -1).astype(np.int32)
R0, P0, S, L, RO = 3584, 288, 16, 12, 2
P = P0 + RO * S; R = R0 + RO * (N - 1) * S
def counts(rng, share):
    return np.where(rng.random((N, 8, P0)) < share, rng.integers(L, 17, (N, 8, P0)), rng.integers(1, L, (N, 8, P0)))
def world(rng, cnt):
    post = rng.integers(0, R0, (N, 8, P0, 16)); home = np.full((N, 8, R0), 65535)
    on = np.argsort(rng.random((N, 8, P0, 16)), axis=-1) < cnt[..., None]
    for q in range(N):
        for g in range(8):
            ix = np.flatnonzero(on[q, g])[:R0]; c = rng.permutation(R0); n = len(ix)
            post[q, g].reshape(-1)[ix] = c[:n]; home[q, g, c[:n]] = ix
            if n: home[q, g, c[n:]] = np.where(rng.random(R0 - n) < 0.5, 65535, ix[rng.integers(0, n, R0 - n)])
    cl = rng.integers(0, 24, (N, 8, P0)); pr = rng.integers(40, 200, (8, 24, 14)); gi = np.arange(8)[None, :, None]
    at = np.minimum(home >> 4, P0 - 1)
    kc = np.where(home == 65535, rng.integers(0, 24, home.shape), np.take_along_axis(cl, at, 2))
    x = np.clip(pr[gi, kc] + rng.integers(-40, 41, (N, 8, R0, 14)), 0, 255)
    cen = rng.integers(0, 256, (N, 8, P0, 16)); cen[..., :14] = pr[gi, cl] + rng.integers(-16, 17, (N, 8, P0, 14))
    m = N * P0; w = m // 24; od = np.argsort(cl.transpose(1, 0, 2).reshape(8, m) + rng.random((8, m)), axis=1); pos = np.argsort(od, axis=1)
    z = np.take_along_axis(od, ((pos[:, :, None] + rng.integers(-w, w + 1, (8, m, 16))) % m).reshape(8, 16 * m), 1)
    near = (P * (z // P0) + z % P0).reshape(8, N, P0, 16).transpose(1, 0, 2, 3)
    near = np.where(rng.random(near.shape) < 0.15, rng.integers(0, N * P, near.shape), near)
    sl = 16 * at[:, :, None, :] + rng.integers(0, 16, (N, 8, RO, R0))
    ab = np.take_along_axis(post.reshape(N, 8, 16 * P0), sl.reshape(N, 8, RO * R0), 2).reshape(N, 8, RO, R0); u = rng.random(ab.shape)
    ab = np.where(u < 0.3, np.arange(R0), np.where(u < 0.5, rng.integers(0, R, ab.shape), ab))
    return {"x": x, "home": home, "cen": cen, "post": post, "near": near, "ab": ab}
def pack(d):
    h = d["home"][..., None]; v = np.concatenate([d["x"], h >> 8, h & 255], axis=-1).astype(np.float32)
    def turn(a): return np.ascontiguousarray(a.transpose(0, 1, 3, 2)).reshape(N, 128, -1)
    return {"rec": turn(v).astype(BF), "post": turn(d["post"]).astype(np.int32), "cen": turn(d["cen"].astype(np.float32)).astype(BF), "near": turn(d["near"]).astype(np.int32),
            "absorb": np.stack([gtable(a.reshape(8, -1)) for a in d["ab"]])}
def setup_inputs(rng):
    return pack(world(rng, counts(rng, rng.choice(np.array([0.2, 0.4, 0.6]), (N, 8, 1)))))
def setup_inputs_room(rng):
    nf = rng.choice(np.array([0, 1, S - 1, S, S + 1, 3 * S]), (N, 8)); nf[0] = (S, S + 1, S - 1, 0, 1, 3 * S, S, 2 * S); nf[1, 0] = S
    fm = np.argsort(rng.random((N, 8, P0)), axis=-1) < nf[..., None]
    cnt = np.where(fm, rng.choice(np.array([L, 16]), fm.shape), np.where(rng.random(fm.shape) < 0.5, L - 1, rng.integers(1, L, fm.shape)))
    d = world(rng, cnt); d["x"][:, 0] = rng.integers(128, 256, (N, R0, 14)); d["cen"][:, 0, :, :14] = 0
    fp = np.flatnonzero(fm[1, 0]); fq = np.flatnonzero(~fm[0, 0])
    d["near"][0, 0, fq] = (P + fp[np.arange(len(fq)) % S])[:, None]
    return pack(d)
def setup_inputs_ties(rng):
    cnt = counts(rng, 0.5); cnt[:, :, :6] = 16
    d = world(rng, cnt); d["x"] = rng.integers(0, 3, (N, 8, R0, 14)); d["cen"][..., :14] = rng.integers(0, 3, (N, 8, P0, 14))
    d["x"][:, 0] = 7; d["cen"][:, 0, :, :14] = np.where(rng.random((N, P0, 1)) < 0.5, 7, rng.integers(5, 9, (N, P0, 14)))
    d["x"][:, 2] *= rng.random((N, R0, 1)) < 0.5; d["cen"][:, 2, :, :14] = rng.integers(5, 9, (N, P0, 14))
    d["ab"][:, :4] = np.arange(R0)
    d["near"][:, 1::2] = P * rng.integers(0, N, (N, 4, P0, 16)) + rng.integers(0, 6, (N, 4, P0, 16))
    return pack(d)
def setup_inputs_ends(rng):
    q = rng.permutation(N); cnt = counts(rng, 0.3); cnt[q[0]] = rng.integers(0, L, (8, P0)); cnt[q[1]] = L
    ch = rng.permutation(P0)[:5]; cnt[:, 3] = rng.integers(1, L, (N, P0)); cnt[:, 3, ch] = 16
    cnt[:, 4] = rng.integers(1, L, (N, P0)); cnt[:, 4, 0] = 16; cnt[:, 4, P0 - 1] = L
    d = world(rng, cnt); ab = d["ab"]; near = d["near"]; d["cen"][:, 3, :, :14] = 0
    ab[:, 1] = rng.choice(np.array([0, R0 - 1]), (N, RO, R0)); ab[:, 2] = rng.integers(R0, R, (N, RO, R0)); ab[:, 5] = rng.integers(0, R0, (N, 1, 1)); ab[:, 3] = np.arange(R0)
    near[:, 4] = P * rng.integers(0, N, (N, P0, 16)) + rng.choice(np.array([0, P0 - 1, P0, P - 1]), (N, P0, 16))
    near[:, 3] = P * rng.integers(0, N, (N, P0, 16)) + np.where(rng.random((N, P0, 16)) < 0.5, P0 + rng.integers(0, 5, (N, P0, 16)), ch[rng.integers(0, 5, (N, P0, 16))])
    for a in range(N):
        s = d["post"][a, 3, ch]; d["x"][a, 3, s[:, 0]] = 0; d["x"][a, 3, s[:, 1:].reshape(-1)] = rng.integers(200, 256, (75, 14))
    return pack(d)
def setup_inputs_sharp(rng):
    d = world(rng, counts(rng, 0.4)); E = N * S - 32; n = P0 - S; i = np.arange(n)
    tg = np.where(i < n - 32, i % E, E + i - (n - 32))
    for g in range(0, 8, 2):
        fs = [np.sort(rng.permutation(P0)[:S]) for q in range(N)]; to = np.concatenate([P * q + fs[q] for q in range(N)])
        for q in range(N):
            fp = fs[q]; fq = np.setdiff1d(np.arange(P0), fp); po = d["post"][q, g]
            dull = (rng.random(n) < 0.5) & ((i < E) | ((i >= 2 * E) & (i < n - 32)))
            z = int(np.flatnonzero(tg == q * S)[0]); dull[z] = False
            cnt = np.zeros(P0, np.int64); cnt[fp] = rng.integers(L, 16, S); cnt[fq] = rng.integers(1, 5, n); cnt[fq[z]] = 1
            key = rng.random((P0, 16)); key[fp, 0] = 2
            on = np.argsort(np.argsort(key, axis=1), axis=1) < cnt[:, None]
            ix = np.flatnonzero(on); m = len(ix); c = 1 + rng.permutation(R0 - 1); dead = c[m:]; low = dead[:len(dead) // 2]; high = dead[len(dead) // 2:]
            po[fp] = rng.choice(high, (S, 16)); po[fq] = rng.choice(low, (n, 16))
            po[on] = c[:m]; po[fq[z], int(np.argmax(on[fq[z]]))] = 0
            h = np.where(rng.random(R0) < 0.5, 65535, ix[rng.integers(0, m, R0)]); h[po[on]] = ix; d["home"][q, g] = h
            x = rng.integers(130, 201, (R0, 14)); x[low] = 0; x[high] = 255
            e = fp[::2]; x[po[e][on[e]]] = 0
            e = fp[1::2]; s = po[e][on[e]]; x[s] = rng.integers(0, 3, (len(s), 14))
            e = fq[~dull]; x[po[e][on[e]]] = 127
            d["x"][q, g] = x; d["cen"][q, g, fq, :14] = 255; d["ab"][q, g, 0] = np.arange(R0)
            d["near"][q, g, fq] = np.where(np.arange(16) < rng.integers(0, 15, (n, 1)), (P * q + fq)[:, None], to[tg][:, None])
    return pack(d)
def setup_inputs_spread(rng):
    d = world(rng, counts(rng, rng.random((N, 8, 1))))
    d["x"] = np.minimum((np.exp2(8 * rng.random((N, 8, R0, 1))) * rng.random((N, 8, R0, 14))).astype(np.int64), 255)
    d["cen"] = rng.integers(0, 256, (N, 8, P0, 16)) >> rng.integers(0, 8, (N, 8, P0, 1))
    d["near"] = rng.integers(0, N * P, (N, 8, P0, 16)); d["ab"] = rng.integers(0, R, (N, 8, RO, R0))
    return pack(d)
def check_inputs(d):
    bad = []
    for k, hi in (("rec", 255), ("cen", 255), ("post", R0 - 1), ("near", N * P - 1), ("absorb", R - 1)):
        v = np.asarray(d[k]).astype(np.float64)
        if not (np.min(v) >= 0 and np.max(v) <= hi) or np.any(v != np.floor(v)): bad.append("range of " + k)
    v = np.asarray(d["rec"]).astype(np.float64).reshape(N, 8, 16, R0); h = v[:, :, 14] * 256 + v[:, :, 15]
    if np.any((h >= 16 * P0) & (h != 65535)): bad.append("homes of rec")
    return bad
def reference(rec, post, cen, near, absorb):
    w = rec.astype(np.float32).astype(np.int32).reshape(N, 8, 16, R0)
    x = np.zeros((N, 8, 14, R), np.int32); x[..., :R0] = w[:, :, :14]
    home = np.full((N, 8, R), 65535, np.int64); home[..., :R0] = w[:, :, 14] * 256 + w[:, :, 15]
    po = np.zeros((N, 8, P, 16), np.int64); po[:, :, :P0] = post.reshape(N, 8, 16, P0).transpose(0, 1, 3, 2)
    ne = np.zeros((N, 8, P, 16), np.int64); ne[:, :, :P0] = near.reshape(N, 8, 16, P0).transpose(0, 1, 3, 2)
    ce = np.zeros((N, 8, 14, P), np.int32); ce[..., :P0] = cen.astype(np.float32).astype(np.int32).reshape(N, 8, 16, P0)[:, :, :14]
    al = np.stack([gentries(a) for a in absorb]).astype(np.int64).reshape(N, 8, RO, R0)
    for t in range(RO):
        new = P0 + S * t
        for q in range(N): x[q, :, :, :R0] = np.maximum(x[q, :, :, :R0], np.take_along_axis(x[q], al[q, :, t][:, None, :], 2))
        live = (np.take_along_axis(home, po.reshape(N, 8, 16 * P), 2) == np.arange(16 * P)).reshape(N, 8, P, 16)
        full = (np.add.reduce(live.astype(np.int64), axis=3) >= L).astype(np.int64)
        num = np.add.accumulate(full, axis=2) - full; sp = (full == 1) & (num < S)
        b = np.zeros((N, 8, S, 14), np.int32); row = np.zeros((N, 8, S), np.int64)
        for q in range(N):
            for g in range(8):
                for k, p in enumerate(np.flatnonzero(sp[q, g])):
                    f = new + k; ix = po[q, g, p].copy(); v = x[q, g][:, ix]; on = live[q, g, p]
                    va = v[:, np.argmax(on)]; da = np.add.reduce(np.abs(v - va[:, None]), axis=0)
                    vb = v[:, np.argmax(np.where(on, da, -1))]; db = np.add.reduce(np.abs(v - vb[:, None]), axis=0)
                    go = on & (db < da)
                    po[q, g, f] = ix; ne[q, g, f] = ne[q, g, p]; ce[q, g, :, p] = va; ce[q, g, :, f] = vb
                    home[q, g, ix[go]] = 16 * f + np.flatnonzero(go)
                    b[q, g, k] = vb; row[q, g, k] = np.argmin(go)
        tab = np.where(sp, num + S * np.arange(N)[:, None, None], -1).transpose(1, 0, 2).reshape(8, N * P)
        mov = np.full((N, 8, N * S), -1, np.int64)
        for q in range(N):
            tj = np.take_along_axis(tab, ne[q].reshape(8, 16 * P), 1).reshape(8, P, 16)
            tg = np.take_along_axis(tj, np.argmax(tj >= 0, axis=2)[:, :, None], 2)[:, :, 0]
            for g in range(8):
                Q = np.flatnonzero((tg[g] >= 0) & ~sp[q, g]); v = x[q, g][:, po[q, g, Q]]
                vb = b[:, g].reshape(N * S, 14).T[:, tg[g, Q]]
                gain = np.add.reduce(np.abs(v - ce[q, g][:, Q][:, :, None]), axis=0) - np.add.reduce(np.abs(v - vb[:, :, None]), axis=0)
                gain = np.where(live[q, g, Q], gain, 0); m = np.argmax(gain, axis=1); ok = np.any(gain > 0, axis=1)
                Q = Q[ok]; m = m[ok]; u, i = np.unique(tg[g, Q], return_index=True)
                mov[q, g, u] = po[q, g, Q[i], m[i]]
        for r in range(N):
            win = mov[r, :, r * S:(r + 1) * S].copy()
            for o, q in enumerate([a for a in range(N) if a != r]):
                c = mov[q, :, r * S:(r + 1) * S]; e = R0 + ((N - 1) * t + o) * S
                x[r, :, :, e:e + S] = np.where((c >= 0)[:, None, :], np.take_along_axis(x[q], np.maximum(c, 0)[:, None, :], 2), 0)
                gg, kk = np.nonzero(c >= 0); home[q, gg, c[gg, kk]] = 65535
                win = np.where((win < 0) & (c >= 0), e + np.arange(S), win)
            gg, kk = np.nonzero(win >= 0); m = row[r, gg, kk]
            home[r, gg, win[gg, kk]] = 16 * (new + kk) + m; po[r, gg, new + kk, m] = win[gg, kk]
    hh = np.stack([home >> 8, home & 255], axis=2)
    ya = np.concatenate([x[..., R0:], hh[..., R0:].astype(np.int32)], axis=2).reshape(N, 128, R - R0)
    return {"ypost": np.ascontiguousarray(po.transpose(0, 1, 3, 2)).reshape(N, 128, P).astype(np.float32),
            "yh": hh[..., :R0].reshape(N, 16, R0).astype(np.float32).astype(BF), "ya": ya.astype(np.float32).astype(BF)}

@@ -1,0 +1,901 @@
+from concourse.bass import DstId, RemoteDMATransfer
+from concourse.mybir import AluOpType as OP, AxisListType, ActivationFunctionType as AF
+
+F, B, I, U, H16 = "float32", "bfloat16", "int32", "uint16", "float16"
+_W = {
+    B: "X0 4208 XB 3584 X1 3808 XA 112 H 4608 V 4864 W 4864 MC 4864 MB 4864 TN 4864 CEN 288 CE 320 TAB0 2688 TAB1 2688 L 448 LO 320 F0 320 F1 320 INC 320 LE 320 ZER 384 Z 320 BT0 128 BT1 128 MV0 128 MV1 128 "
+       "VS 272 VSa 256 VSc 256 AD 256 BD 256 AA 256 BA 256 LS2 32 LT 32 RB 16 GE 32 GT 32 GS 16 LS16 16 CX1 304 CEX 304 CXT 384 E 2048 TB 24 TH 24 T8 384 BX1 128 BTX 128 X48 48 XT 384 TS 304 ZQ 2432 D0 2432 "
+       "Y 192 VB 320 LOS 320 OHn 128 LN 128 FV 16 RB2 16 MVV0 128 MVV1 128 YA 224 YB 224 BO 128 TRI 128 ID 128 NID 128 U16 144 U14 144 UH 144 UC 144 WC 8 WB 8 WA 8 WV 8 SEL 8 LW 128 ZW 240 MKU 192 I16 16 EO 32 C31 16 "
+       "IOB 128 C128 384 C15 384 C256 24 HV0 256 HV1 256 SA 128 SB1 128 SB2 128 RP 256 FST 128 BR0 512 BR1 512 TA 128 TB2 128 AH 224 AL 224 DA 224 DB 224 AR 3584 YR 4608 S1 128 S2 128 S3 128 S4 128 RM 1024",
+    F: "PIf 320 SLOT 288 MA 320 pk 2 t2 1 SPf 16 CSf 16 LAf 16 LK 16 KL 16 KA 16 obf 1 g1 16 GO 16 RO 32 mx 1 T1 192 T2 192 T3 96 T4 48 hs 24 ok 24 OHm 128 PGm 256 W8 40 GLf 16 kk 7 sm 16 TT 96 TR 96 OH 16 OW 16 COL 48 "
+       "IOT 256 IOS 288 G1 128 G2 136 G3 192 UF 144 L8f 12 C16 16 C16k 16 DGO 16 DMV 8 C7 7 CPf 320",
+    I: "POI 288 ABI 448 NEI 320 NL0 32 NL1 32 kx 1 kr 1 ki 24 Ti 24 lo 24 IC 4 AI 224 PQ 288 PQ2 288",
+    U: "PU 304 ABU 224 NU 304 pk2 2 NLu 8 SPu 16 CSu 16 LAu 16 obu 2 LBu 16 TLu 304 QTu 8 QTo 2 VLu 24 QLu 8 MVL 8 GLu 16 ARu 2 L8u 12 CU 304 PP 288",
+    H16: "SC 2432",
+}
+_S = {}
+for _d, _t in _W.items():
+    _t = _t.split()
+    for _i in range(0, len(_t), 2):
+        _S[_t[_i]] = (int(_t[_i + 1]), _d)
+_PS = ["PA", "PB", "PC", "PD", "PN", "PG", "PM0", "PM1"]
+SCRATCH = {}
+_PACK = {}
+_n = {F: 0, I: 0, B: 0}
+for _k in ("g1 KL KA LK GO RO LAf SPf CSf T3 T4 hs ok kk sm OH OW GLf W8 DGO DMV C7 C16 C16k obf t2 pk mx L8f TT TR G1 G2 G3 OHm kx kr ki Ti lo IC AI WC WB WA WV SEL I16 EO C31 GE GT LT LS2 RB RB2 "
+           "TB TH C256 LW MKU BO TRI ID NID FST SA SB1 SB2 IOB UH UC U14 U16 ZW RP LS16 GS S1 S2 S3 S4 TA TB2 BX1 Y OHn LN FV AH AL DA DB VSc VSa AD BD AA BA Z").split():
+    _w, _d = _S[_k]
+    _PACK[_k] = ("PK" + _d, _n[_d])
+    _n[_d] += (_w + 15) // 16 * 16
+for _k, (_w, _d) in _S.items():
+    if _k not in _PACK:
+        SCRATCH[_k] = ("sbuf", [128, _w], _d)
+for _d in (F, I, B):
+    SCRATCH["PK" + _d] = ("sbuf", [128, _n[_d]], _d)
+for _k in _PS:
+    SCRATCH[_k] = ("psum", [128, 512], F)
+_EX = ["a0", "b0", "c0", "a1", "b1", "c1"]
+SEMAPHORES = ["cv", "ca", "ct", "cg"] + ["r" + e for e in _EX] + ["y" + e for e in _EX] + ["ls"] + ["d%d" % i for i in range(20)]
+
+
+def bits(es):
+    return sum(1 << e for e in es)
+
+
+def parts(es, n):
+    out, left = [], list(es)
+    for i in range(n):
+        k, s = n - i, 1
+        while s * 2 <= (len(left) + k - 1) // k and s * 2 + (k - 1) <= len(left):
+            s *= 2
+        out.append(left[:s])
+        left = left[s:]
+    return out
+
+
+def plan(r, T, topo):
+    c = T.cores[r]
+    direct = [d for d in range(len(T.cores)) if d != r and topo.may_write(c, T.cores[d])]
+    cross = [d for d in range(len(T.cores)) if d != r and d not in direct]
+    rel = [x for x in topo.cores_of(c) if x != c and topo.die(x) == topo.die(c) and T.rank_of(x) is None and all(topo.may_write(x, T.cores[d]) for d in cross)]
+    rel = rel[:2] if cross else []
+    return direct, [(x, cross[i::len(rel)]) for i, x in enumerate(rel)]
+
+
+def masks_c(r, T, topo):
+    direct, rel = plan(r, T, topo)
+    c, last, on = T.cores[r], {}, {}
+    if direct:
+        for d, es in zip(direct, parts(topo.engines(c, T.cores[direct[0]]), len(direct))):
+            last[d] = es
+    ds = [(x, d) for x, q in rel for d in q]
+    if ds:
+        for (x, d), es in zip(ds, parts(topo.engines(c, ds[0][0]), len(ds))):
+            on[d] = es
+    for x, q in rel:
+        for d, es in zip(q, parts(topo.engines(x, T.cores[q[0]]), len(q))):
+            last[d] = es
+    return last, on
+
+
+def spot(T, r, d, t):
+    a = (0 if t else 3584) + (r if r < d else r - 1) * 16
+    return T["XA" if t else "X1"][:, a:a + 16]
+
+
+def dst(topo, x, c):
+    rid, pid = topo.addr(x, c)
+    return DstId(rid=rid, pnc=pid)
+
+
+def relay_program(g, core, T, topo):
+    for r in range(len(T.cores)):
+        direct, rel = plan(r, T, topo)
+        for x, q in rel:
+            if x == core:
+                n = 0
+                last, on = masks_c(r, T, topo)
+                for ex in _EX:
+                    k, t = ex[0], int(ex[1])
+                    sr = T.sem["y" + ex]
+                    if k == "c":
+                        g.wait_ge(T.sem["r" + ex], sum(len(on[d]) for d in q))
+                        g.remote_dma_fused([RemoteDMATransfer(dst_ids=[dst(topo, T.cores[d], core)], dma_engine_mask=bits(last[d]), remote_sem=sr, src=T["MV%d" % t][:, 16 * d:16 * d + 16],
+                                                              dst=spot(T, r, d, t)) for d in q], local_sem=T.sem.ls)
+                        n += sum(len(last[d]) for d in q)
+                    else:
+                        es = topo.engines(core, T.cores[q[0]])
+                        ap = T["NL%d" % t][:, 4 * r:4 * r + 1] if k == "a" else T["BT%d" % t][:, 16 * r:16 * r + 16]
+                        g.wait_ge(T.sem["r" + ex], len(topo.engines(T.cores[r], core)))
+                        g.remote_dma_fused([RemoteDMATransfer(dst_ids=[dst(topo, T.cores[d], core) for d in q], dma_engine_mask=bits(es), remote_sem=sr, srcs=[ap], dsts=[ap for d in q])], local_sem=T.sem.ls)
+                        n += len(es)
+                g.wait_ge(T.sem.ls, n)
+
+
+def rank_program(g, core, T, topo):
+    r = T.rank_of(core)
+    if r is None:
+        relay_program(g, core, T, topo)
+        return
+    N = len(T.cores)
+    E = {"v": g.vector, "a": g.scalar, "t": g.tensor, "g": g, "s": g.sync}
+    CS = {"v": "cv", "a": "ca", "t": "ct", "g": "cg"}
+    cnt = {}
+    know = {e: {} for e in E}
+    hist = {}
+    ndma = [0]
+
+    def v(n, a=0, b=None, st=1, p0=0, p1=128, ps=1):
+        w = _S[n][0] if n in _S else (512 if n in _PS else T[n].shape[1])
+        b = w if b is None else b
+        if n in _PACK:
+            nn, o = _PACK[n]
+            return (nn, a + o, b + o, st, p0, p1, ps)
+        return (n, a, b, st, p0, p1, ps)
+
+    def ind(w, o):
+        return ("IND", w, o)
+
+    def ap(x):
+        if x[0] == "IND":
+            return ap(x[1]).indirect(ap(x[2]))
+        n, a, b, st, p0, p1, ps = x
+        if ps != 1:
+            return T[n][p0:p1:ps, a:b]
+        if p0 == 0 and p1 == 128:
+            return T[n][:, a:b] if st == 1 else T[n][:, a:b:st]
+        return T[n][p0:p1, a:b] if st == 1 else T[n][p0:p1, a:b:st]
+
+    def regs(xs):
+        out = []
+        for x in xs:
+            if isinstance(x, tuple):
+                out += [x[1], x[2]] if x[0] == "IND" else [x]
+        return out
+
+    def deps(eng, outs, ins):
+        need = {}
+        for w, xs in ((True, outs), (False, ins)):
+            for x in xs:
+                ps = x[0] in _PS
+                for h in hist.get(x[0], []):
+                    if ps:
+                        if h["e"] == eng and (eng == "t" or not (w or h["w"])):
+                            continue
+                    else:
+                        if h["b"] <= x[1] or h["a"] >= x[2] or not (w or h["w"]):
+                            continue
+                        if h["st"] > 1 and h["st"] == x[3] and (h["a"] - x[1]) % x[3]:
+                            continue
+                    if need.get(h["s"], (0, None))[0] < h["n"]:
+                        need[h["s"]] = (h["n"], h["k"])
+        return need
+
+    def waits(eng, need):
+        for s, (n, k) in sorted(need.items(), key=lambda z: -len(z[1][1])):
+            if know[eng].get(s, 0) < n:
+                E[eng].wait_ge(T.sem[s], n)
+                for a, b in k.items():
+                    know[eng][a] = max(know[eng].get(a, 0), b)
+                know[eng][s] = n
+
+    def note(eng, sem, n, outs, ins, k):
+        for w, xs in ((True, outs), (False, ins)):
+            for x in xs:
+                hs = hist.setdefault(x[0], [])
+                if x[0] in _PS:
+                    hs[:] = [h for h in hs if not (h["e"] == eng and h["w"] == w)]
+                elif w and x[3] == 1 and x[4] == 0 and x[5] == 128:
+                    hs[:] = [h for h in hs if not (h["a"] >= x[1] and h["b"] <= x[2])]
+                elif not w:
+                    hs[:] = [h for h in hs if not (h["e"] == eng and h["s"] == sem and not h["w"] and h["a"] >= x[1] and h["b"] <= x[2])]
+                hs.append({"a": x[1], "b": x[2], "st": x[3], "w": w, "e": eng, "s": sem, "n": n, "k": k})
+
+    def run(eng, fn, outs, ins, sem=None, inc=1):
+        o, i = regs(outs), regs(ins)
+        i = i + [x[2] for x in outs if x[0] == "IND"]
+        waits(eng, deps(eng, o, i))
+        s = sem or CS[eng]
+        fn().then_inc(T.sem[s], inc)
+        cnt[s] = cnt.get(s, 0) + inc
+        note(eng, s, cnt[s], o, i, dict(know[eng]))
+
+    def s_(x):
+        return ap(x) if isinstance(x, tuple) else x
+
+    def tt(o, a, b, op):
+        run("v", lambda: g.vector.tensor_tensor(ap(o), ap(a), ap(b), op), [o], [a, b])
+
+    def ts(o, a, s1, op0, s2=None, op1=None):
+        if op1 is None:
+            run("v", lambda: g.vector.tensor_scalar(ap(o), ap(a), s_(s1), None, op0), [o], [a, s1])
+        else:
+            run("v", lambda: g.vector.tensor_scalar(ap(o), ap(a), s_(s1), s_(s2), op0, op1), [o], [a, s1, s2])
+
+    def tc(o, a):
+        run("v", lambda: g.vector.tensor_copy(ap(o), ap(a)), [o], [a])
+
+    def tr(o, a, op):
+        run("v", lambda: g.vector.tensor_reduce(ap(o), ap(a), AxisListType.X, op), [o], [a])
+
+    def vtr(o, a):
+        run("v", lambda: g.vector.transpose(ap(o), ap(a)), [o], [a])
+
+    def scan(o, a, b, init, op0, op1):
+        run("v", lambda: g.vector.tensor_tensor_scan(ap(o), ap(a), ap(b), s_(init), op0, op1), [o], [a, b, init])
+
+    def ms(o, c):
+        run("v", lambda: g.vector.memset(ap(o), c), [o], [])
+
+    def act(o, a, f=AF.Copy, bias=0.0, scale=1.0):
+        run("a", lambda: g.scalar.activation(ap(o), ap(a), f, s_(bias), s_(scale)), [o], [a, bias, scale])
+
+    def mm(o, l, x, start=True, stop=True):
+        run("t", lambda: g.tensor.matmul(ap(o), ap(l), ap(x), start, stop), [o], [l, x])
+
+    def iota(o, pat, base=0, ch=0):
+        run("g", lambda: g.iota(ap(o), pat, base, ch, allow_small_or_imprecise_dtypes=True), [o], [])
+
+    def dma(q, o, a):
+        s = "d%d" % ndma[0]
+        ndma[0] += 1
+        run(q, lambda: (g.sync if q == "s" else g.scalar).dma_start(ap(o), ap(a)), [o], [a], s, 16)
+
+    direct, rel = plan(r, T, topo)
+    last, on = masks_c(r, T, topo)
+    nls = [0]
+
+    def bcast(ex, x):
+        waits("g", deps("g", [], [x]))
+        rs = [c for c, q in rel]
+        if rs:
+            es = topo.engines(core, rs[0])
+            g.remote_dma_fused([RemoteDMATransfer(dst_ids=[dst(topo, c, core) for c in rs], dma_engine_mask=bits(es), remote_sem=T.sem["r" + ex], srcs=[ap(x)], dsts=[ap(x) for c in rs])], local_sem=T.sem.ls)
+            nls[0] += len(es)
+        if direct:
+            es = topo.engines(core, T.cores[direct[0]])
+            g.remote_dma_fused([RemoteDMATransfer(dst_ids=[dst(topo, T.cores[d], core) for d in direct], dma_engine_mask=bits(es), remote_sem=T.sem["y" + ex], srcs=[ap(x)], dsts=[ap(x) for d in direct])], local_sem=T.sem.ls)
+            nls[0] += len(es)
+
+    def movers(t):
+        ex, nm = "c%d" % t, "MV%d" % t
+        waits("g", deps("g", [], [v(nm)]))
+        x_ = [RemoteDMATransfer(dst_ids=[dst(topo, x, core)], dma_engine_mask=bits(on[d]), remote_sem=T.sem["r" + ex], src=T[nm][:, 16 * d:16 * d + 16], dst=T[nm][:, 16 * d:16 * d + 16]) for x, q in rel for d in q]
+        if x_:
+            g.remote_dma_fused(x_, local_sem=T.sem.ls)
+            nls[0] += sum(len(e) for e in on.values())
+        x_ = [RemoteDMATransfer(dst_ids=[dst(topo, T.cores[d], core)], dma_engine_mask=bits(last[d]), remote_sem=T.sem["y" + ex], src=T[nm][:, 16 * d:16 * d + 16], dst=spot(T, r, d, t)) for d in direct]
+        if x_:
+            g.remote_dma_fused(x_, local_sem=T.sem.ls)
+            nls[0] += sum(len(last[d]) for d in direct)
+
+    def arrive(ex, regions):
+        n = 0
+        for q in range(N):
+            if q != r:
+                dq, rq = plan(q, T, topo)
+                if ex[0] == "c":
+                    n += len(masks_c(q, T, topo)[0][r])
+                elif r in dq:
+                    n += len(topo.engines(T.cores[q], T.cores[dq[0]]))
+                else:
+                    x, k = [(x, k) for x, k in rq if r in k][0]
+                    n += len(topo.engines(x, T.cores[k[0]]))
+        cnt["y" + ex] = n
+        for x in regions:
+            hist.setdefault(x[0], []).append({"a": x[1], "b": x[2], "st": x[3], "w": True, "e": "net", "s": "y" + ex, "n": n, "k": {}})
+
+    def col(i):
+        return v("COL", i, i + 1)
+
+    (P_, M_, G_, G15, ODD, EVN, C13, K14, K15, C16_, UHC, WCC, R15, F15, I0, BC, LT8, GE8, K16, AR_, SAW, SBW, WBC, WAC, WVC, UCC, P1_, G14, WO, WO1, H18, H19) = range(32)
+    TQ, TQB = 32, 40
+    AS = AF.Identity
+
+    dma("s", v("POI"), v("post"))
+    dma("s", v("X0", 0, 1792), v("rec", 0, 1792))
+    dma("a", v("X0", 1792, 3584), v("rec", 1792, 3584))
+    dma("s", v("ABI"), v("absorb"))
+    dma("a", v("CEN"), v("cen"))
+    dma("s", v("XB"), v("rec"))
+    dma("s", v("NEI", 0, 288), v("near"))
+    ic = [v("IC", i, i + 1) for i in range(4)]
+    iota(ic[0], [[0, 1]], 0, 1)
+    iota(v("IOT"), [[1, 256]])
+    iota(v("IOS"), [[16, 288]])
+    iota(v("G1"), [[1, 8], [0, 16]])
+    for q in range(8):
+        iota(v("RM", 128 * q, 128 * q + 128), [[16, 8], [8, 2], [0, 8]], q)
+    iota(v("I16"), [[1, 16]])
+    iota(v("EO"), [[1, 2], [0, 16]])
+    iota(v("C31"), [[-1, 16]], 31)
+    iota(v("C16"), [[-1, 16]], 16)
+    iota(v("C16k"), [[16, 16]])
+    iota(v("E"), [[1, 128], [0, 16]])
+    iota(v("TAB0"), [[0, 2688]], 4096)
+    ts(ic[1], ic[0], 15, OP.bitwise_and)
+    ts(ic[2], ic[0], 4, OP.arith_shift_right)
+    ts(ic[3], ic[2], 1, OP.bitwise_and)
+    for i in range(3):
+        tc(col(i), ic[i])
+    tc(col(ODD), ic[3])
+    ts(col(G15), col(G_), 16, OP.mult, 15, OP.add)
+    ts(col(EVN), col(ODD), -1, OP.mult, 1, OP.add)
+    ts(col(C13), col(M_), 14, OP.is_lt)
+    ts(col(K14), col(M_), 14, OP.is_equal)
+    ts(col(K15), col(M_), 15, OP.is_equal)
+    ts(col(UHC), col(K14), 256, OP.mult, col(K15), OP.add)
+    ts(v("UH"), v("IOT", 0, 144), col(G15), OP.is_equal, col(UHC), OP.mult)
+    ts(v("ID"), v("IOT", 0, 128), col(P_), OP.is_equal)
+    ts(v("BO"), v("G1"), col(G_), OP.is_equal)
+    ts(v("TRI"), v("IOT", 0, 128), col(P_), OP.is_ge)
+    tt(v("TRI"), v("TRI"), v("BO"), OP.mult)
+    tc(v("PU", 0, 288), v("POI"))
+    for a, b in ((0, 96), (96, 208)):
+        act(v("H", 16 * a, 16 * b), ind(v("X0", 0, 3584), v("PU", a, b)))
+    ms(v("X0", 3584, 3808), 0)
+    ms(v("X1", 3584, 3808), 0)
+    ms(v("PIf", 288, 320), 0)
+    ms(v("CPf", 288, 320), 0)
+    ms(v("L"), 0)
+    ms(v("CE", 288, 320), 0)
+    tc(v("PIf", 0, 288), v("POI"))
+    ts(v("SLOT"), v("IOS"), col(M_), OP.add)
+    tc(v("H", 16 * 208, 4608), ind(v("X0", 0, 3584), v("PU", 208, 288)))
+    tc(v("ABU"), v("ABI", 0, 224))
+    for a, b in ((0, 96), (96, 208), (208, 288)):
+        for m in range(16):
+            mm(v("PA", a, b), v("UH", 15 - m, 143 - m), v("H", 16 * a + m, 16 * b, 16), m == 0, m == 15)
+    ts(col(SAW), col(K14), 8, OP.mult, col(C13), OP.add)
+    ts(col(SBW), col(K14), 16, OP.mult, col(C13), OP.add)
+    ts(col(G14), col(G15), -1, OP.add)
+    ts(col(P1_), col(P_), 1, OP.add)
+    ts(v("TA"), v("ID"), col(C13), OP.mult)
+    for nm, rr, wc in (("SA", G14, SAW), ("SB1", G15, SBW)):
+        ts(v(nm), v("IOT", 0, 128), col(rr), OP.is_equal, col(wc), OP.mult)
+        tt(v(nm), v(nm), v("TA"), OP.add)
+    ts(v("TB2"), v("IOT", 0, 128), col(P1_), OP.is_equal)
+    tt(v("TB2"), v("ID"), v("TB2"), OP.subtract)
+    ts(v("SB2"), v("TB2"), col(K14), OP.mult)
+    ms(v("ZER"), 0)
+    ms(v("F0", 288, 304), 1)
+    ms(v("F1", 304, 320), 1)
+    ms(v("VS", 256, 272), 0)
+    ts(col(R15), col(M_), 16, OP.mult, 15, OP.add)
+    ts(col(C16_), col(C13), 16, OP.mult)
+    act(v("CE", 0, 288), v("CEN"), AS, col(K14), col(C13))
+    for a, b in ((0, 112), (112, 224)):
+        tt(v("X1", 16 * a, 16 * b), ind(v("X0", 0, 3808), v("ABU", a, b)), v("XB", 16 * a, 16 * b), OP.max)
+
+    def sums(src, w, mid, out, b1, b2):
+        mm(v(b1, 0, w), v("SA"), v(src, 0, w))
+        act(v(mid, 0, w), v(b1, 0, w))
+        mm(v(b2, 0, w), v("SB1"), v(src, 0, w), True, False)
+        mm(v(b2, 0, w), v("SB2"), v(mid, 0, w), False, True)
+        act(v(out, 0, w), v(b2, 0, w))
+
+    def nbs(t):
+        return [128, 128, 32 + 16 * t]
+
+    def centres(t):
+        sums("CE", 288 + 16 * t, "CX1", "CEX", "PM0", "PM1")
+        nb = nbs(t)
+        for b in range(3):
+            mm(v("PM0", 128 * b, 128 * b + 128, 1, 0, nb[b]), v("CEX", 128 * b, 128 * b + nb[b]), v("ID"))
+        act(v("CXT", 0, 256), v("PM0", 0, 256))
+        act(v("CXT", 256, 384, 1, 0, nb[2]), v("PM0", 256, 384, 1, 0, nb[2]))
+
+    centres(0)
+
+    def rows_open():
+        ts(col(LT8), col(M_), 8, OP.is_lt)
+        ts(col(GE8), col(M_), 8, OP.is_ge)
+        ts(v("AI"), v("ABI", 224, 448), 255, OP.bitwise_and)
+        tc(v("AL"), v("AI"))
+        tt(v("AH"), v("ABI", 224, 448), v("AI"), OP.subtract)
+        act(v("S1"), v("ID"), AF.Copy, 0.0, col(LT8))
+        act(v("S4"), v("ID"), AF.Copy, 0.0, col(GE8))
+        ts(v("S2"), v("IOT", 0, 128), -8, OP.add, col(P_), OP.is_equal)
+        ts(v("S2"), v("S2"), col(LT8), OP.mult)
+        ts(v("S3"), v("IOT", 0, 128), 8, OP.add, col(P_), OP.is_equal)
+        ts(v("S3"), v("S3"), col(GE8), OP.mult)
+        ts(v("RM"), v("RM"), col(P_), OP.is_equal)
+        mm(v("PC", 0, 224), v("S1"), v("AH"), True, False)
+        mm(v("PC", 0, 224), v("S2"), v("AL"), False, True)
+        mm(v("PD", 0, 224), v("S3"), v("AH"), True, False)
+        mm(v("PD", 0, 224), v("S4"), v("AL"), False, True)
+        act(v("DA"), v("PC", 0, 224))
+        act(v("DB"), v("PD", 0, 224))
+
+    def rows(i, bank):
+        for j in range(2):
+            q = 2 * i + j
+            mm(v(bank, 224 * j, 224 * j + 224), v("RM", 128 * (q % 8), 128 * (q % 8) + 128), v("DA" if q < 8 else "DB"))
+        act(v("AR", 448 * i, 448 * i + 448), v(bank, 0, 448))
+
+    def vgather(t, b):
+        o = v("VW"[t], 2048 * b, 2048 * b + 16 * nbs(t)[b])
+        if t == 0:
+            act(o, ind(v("X1", 0, 3584), v("PU", 128 * b, 128 * b + nbs(t)[b])), AS, col(K14), col(C13))
+        else:
+            tt(o, ind(v("X1", 0, 3808), v("CU", 128 * b, 128 * b + nbs(t)[b])), v("V", 2048 * b, 2048 * b + 16 * nbs(t)[b]), OP.max)
+
+    def count(t, a, b, fresh):
+        Ft, P = "F%d" % t, 288 + 16 * t
+        e = min(b, P)
+        mm(v("PA", a, e), v("BO"), v("L", a, e))
+        mm(v("PB", a, b), v("TRI"), v("L", a, b))
+        ts(v(Ft, a, e), v("PA", a, e), 12, OP.is_ge)
+        act(v("Z", a, b), v("PB", a, b), AF.Relu, 1.0, -1.0)
+        mm(v("PB", a, b), v("BO"), v("Z", a, b))
+        act(v("MA", a, b), v("PB", a, b))
+        scan(v("INC", a, b), v(Ft, a, b), v("ZER", a, b), 0.0 if fresh else v("INC", a - 1, a), OP.add, OP.add)
+        ts(v("LE", a, b), v("INC", a, b), col(M_), OP.is_le)
+        tr(v("pk", 0, 1) if fresh else v("pk", 1, 2), v("LE", a, b), OP.add)
+        if not fresh:
+            tt(v("pk", 0, 1), v("pk", 0, 1), v("pk", 1, 2), OP.add)
+
+    def numbers(t):
+        P, k1 = 288 + 16 * t, v("pk", 0, 1)
+        ts(v("pk2"), v("ZER", 0, 2), k1, OP.add)
+        tc(v("SPu"), ind(v("PIf"), v("pk2", 0, 1)))
+        if t == 1:
+            tc(v("CSu"), ind(v("CPf"), v("pk2", 0, 1)))
+        ts(v("t2"), k1, P, OP.is_ge, 2560 + 16 * r - 320 * r - P, OP.mult)
+        ts(v("NL%d" % t, 4 * r, 4 * r + 1), v("t2"), k1, OP.add, 320 * r, OP.add)
+        bcast("a%d" % t, v("NL%d" % t, 4 * r, 4 * r + 1))
+
+    def kp(bank, x):
+        mm(v(bank, 0, 16), v("ID"), v("C31"), True, False)
+        for k in range(16):
+            mm(v(bank, 0, 16), v("U16", 15 - k, 143 - k), v(x, 16 * k, 16 * k + 16), False, k == 15)
+
+    def split_a(t):
+        P, pk1 = 288 + 16 * t, v("pk2", 0, 1)
+        if t == 0:
+            act(v("VS", 0, 256), ind(v("X1", 0, 3584), v("SPu")), AS, col(K14), col(C13))
+            tc(v("VSc"), ind(v("X1", 0, 3584), v("SPu")))
+        else:
+            act(v("VSa"), ind(v("X1", 0, 3808), v("SPu")), AS, col(K14), col(C13))
+        tt(v("LAf"), ind(v("MA", 0, P + 16), pk1), v("C16k"), OP.add)
+        tc(v("LAu"), v("LAf"))
+        tt(v("LS2"), ind(v("L", 0, 320), v("pk2")), v("EO"), OP.mult)
+        vtr(v("LT"), v("LS2"))
+        tt(v("LK"), v("LT", 0, 16), v("LT", 16, 32), OP.add)
+        if t == 1:
+            tt(v("VS", 0, 256), ind(v("X1", 0, 3808), v("CSu")), v("VSa"), OP.max)
+            tc(v("VSc"), v("VS", 0, 256))
+        tt(v("AD"), ind(v("VS"), v("LAu")), v("VSc"), OP.subtract)
+        tc(v("LO", 0, P), v("L", 0, P))
+        tc(ind(v("LO", 0, P + 16), pk1), v("ZER", 0, 16))
+
+    def split_b(t):
+        tt(v("KL"), v("PC", 0, 16), v("LK"), OP.mult)
+        tr(v("kx"), v("KL"), OP.max)
+        ts(v("kr"), v("kx"), 15, OP.bitwise_and)
+        ts(v("obu", 0, 1), v("kr"), -1, OP.mult, col(R15), OP.add)
+        bt = v("BT%d" % t, 16 * r, 16 * r + 16)
+        tc(bt, ind(v("VS"), v("obu", 0, 1)))
+        bcast("b%d" % t, bt)
+
+    def split_c(t):
+        ts(v("obf"), v("kr"), -1, OP.mult, col(R15), OP.add)
+        ts(v("RB"), v("I16"), v("obf"), OP.mult)
+        mm(v("PD", 0, 16), v("BO"), v("RB"))
+        tc(v("LBu"), v("PD", 0, 16))
+        tt(v("BD"), ind(v("VS"), v("LBu")), v("VSc"), OP.subtract)
+        act(v("KA"), v("PC", 0, 16))
+        act(v("BA"), v("BD"), AF.Abs)
+        kp("PD", "BA")
+
+    def split_g():
+        tt(v("g1"), v("PD", 0, 16), v("KA"), OP.is_lt)
+        tt(v("GO"), v("g1"), v("LK"), OP.mult)
+
+    def split_d(t):
+        P, pk1 = 288 + 16 * t, v("pk2", 0, 1)
+        tc(v("SPf"), ind(v("PIf"), pk1))
+        act(v("GE", 0, 16), v("GO"), AF.Copy, 0.0, col(EVN))
+        act(v("GE", 16, 32), v("GO"), AF.Copy, 0.0, col(ODD))
+        vtr(v("GT"), v("GE"))
+        tt(v("GS"), v("GT", 0, 16), v("GT", 16, 32), OP.add)
+        tt(v("g1"), v("GO"), v("C16"), OP.mult)
+        tt(v("KL"), v("C16"), v("g1"), OP.subtract)
+        tr(v("mx"), v("KL"), OP.max)
+        ts(v("RO", 0, 16), v("KL"), v("mx"), OP.is_equal, col(EVN), OP.mult)
+        ts(v("RO", 16, 32), v("KL"), v("mx"), OP.is_equal, col(ODD), OP.mult)
+        ts(v("obf"), v("mx"), -1, OP.mult, col(K16), OP.add)
+        act(v("RB2"), v("I16"), AF.Copy, 0.0, v("obf"))
+        mm(v("PC", 0, 16), v("BO"), v("RB2"))
+        act(v("FV"), v("PC", 0, 16), AS, col(H18 + t), col(K15))
+        act(v("MVV%d" % t, 16 * r, 16 * r + 16), v("FV"))
+        tt(v("GLf"), v("SPf"), v("DGO"), OP.subtract)
+        tt(v("GLf"), v("GLf"), v("GS"), OP.mult)
+        tt(v("GLf"), v("GLf"), v("DGO"), OP.add)
+        tc(v("GLu"), v("GLf"))
+        if t == 0:
+            tt(v("LS16"), ind(v("L", 0, 320), pk1), v("GS"), OP.subtract)
+            tc(ind(v("L", 0, 320), pk1), v("LS16"))
+            tt(v("RB"), v("AD", 0, 256, 16), v("VSc", 0, 256, 16), OP.add)
+            tc(ind(v("CE"), pk1), v("RB"))
+            tc(v("CE", P, P + 16), v("BT%d" % t, 16 * r, 16 * r + 16))
+            tc(v("NU", P, P + 16), ind(v("NEI"), pk1))
+
+    def go_homes(t):
+        tc(ind(v("X0"), v("GLu")), v("HV%d" % t))
+
+    def mcent(t, b, js=(0, 1, 2, 3)):
+        nb = nbs(t)
+        for j in js:
+            n = min(512, 16 * nb[b] - 512 * j)
+            if n > 0:
+                c = 2048 * b + 512 * j
+                pm = "PM%d" % (j % 2)
+                kk = 128 if b < 2 else nb[b]
+                mm(v(pm, 0, n), v("CXT", 128 * b, 128 * b + 128, 1, 0, kk), v("E", 512 * j, 512 * j + n, 1, 0, kk), True, b != 1)
+                if b == 1:
+                    mm(v(pm, 0, n), v("NID"), v("VW"[t], c, c + n), False, True)
+                    act(v("MC", c, c + n), v(pm, 0, n), AF.Abs)
+                else:
+                    tt(v("MC", c, c + n), v(pm, 0, n), v("VW"[t], c, c + n), OP.max)
+
+    def by_slot(bank, x, w, t, b):
+        nb = nbs(t)
+        for m in range(16):
+            mm(v(bank, 24 * m + b, 24 * m + b + 22, 3, 0, nb[b]), v(x, 2048 * b + m, 2048 * b + 16 * nb[b], 16), v(w), False, False)
+
+    def gain_open(t):
+        nb = nbs(t)
+        mm(v("PG", 0, 384), v("FST"), v("C15"), True, False)
+        for b in range(3):
+            for m in range(16):
+                mm(v("PG", 24 * m + b, 24 * m + b + 22, 3, 0, nb[b]), v("LO", 128 * b, 128 * b + nb[b]), v("LW", 8 * m, 8 * m + 8), False, False)
+
+    def close(bank):
+        mm(v(bank, 0, 384), v("FST"), v("ZER"), False, True)
+
+    def tree(bank, op, out):
+        tc(v("T1"), v(bank, 192, 384))
+        tt(v("T2"), v(bank, 0, 192), v("T1"), op)
+        tt(v("T3"), v("T2", 0, 96), v("T2", 96, 192), op)
+        tt(v("T4"), v("T3", 0, 48), v("T3", 48, 96), op)
+        tt(out, v("T4", 0, 24), v("T4", 24, 48), op)
+
+    def turn(x, n, out):
+        for b in range(3):
+            mm(v("PA", 128 * b, 128 * b + 128, 1, 0, n), v(x, b, 3 * n, 3), v("ID"))
+        tc(v(out, 0, 384, 1, 0, n), v("PA", 0, 384, 1, 0, n))
+
+    def table(t):
+        arrive("a%d" % t, [v("NL%d" % t)])
+        tc(v("NLu"), v("NL%d" % t, 0, 32, 4))
+        tc(ind(v("TAB%d" % t), v("NLu")), v("IOB"))
+
+    def near(t, b, vec=False):
+        o, i = v("TN", 2048 * b, 2048 * b + 16 * nbs(t)[b]), ind(v("TAB%d" % t), v("NU", 128 * b, 128 * b + nbs(t)[b]))
+        if vec:
+            tc(o, i)
+        else:
+            act(o, i)
+
+    def near_sums(t, bs):
+        mm(v("PN", 0, 384), v("FST"), v("C128"), True, False)
+        for b in bs:
+            by_slot("PN", "TN", "SEL", t, b)
+        close("PN")
+
+    def targets(t):
+        P = 288 + 16 * t
+        tree("PN", OP.min, v("ki"))
+        ts(v("Ti"), v("ki"), 127, OP.bitwise_and)
+        tc(v("TB"), v("Ti"))
+        sums("BT%d" % t, 128, "BX1", "BTX", "PC", "PD")
+        turn("TB", 8, "T8")
+        mm(v("PB", 0, P), v("RP", 0, 128, 1, 0, 8), v("T8", 0, P, 1, 0, 8))
+        tc(v("TLu", 0, P), v("PB", 0, P))
+
+    def far(t):
+        nb = nbs(t)
+        V = "VW"[t]
+        by_slot("PG", "MC", "WV", t, 1)
+        for j in range(5):
+            if j < 4:
+                c, br, pm = 2048 + 512 * j, "BR%d" % (j % 2), "PM%d" % (j % 2)
+                act(v(br), ind(v("BTX"), v("TLu", 128 + 32 * j, 160 + 32 * j)))
+                mm(v(pm), v("ID"), v(br), True, False)
+                mm(v(pm), v("NID"), v(V, c, c + 512), False, True)
+            if j > 0:
+                c, pm = 1536 + 512 * j, "PM%d" % ((j - 1) % 2)
+                act(v("MB", c, c + 512), v(pm), AF.Abs)
+        for b in (2, 0):
+            c, n = 2048 * b, 16 * nb[b]
+            tt(v("MB", c, c + n), ind(v("BTX"), v("TLu", 128 * b, 128 * b + nb[b])), v(V, c, c + n), OP.max)
+            if b == 2:
+                ts(v("hs"), v("ki"), 4096, OP.is_lt)
+                ts(v("ok"), v("TB"), -255, OP.add)
+                tt(v("TH"), v("ok"), v("hs"), OP.mult)
+        if t == 0:
+            by_slot("PG", "MC", "WC", t, 2)
+        by_slot("PG", "MB", "WB", t, 2)
+        by_slot("PG", "MB", "WB", t, 0)
+        by_slot("PG", "MB", "WA", t, 1)
+        close("PG")
+
+    def pick(t):
+        P = 288 + 16 * t
+        tree("PG", OP.max, v("ki"))
+        ts(v("ok"), v("ki"), 262160, OP.is_ge)
+        ts(v("lo"), v("ki"), 15, OP.bitwise_and)
+        tt(v("X48", 24, 48), v("ok"), v("TH"), OP.mult)
+        tc(v("X48", 0, 24), v("lo"))
+        turn("X48", 16, "XT")
+        mm(v("PB", 0, 304), v("RP", 128, 256, 1, 0, 16), v("XT", 0, 304, 1, 0, 16))
+        act(v("TS"), v("PB", 0, 304))
+        tt(v("Y"), ind(v("X48", 0, 24), v("L8u")), v("MKU"), OP.mult)
+        mm(v("PD", 0, 24), v("ID"), v("C256"), True, False)
+        for q in range(8):
+            mm(v("PD", 0, 24), v("ZW", 112 - 16 * q, 240 - 16 * q), v("Y", 24 * q, 24 * q + 24), False, q == 7)
+        mm(v("PC", 0, 304), v("RP", 0, 128, 1, 0, 16), v("XT", 0, 304, 1, 0, 16))
+        ts(v("VLu"), v("PD", 0, 24), col(R15), OP.add)
+        for q in range(6, 8):
+            act(v("ZQ", 304 * q, 304 * q + 304), v("TS"), AF.Abs, col(TQB + q), 1000.0)
+        act(v("VB", 0, P), ind(v("VW"[t], 0, 16 * P), v("VLu", 0, P // 16)))
+        for q in range(6):
+            ts(v("ZQ", 304 * q, 304 * q + 304), v("TS"), col(TQ + q), OP.not_equal, 1000, OP.mult)
+        scan(v("SC"), v("D0"), v("ZQ"), 1000.0, OP.add, OP.min)
+        ts(v("QTu"), v("SC", 303, 2432, 304), 303, OP.add, 304, OP.min)
+        tc(v("MV%d" % t), ind(v("VB"), v("QTu")))
+        act(v("LOS", 0, 304), v("PC", 0, 304))
+        movers(t)
+
+    def own(t):
+        ex, x = v("W8", 0, 8), v("W8", 24, 32)
+        ts(ex, v("SC", 303, 2432, 304), 0, OP.is_le)
+        ts(v("OHm"), ind(v("LOS"), v("QTu")), col(F15), OP.is_equal)
+        tt(v("PGm", 0, 128), ind(v("PIf"), v("QTu")), v("OHm"), OP.mult)
+        if t == 0:
+            ts(v("QTo", 0, 1), v("SC", 303 + 304 * r, 304 + 304 * r), 303, OP.add, 304, OP.min)
+            ts(v("OHn"), ind(v("LOS"), v("QTu")), col(F15), OP.not_equal)
+            tt(v("LN"), ind(v("L", 0, 320), v("QTu")), v("OHn"), OP.mult)
+            ts(x, v("SC", 303, 2432, 304), 303 + 3744, OP.add)
+            tt(x, x, v("DMV"), OP.subtract)
+            tt(x, x, ex, OP.mult)
+            tt(x, x, v("DMV"), OP.add)
+            ts(v("QLu"), x, -3744, OP.add)
+            tc(ind(v("L"), v("QLu")), v("LN"))
+        ox = v("W8", r, r + 1)
+        ts(v("sm", 0, 1), ox, -1, OP.mult, 1, OP.add)
+        tt(v("sm", 1, 2), ox, own1(0), OP.mult)
+
+    def own1(o):
+        src = v("PGm", o + 16 * r, o + 16 * r + 16)
+        ts(v("TT", 0, 16), src, col(EVN), OP.mult)
+        ts(v("TT", 16, 32), src, col(ODD), OP.mult)
+        vtr(v("TR", 0, 32), v("TT", 0, 32))
+        tt(v("OH"), v("TR", 0, 16), v("TR", 16, 32), OP.add)
+        tr(v("sm", 10, 11), v("OH"), OP.add)
+        return v("sm", 10, 11)
+
+    def own_c():
+        tt(v("PGm", 128 + 16 * r, 144 + 16 * r), ind(v("CPf"), v("QTo", 0, 1)), v("OHm", 16 * r, 16 * r + 16), OP.mult)
+        tt(v("sm", 8, 9), v("W8", r, r + 1), own1(128), OP.mult)
+
+    def own_ids():
+        for k in range(16):
+            mm(v("PA", 0, 8), v("UF", 15 - k, 143 - k), v("PGm", k, 128, 16), k == 0, k == 15)
+
+    def own2(t):
+        ex, x = v("W8", 0, 8), v("W8", 24, 32)
+        tc(v("W8", 8, 16), v("PA", 0, 8))
+        tt(x, v("W8", 8, 16), v("DMV"), OP.subtract)
+        tt(x, x, ex, OP.mult)
+        tt(x, x, v("DMV"), OP.add)
+        tc(v("MVL"), x)
+
+    def mv_homes(t):
+        tc(ind(v("X0"), v("MVL")), v("MVV%d" % t))
+
+    def land(t):
+        P = 288 + 16 * t
+        nx, a0 = ("XA", 0) if t else ("X1", 3584)
+        arrive("c%d" % t, [v(nx, a0, a0 + 112)])
+        for k in range(16):
+            mm(v("PC", 0, 7), v("U14", 15 - k, 143 - k), v(nx, a0 + k, a0 + 112, 16), k == 0, k == 15)
+        tt(v("kk"), v("PC", 0, 7), v("C7"), OP.mult)
+        km, hw, wo, w, wc = [v("sm", i, i + 1) for i in (2, 3, 4, 5, 9)]
+        nown, ido, ox = v("sm", 0, 1), v("sm", 1, 2), v("W8", r, r + 1)
+        tr(km, v("kk"), OP.max)
+        ts(hw, km, ox, OP.max, 0, OP.is_gt)
+        ts(v("TT", 0, 32), v("RO"), hw, OP.mult)
+        ts(wo, km, -16, OP.mult, col(WO + t), OP.add)
+        ts(w, wo, nown, OP.mult, ido, OP.add)
+        ts(v("TT", 32, 64), v("TT", 0, 32), w, OP.mult)
+        n = 64
+        if t == 0:
+            n = 96
+            ts(wc, wo, nown, OP.mult, v("sm", 8, 9), OP.add)
+            ts(v("TT", 64, 96), v("TT", 0, 32), wc, OP.mult)
+        vtr(v("TR", 0, n), v("TT", 0, n))
+        tt(v("OH"), v("TR", 0, 16), v("TR", 16, 32), OP.add)
+        if t == 0:
+            tt(v("L", P, P + 16), v("GS"), v("OH"), OP.add)
+        for nm, pf, o in (("SPf", "PIf", 32), ("CSf", "CPf", 64)):
+            if nm == "SPf" or t == 0:
+                tt(v("OW"), v("TR", o, o + 16), v("TR", o + 16, o + 32), OP.add)
+                tt(v("g1"), v(nm), v("OH"), OP.mult)
+                tt(v("OW"), v(nm), v("OW"), OP.add)
+                tt(v(pf, P, P + 16), v("OW"), v("g1"), OP.subtract)
+
+    def land_home(t):
+        hw, wo = v("sm", 3, 4), v("sm", 4, 5)
+        ts(v("sm", 6, 7), hw, v("sm", 0, 1), OP.mult)
+        tt(v("sm", 7, 8), wo, col(AR_), OP.subtract)
+        ts(v("ARu", 0, 1), v("sm", 7, 8), v("sm", 6, 7), OP.mult, col(AR_), OP.add)
+        tc(ind(v("X0"), v("ARu", 0, 1)), v("FV"))
+
+    tt(v("L", 0, 288), v("PA", 0, 288), v("SLOT"), OP.is_equal)
+    count(0, 0, 304, True)
+    ts(v("EO"), v("EO"), col(ODD), OP.is_equal)
+    numbers(0)
+    iota(v("IOB"), [[1, 128]])
+    iota(v("C128"), [[128, 16], [0, 24]])
+    iota(v("C15"), [[-1, 16], [0, 24]], 15)
+    iota(v("G2", 128, 136), [[1, 8]])
+    iota(v("G2", 0, 128), [[1, 16], [16, 8]])
+    iota(v("COL", TQ, TQ + 8), [[16, 8]], -255)
+    ts(v("E"), v("E"), col(P_), OP.is_equal)
+    ts(v("I16"), v("I16"), col(M_), OP.is_equal)
+    ts(v("U16"), v("IOT", 0, 144), col(G15), OP.is_equal, col(C16_), OP.mult)
+    split_a(0)
+    vgather(0, 0)
+    act(v("NID"), v("ID"), AF.Copy, 0.0, -1.0)
+    act(v("AA"), v("AD"), AF.Abs)
+    kp("PC", "AA")
+    ms(v("NEI", 288, 320), 0)
+    tc(v("NU", 0, 288), v("NEI", 0, 288))
+    ms(v("FST"), 0)
+    ms(v("FST", 0, 128, 1, 0, 1), 1)
+    mcent(0, 0)
+    split_b(0)
+    vgather(0, 1)
+    split_c(0)
+    ts(col(I0), col(M_), 0, OP.is_equal)
+    ts(col(WCC), col(C13), 48, OP.mult, -16, OP.add)
+    ts(col(WBC), col(WCC), -1, OP.mult)
+    ts(col(WAC), col(C13), -16, OP.mult)
+    ts(col(WVC), col(C13), 16, OP.mult)
+    for nm, wc in (("WC", WCC), ("WB", WBC), ("WA", WAC), ("WV", WVC), ("SEL", I0)):
+        ts(v(nm), v("G2", 128, 136), col(G_), OP.is_equal, col(wc), OP.mult)
+    ts(v("LW"), v("G2", 0, 128), col(P_), OP.is_equal, 262144, OP.mult)
+    split_g()
+    rows_open()
+    vgather(0, 2)
+    for i in range(4):
+        rows(i, ("PN", "PG", "PC", "PD")[i])
+    table(0)
+    near(0, 1, True)
+    mcent(0, 2)
+    near(0, 0)
+    near(0, 2)
+    gain_open(0)
+    by_slot("PG", "MC", "WC", 0, 0)
+    near_sums(0, (1, 0, 2))
+    mcent(0, 1, (0, 1))
+    ts(v("PQ"), v("POI"), 15, OP.bitwise_and)
+    ts(v("PQ2"), v("POI"), 4, OP.arith_shift_right)
+    ts(v("PQ"), v("PQ"), 224, OP.mult)
+    tt(v("PQ"), v("PQ"), v("PQ2"), OP.add)
+    tc(v("PP"), v("PQ"))
+    ts(v("RP", 0, 128), v("G1"), col(P_), OP.is_equal)
+    ts(v("RP", 128, 256), v("G1"), 8, OP.add, col(P_), OP.is_equal)
+    arrive("b0", [v("BT0")])
+    targets(0)
+    mcent(0, 1, (2, 3))
+    for i in range(4, 8):
+        rows(i, ("PC", "PD")[i % 2])
+    iota(v("ZW"), [[1, 240]], -112)
+    iota(v("G3"), [[0, 24], [1, 8]])
+    iota(v("L8f"), [[2, 12]])
+    iota(v("C256"), [[256, 24]])
+    iota(v("DMV"), [[16, 8]], 4064)
+    iota(v("C7"), [[-1, 7]], 7)
+    iota(v("D0"), [[0, 2432]], -1)
+    iota(v("D0", 0, 2432, 304), [[0, 8]], 5000)
+    iota(v("VB"), [[0, 320]])
+    iota(v("LOS", 304, 320), [[0, 16]])
+    iota(v("MVV0"), [[0, 128]], 255)
+    iota(v("MVV1"), [[0, 128]], 255)
+    iota(v("TAB1"), [[0, 2688]], 4096)
+    far(0)
+    ts(col(K16), col(M_), 16, OP.mult, 16, OP.add)
+    for t in range(2):
+        ts(col(H18 + t), col(K14), 18 + t, OP.mult)
+        ts(col(WO + t), col(M_), 3584 + 112 * t + 112, OP.add)
+    ts(v("DGO"), v("C16k"), col(M_), OP.add, 3808, OP.add)
+    split_d(0)
+    ts(v("ZW"), v("ZW"), col(M_), OP.is_equal, -1, OP.mult)
+    ts(v("MKU"), v("G3"), col(G_), OP.is_equal)
+    ts(v("L8u"), v("L8f"), col(GE8), OP.add)
+    ts(v("COL", TQ, TQ + 8), v("COL", TQ, TQ + 8), col(M_), OP.add)
+    ts(v("COL", TQB, TQB + 8), v("COL", TQ, TQ + 8), -1000, OP.mult)
+    ts(col(F15), col(M_), -1, OP.mult, 15, OP.add)
+    act(v("YR", 0, 2048), ind(v("AR"), v("PP", 0, 128)))
+    pick(0)
+    act(v("YR", 2048, 4096), ind(v("AR"), v("PP", 128, 256)))
+    act(v("YR", 4096, 4608), ind(v("AR"), v("PP", 256, 288)))
+    act(v("X1", 0, 3584), v("X1", 0, 3584), AF.Copy, 0.0, col(C13))
+    ts(v("DMV"), v("DMV"), col(M_), OP.add)
+    for t in range(2):
+        act(v("HV%d" % t), v("IOT"), AS, col(H18 + t), col(K15))
+    ts(col(UCC), col(I0), 8, OP.add)
+    ts(col(UCC), col(M_), col(UCC), OP.is_equal, col(I0), OP.add)
+    ts(v("UC"), v("IOT", 0, 144), col(G15), OP.is_equal, col(UCC), OP.mult)
+    ts(v("UF"), v("IOT", 0, 144), col(G15), OP.is_equal)
+    ts(v("U14"), v("IOT", 0, 144), col(G15), OP.is_equal, col(K14), OP.mult)
+    own(0)
+    for a, b in ((0, 128), (128, 288)):
+        for m in range(16):
+            mm(v("PN", a, b), v("UC", 15 - m, 143 - m), v("YR", 16 * a + m, 16 * b, 16), m == 0, m == 15)
+    tc(v("CPf", 0, 288), v("PN", 0, 288))
+    tc(v("CSf"), ind(v("CPf"), v("pk2", 0, 1)))
+    count(1, 0, 288, True)
+    own_c()
+    tc(v("CU", 0, 288), v("CPf", 0, 288))
+    land(0)
+    count(1, 288, 320, False)
+    numbers(1)
+    tc(v("PU", 288, 304), v("PIf", 288, 304))
+    split_a(1)
+    act(v("AA"), v("AD"), AF.Abs)
+    kp("PC", "AA")
+    centres(1)
+    tc(v("CU", 288, 304), v("CPf", 288, 304))
+    act(v("V", 4608, 4864), ind(v("X1", 0, 3808), v("PU", 288, 304)), AS, col(K14), col(C13))
+    dma("s", v("ypost", 0, 304), v("PIf", 0, 304))
+    split_b(1)
+    split_c(1)
+    vgather(1, 0)
+    mcent(1, 0)
+    own_ids()
+    split_g()
+    table(1)
+    for b in range(3):
+        near(1, b)
+    vgather(1, 1)
+    vgather(1, 2)
+    mcent(1, 2)
+    gain_open(1)
+    by_slot("PG", "MC", "WC", 1, 0)
+    by_slot("PG", "MC", "WC", 1, 2)
+    near_sums(1, (0, 1, 2))
+    mcent(1, 1, (0, 1))
+    ts(col(AR_), col(M_), 4192, OP.add)
+    ms(v("X0", 3584, 3808), 255)
+    own2(0)
+    go_homes(0)
+    mv_homes(0)
+    land_home(0)
+    arrive("b1", [v("BT1")])
+    targets(1)
+    mcent(1, 1, (2, 3))
+    far(1)
+    split_d(1)
+    go_homes(1)
+    pick(1)
+    own(1)
+    own_ids()
+    own2(1)
+    mv_homes(1)
+    dma("s", v("yh", 0, 3584, 1, 0, 16, 2), v("X0", 0, 3584, 1, 14, 128, 16))
+    dma("a", v("yh", 0, 3584, 1, 1, 16, 2), v("X0", 0, 3584, 1, 15, 128, 16))
+    ts(col(BC), col(C13), -1, OP.mult, 1, OP.add)
+    land(1)
+    dma("s", v("ypost", 304, 320), v("PIf", 304, 320))
+    land_home(1)
+    ts(v("YA", 0, 112), v("X1", 3584, 3696), col(C13), OP.mult)
+    ts(v("YA", 112, 224), v("XA"), col(C13), OP.mult)
+    ts(v("YB"), v("X0", 3584, 3808), col(BC), OP.mult)
+    tt(v("YA"), v("YA"), v("YB"), OP.add)
+    dma("a", v("ya"), v("YA"))
+    cnt["ls"] = nls[0]
+    waits("g", {s: (n, {}) for s, n in cnt.items() if n})

@@ -3,39 +3,42 @@ from concourse.mybir import AluOpType as OP, AxisListType, ActivationFunctionTyp
 
 F, B, I, U, H16 = "float32", "bfloat16", "int32", "uint16", "float16"
 _W = {
-    B: "X0 4208 XB 3584 X1 3808 XA 112 H 4608 V 4864 W 4864 MC 4864 MB 4864 TN 4864 CEN 288 CE 320 TAB0 2688 TAB1 2688 L 448 LO 320 F0 320 F1 320 INC 320 LE 320 ZER 384 Z 320 BT0 128 BT1 128 MV0 128 MV1 128 "
-       "VS 272 VSa 256 VSc 256 AD 256 BD 256 AA 256 BA 256 LS2 32 LT 32 RB 16 GE 32 GT 32 GS 16 LS16 16 CX1 304 CEX 304 CXT 384 E 2048 TB 24 TH 24 T8 384 BX1 128 BTX 128 X48 48 XT 384 TS 304 ZQ 2432 D0 2432 "
-       "Y 192 VB 320 LOS 320 OHn 128 LN 128 FV 16 RB2 16 MVV0 128 MVV1 128 YA 224 YB 224 BO 128 TRI 128 ID 128 NID 128 U16 144 U14 144 UH 144 UC 144 WC 8 WB 8 WA 8 WV 8 SEL 8 LW 128 ZW 240 MKU 192 I16 16 EO 32 C31 16 "
-       "IOB 128 C128 384 C15 384 C256 24 HV0 256 HV1 256 SA 128 SB1 128 SB2 128 RP 256 FST 128 BR0 512 BR1 512 TA 128 TB2 128 AH 224 AL 224 DA 224 DB 224 AR 3584 YR 4608 S1 128 S2 128 S3 128 S4 128 RM 1024",
-    F: "PIf 320 SLOT 288 MA 320 pk 2 t2 1 SPf 16 CSf 16 LAf 16 LK 16 KL 16 KA 16 obf 1 g1 16 GO 16 RO 32 mx 1 T1 192 T2 192 T3 96 T4 48 hs 24 ok 24 OHm 128 PGm 256 W8 40 GLf 16 kk 7 sm 16 TT 96 TR 96 OH 16 OW 16 COL 48 "
-       "IOT 256 IOS 288 G1 128 G2 136 G3 192 UF 144 L8f 12 C16 16 C16k 16 DGO 16 DMV 8 C7 7 CPf 320",
-    I: "POI 288 ABI 448 NEI 320 NL0 32 NL1 32 kx 1 kr 1 ki 24 Ti 24 lo 24 IC 4 AI 224 PQ 288 PQ2 288",
-    U: "PU 304 ABU 224 NU 304 pk2 2 NLu 8 SPu 16 CSu 16 LAu 16 obu 2 LBu 16 TLu 304 QTu 8 QTo 2 VLu 24 QLu 8 MVL 8 GLu 16 ARu 2 L8u 12 CU 304 PP 288",
-    H16: "SC 2432",
+    B: "X0 4064 XB 3584 X1 3808 XA 112 H 4864 V 4864 W 4864 MC 4864 MB 4864 TN 4864 CE 320 TAB0 2688 TAB1 2688 L 448 LO 320 LB 320 F0 320 F1 320 INC 320 JK 320 ZER 384 Z 320 "
+       "BT0 128 BT1 128 MV0 128 MV1 128 BQ 304 VS 272 VSa 256 VSc 256 AD 256 BD 256 AA 256 BA 256 LSE 128 LS 16 GS 16 NG 16 RO 16 RB 16 A2 448 S3 512 TS 304 ZQ 2432 D0 304 Y 192 VB 320 LN 128 FV 16 FD 112 WN 112 "
+       "MVV0 128 MVV1 128 YA 224 YB 112 BO 128 TRI 128 ID 128 NID 128 IDL 128 U16 144 UN16 144 UH 144 UC 144 W8 48 ZW 240 MKU 192 I16 16 I17 16 C15 16 IOB 128 C256 24 HV0 256 HV1 256 FST 128 "
+       "CNG 384 U1 144 RP 256 X24 24 L24 24 T8 304 L8 304 LOS 320 OHm 128 DN 384 DG 384 CO0 128 CO1 128 CO2 128 CO3 128 RN 128 RC 128 B15 128 PR0 128 PR1 128 D1 128 XM 112 TH 24",
+    F: "PIf 320 PIm 320 PB_ 320 CPf 320 SLOT 288 MA 320 acc 4 t1 4 SPf 16 CSf 16 LAf 16 g1 16 g2 16 g3 16 exo 16 ROo 16 SPo 16 CSo 16 T2 16 T3 16 xw 16 hs 24 t24 24 GLf 16 QLf 8 COL 64 "
+       "IOT 256 IOS 288 G1 128 G2 128 G3 192 G8 8 SQ 24 L8f 12 C16k 16 DGO 16 DQ 8 DM 8 ZC0 112 ZC1 112 X15f 24 K86f 8",
+    I: "POI 288 ABI 448 NEI 320 kx 1 kr 1 kn 384 ki 384 Ti 24 lo 24 IC 4 AI 224 AJ 224 nn 128 iw 16",
+    U: "PU 304 ABU 224 NU 304 pk8 8 NO0 2 NO1 2 NL0 8 NL1 8 SPu 16 CSu 16 LAu 16 obu 2 LBu 16 TLu 24 QTu 8 VLu 24 QLu 8 MVL 8 GLu 16 L8u 12 CU 304 X15 24 XS 24 K86 8 K7 8",
+    H16: "SC 2432 PGh 128 UF 144 BOh 128 IDh 128 DMh 8",
 }
 _S = {}
 for _d, _t in _W.items():
     _t = _t.split()
     for _i in range(0, len(_t), 2):
         _S[_t[_i]] = (int(_t[_i + 1]), _d)
-_PS = ["PA", "PB", "PC", "PD", "PN", "PG", "PM0", "PM1"]
-SCRATCH = {}
-_PACK = {}
-_n = {F: 0, I: 0, B: 0}
-for _k in ("g1 KL KA LK GO RO LAf SPf CSf T3 T4 hs ok kk sm OH OW GLf W8 DGO DMV C7 C16 C16k obf t2 pk mx L8f TT TR G1 G2 G3 OHm kx kr ki Ti lo IC AI WC WB WA WV SEL I16 EO C31 GE GT LT LS2 RB RB2 "
-           "TB TH C256 LW MKU BO TRI ID NID FST SA SB1 SB2 IOB UH UC U14 U16 ZW RP LS16 GS S1 S2 S3 S4 TA TB2 BX1 Y OHn LN FV AH AL DA DB VSc VSa AD BD AA BA Z").split():
-    _w, _d = _S[_k]
-    _PACK[_k] = ("PK" + _d, _n[_d])
-    _n[_d] += (_w + 15) // 16 * 16
+_PS = ["PA", "PB", "PC", "PX", "PN", "PG", "PM0", "PM1"]
+_OWN = ("X0 XB X1 XA H V W MC MB TN CE TAB0 TAB1 L LO LOS BT0 BT1 MV0 MV1 VS S3 ZQ VB FV YA PIf PIm CPf MA POI ABI NEI kn ki Ti lo nn SC").split()
+SCRATCH, _PACK, _n = {}, {}, {}
 for _k, (_w, _d) in _S.items():
-    if _k not in _PACK:
+    if _k in _OWN or _d == U:
         SCRATCH[_k] = ("sbuf", [128, _w], _d)
-for _d in (F, I, B):
+    else:
+        _PACK[_k] = ("PK" + _d, _n.get(_d, 0))
+        _n[_d] = _n.get(_d, 0) + (_w + 15) // 16 * 16
+for _d in _n:
     SCRATCH["PK" + _d] = ("sbuf", [128, _n[_d]], _d)
 for _k in _PS:
     SCRATCH[_k] = ("psum", [128, 512], F)
 _EX = ["a0", "b0", "c0", "a1", "b1", "c1"]
-SEMAPHORES = ["cv", "ca", "ct", "cg"] + ["r" + e for e in _EX] + ["y" + e for e in _EX] + ["ls"] + ["d%d" % i for i in range(20)]
+SEMAPHORES = ["cv", "ca", "ct", "cg"] + ["r" + e for e in _EX] + ["y" + e for e in _EX] + ["ls"] + ["d%d" % i for i in range(16)]
+MS = (4, 8, 4, 8)
+KA = (2, 2)
+PEN, MARG, SLK = 3000, 500, 100
+CH = 32
+NACT = 5
+GA, SCA, HOP, NET, DMA = 1.6, 3.8, 130, 3000, 1800
 
 
 def bits(es):
@@ -57,30 +60,26 @@ def plan(r, T, topo):
     c = T.cores[r]
     direct = [d for d in range(len(T.cores)) if d != r and topo.may_write(c, T.cores[d])]
     cross = [d for d in range(len(T.cores)) if d != r and d not in direct]
-    rel = [x for x in topo.cores_of(c) if x != c and topo.die(x) == topo.die(c) and T.rank_of(x) is None and all(topo.may_write(x, T.cores[d]) for d in cross)]
-    rel = rel[:2] if cross else []
-    return direct, [(x, cross[i::len(rel)]) for i, x in enumerate(rel)]
+    rel = [x for x in topo.cores_of(c) if x != c and topo.die(x) == topo.die(c) and T.rank_of(x) is None and all(topo.may_write(x, T.cores[d]) for d in cross)][:2]
+    off = topo.engines(c, T.cores[direct[0]])
+    return direct, [(x, cross[i::len(rel)]) for i, x in enumerate(rel)], off, [e for e in topo.engines(c, rel[0]) if e not in off]
 
 
-def masks_c(r, T, topo):
-    direct, rel = plan(r, T, topo)
-    c, last, on = T.cores[r], {}, {}
-    if direct:
-        for d, es in zip(direct, parts(topo.engines(c, T.cores[direct[0]]), len(direct))):
-            last[d] = es
-    ds = [(x, d) for x, q in rel for d in q]
-    if ds:
-        for (x, d), es in zip(ds, parts(topo.engines(c, ds[0][0]), len(ds))):
-            on[d] = es
-    for x, q in rel:
-        for d, es in zip(q, parts(topo.engines(x, T.cores[q[0]]), len(q))):
-            last[d] = es
-    return last, on
+def engines_to(ex, r, d, T, topo):
+    direct, rel, off, on = plan(r, T, topo)
+    q, es = [(direct, off)] + [(q, topo.engines(x, T.cores[d])) for x, q in rel if d in q], None
+    q, es = q[-1]
+    return parts(es, len(q))[q.index(d)] if ex[0] == "c" else es
 
 
-def spot(T, r, d, t):
-    a = (0 if t else 3584) + (r if r < d else r - 1) * 16
-    return T["XA" if t else "X1"][:, a:a + 16]
+def message(ex, r, d, T):
+    t, o = ex[1], r if r < d else r - 1
+    if ex[0] == "a":
+        return T["NO" + t][:, 0:1], T["NL" + t][:, o:o + 1]
+    if ex[0] == "b":
+        return T["BT" + t][:, 16 * r:16 * r + 16], T["BT" + t][:, 16 * r:16 * r + 16]
+    a = 16 * o + (3584 if t == "0" else 0)
+    return T["MV" + t][:, 16 * d:16 * d + 16], T["X1" if t == "0" else "XA"][:, a:a + 16]
 
 
 def dst(topo, x, c):
@@ -88,27 +87,24 @@ def dst(topo, x, c):
     return DstId(rid=rid, pnc=pid)
 
 
+def onward(ex, r, q, core, T, topo):
+    if ex[0] == "c":
+        return [RemoteDMATransfer(dst_ids=[dst(topo, T.cores[d], core)], dma_engine_mask=bits(engines_to(ex, r, d, T, topo)), remote_sem=T.sem["y" + ex],
+                                  src=message(ex, r, d, T)[0], dst=message(ex, r, d, T)[1]) for d in q]
+    return [RemoteDMATransfer(dst_ids=[dst(topo, T.cores[d], core) for d in q], dma_engine_mask=bits(engines_to(ex, r, q[0], T, topo)), remote_sem=T.sem["y" + ex],
+                              srcs=[message(ex, r, q[0], T)[0]], dsts=[message(ex, r, d, T)[1] for d in q])]
+
+
 def relay_program(g, core, T, topo):
     for r in range(len(T.cores)):
-        direct, rel = plan(r, T, topo)
+        direct, rel, off, on = plan(r, T, topo)
         for x, q in rel:
             if x == core:
                 n = 0
-                last, on = masks_c(r, T, topo)
                 for ex in _EX:
-                    k, t = ex[0], int(ex[1])
-                    sr = T.sem["y" + ex]
-                    if k == "c":
-                        g.wait_ge(T.sem["r" + ex], sum(len(on[d]) for d in q))
-                        g.remote_dma_fused([RemoteDMATransfer(dst_ids=[dst(topo, T.cores[d], core)], dma_engine_mask=bits(last[d]), remote_sem=sr, src=T["MV%d" % t][:, 16 * d:16 * d + 16],
-                                                              dst=spot(T, r, d, t)) for d in q], local_sem=T.sem.ls)
-                        n += sum(len(last[d]) for d in q)
-                    else:
-                        es = topo.engines(core, T.cores[q[0]])
-                        ap = T["NL%d" % t][:, 4 * r:4 * r + 1] if k == "a" else T["BT%d" % t][:, 16 * r:16 * r + 16]
-                        g.wait_ge(T.sem["r" + ex], len(topo.engines(T.cores[r], core)))
-                        g.remote_dma_fused([RemoteDMATransfer(dst_ids=[dst(topo, T.cores[d], core) for d in q], dma_engine_mask=bits(es), remote_sem=sr, srcs=[ap], dsts=[ap for d in q])], local_sem=T.sem.ls)
-                        n += len(es)
+                    g.wait_ge(T.sem["r" + ex], len(on) // len(rel) if ex[0] == "c" else len(on))
+                    g.remote_dma_fused(onward(ex, r, q, core, T, topo), local_sem=T.sem.ls)
+                    n += len(topo.engines(core, T.cores[q[0]]))
                 g.wait_ge(T.sem.ls, n)
 
 
@@ -119,783 +115,626 @@ def rank_program(g, core, T, topo):
         return
     N = len(T.cores)
     E = {"v": g.vector, "a": g.scalar, "t": g.tensor, "g": g, "s": g.sync}
-    CS = {"v": "cv", "a": "ca", "t": "ct", "g": "cg"}
-    cnt = {}
-    know = {e: {} for e in E}
-    hist = {}
-    ndma = [0]
+    ops, hist, ndma = [], {}, [0]
 
     def v(n, a=0, b=None, st=1, p0=0, p1=128, ps=1):
         w = _S[n][0] if n in _S else (512 if n in _PS else T[n].shape[1])
         b = w if b is None else b
-        if n in _PACK:
-            nn, o = _PACK[n]
-            return (nn, a + o, b + o, st, p0, p1, ps)
-        return (n, a, b, st, p0, p1, ps)
+        nn, o = _PACK.get(n, (n, 0))
+        return (nn, a + o, b + o, st, p0, p1, ps)
 
     def ind(w, o):
         return ("IND", w, o)
 
     def ap(x):
+        if not isinstance(x, tuple):
+            return x
         if x[0] == "IND":
             return ap(x[1]).indirect(ap(x[2]))
         n, a, b, st, p0, p1, ps = x
         if ps != 1:
             return T[n][p0:p1:ps, a:b]
-        if p0 == 0 and p1 == 128:
-            return T[n][:, a:b] if st == 1 else T[n][:, a:b:st]
         return T[n][p0:p1, a:b] if st == 1 else T[n][p0:p1, a:b:st]
 
     def regs(xs):
-        out = []
-        for x in xs:
-            if isinstance(x, tuple):
-                out += [x[1], x[2]] if x[0] == "IND" else [x]
-        return out
+        return [y for x in xs if isinstance(x, tuple) for y in (x[1:] if x[0] == "IND" else [x])]
 
-    def deps(eng, outs, ins):
-        need = {}
-        for w, xs in ((True, outs), (False, ins)):
-            for x in xs:
-                ps = x[0] in _PS
-                for h in hist.get(x[0], []):
-                    if ps:
-                        if h["e"] == eng and (eng == "t" or not (w or h["w"])):
-                            continue
-                    else:
-                        if h["b"] <= x[1] or h["a"] >= x[2] or not (w or h["w"]):
-                            continue
-                        if h["st"] > 1 and h["st"] == x[3] and (h["a"] - x[1]) % x[3]:
-                            continue
-                    if need.get(h["s"], (0, None))[0] < h["n"]:
-                        need[h["s"]] = (h["n"], h["k"])
-        return need
+    def width(x):
+        return 16 * (x[2][2] - x[2][1]) if x[0] == "IND" else (x[2] - x[1] + x[3] - 1) // x[3]
 
-    def waits(eng, need):
-        for s, (n, k) in sorted(need.items(), key=lambda z: -len(z[1][1])):
-            if know[eng].get(s, 0) < n:
-                E[eng].wait_ge(T.sem[s], n)
-                for a, b in k.items():
-                    know[eng][a] = max(know[eng].get(a, 0), b)
-                know[eng][s] = n
+    def short(x):
+        return x[0] not in _PS and SCRATCH[x[0]][2] in (B, U, H16)
 
-    def note(eng, sem, n, outs, ins, k):
-        for w, xs in ((True, outs), (False, ins)):
+    def step(alt, outs, ins, acc=False, sem=None, lat=HOP):
+        o, i = regs([x[1] if x[0] == "IND" else x for x in outs]), regs(ins) + [x[2] for x in outs if x[0] == "IND"]
+        me, pre, one = len(ops), {}, list(alt)[0] if len(alt) == 1 else None
+        for w, xs in ((True, o), (False, i)):
             for x in xs:
                 hs = hist.setdefault(x[0], [])
-                if x[0] in _PS:
-                    hs[:] = [h for h in hs if not (h["e"] == eng and h["w"] == w)]
-                elif w and x[3] == 1 and x[4] == 0 and x[5] == 128:
-                    hs[:] = [h for h in hs if not (h["a"] >= x[1] and h["b"] <= x[2])]
-                elif not w:
-                    hs[:] = [h for h in hs if not (h["e"] == eng and h["s"] == sem and not h["w"] and h["a"] >= x[1] and h["b"] <= x[2])]
-                hs.append({"a": x[1], "b": x[2], "st": x[3], "w": w, "e": eng, "s": sem, "n": n, "k": k})
+                for h in hs:
+                    y = h[0]
+                    if x[0] in _PS:
+                        if (acc and w and h[3]) or (not w and not h[1] and one and ops[h[2]]["one"] == one):
+                            continue
+                    elif y[2] <= x[1] or y[1] >= x[2] or not (w or h[1]) or y[5] <= x[4] or y[4] >= x[5] or (y[3] == x[3] and (y[1] - x[1]) % x[3]):
+                        continue
+                    pre[h[2]] = True
+        for w, xs in ((True, o), (False, i)):
+            for x in xs:
+                hs = hist[x[0]]
+                if w and not acc and (x[0] in _PS or (x[3] == 1 and x[4] == 0 and x[5] == 128)):
+                    hs[:] = [h for h in hs if not (x[0] in _PS or (h[0][1] >= x[1] and h[0][2] <= x[2]))]
+                hs.append((x, w, me, acc and w))
+        ops.append({"alt": alt, "one": one, "pre": [p for p in pre if p != me], "sem": sem, "lat": lat})
+        return me
 
-    def run(eng, fn, outs, ins, sem=None, inc=1):
-        o, i = regs(outs), regs(ins)
-        i = i + [x[2] for x in outs if x[0] == "IND"]
-        waits(eng, deps(eng, o, i))
-        s = sem or CS[eng]
-        fn().then_inc(T.sem[s], inc)
-        cnt[s] = cnt.get(s, 0) + inc
-        note(eng, s, cnt[s], o, i, dict(know[eng]))
+    def cost(o, xs, two=False):
+        n = width(o)
+        if o[0] == "IND":
+            return 60 + SCA * n
+        if xs[0][0] == "IND":
+            return 60 + GA * n
+        n = width(xs[0])
+        return max(64, 2 * n if two and not any(x[0] in _PS for x in xs) else (n / 2 if not two and short(o) and all(short(x) for x in xs) else n))
 
-    def s_(x):
-        return ap(x) if isinstance(x, tuple) else x
+    def on_v(fn, o, xs, c):
+        return step({"v": (lambda: [fn()], c)}, [o], xs)
 
     def tt(o, a, b, op):
-        run("v", lambda: g.vector.tensor_tensor(ap(o), ap(a), ap(b), op), [o], [a, b])
+        on_v(lambda: g.vector.tensor_tensor(ap(o), ap(a), ap(b), op), o, [a, b], cost(o, [a, b], True))
+
+    def f_ts(o, a, s1, op0, s2=None, op1=None):
+        if op1 is None:
+            return lambda: g.vector.tensor_scalar(ap(o), ap(a), ap(s1), None, op0)
+        return lambda: g.vector.tensor_scalar(ap(o), ap(a), ap(s1), ap(s2), op0, op1)
+
+    def plain(*xs):
+        return all(not isinstance(x, tuple) or (x[0] != "IND" or x is not xs[0]) and all(y[0] in _PS or SCRATCH[y[0]][2] in (F, B) for y in regs([x])[:1]) for x in xs)
 
     def ts(o, a, s1, op0, s2=None, op1=None):
-        if op1 is None:
-            run("v", lambda: g.vector.tensor_scalar(ap(o), ap(a), s_(s1), None, op0), [o], [a, s1])
+        if plain(o, a) and not any(x[0] in _PS for x in regs([s1, s2])) and (op0, op1) in ((OP.mult, None), (OP.add, None), (OP.mult, OP.add)):
+            lin(o, a, None if op0 == OP.add else s1, s1 if op0 == OP.add else s2)
         else:
-            run("v", lambda: g.vector.tensor_scalar(ap(o), ap(a), s_(s1), s_(s2), op0, op1), [o], [a, s1, s2])
+            on_v(f_ts(o, a, s1, op0, s2, op1), o, [a, s1, s2], cost(o, [a]))
 
     def tc(o, a):
-        run("v", lambda: g.vector.tensor_copy(ap(o), ap(a)), [o], [a])
-
-    def tr(o, a, op):
-        run("v", lambda: g.vector.tensor_reduce(ap(o), ap(a), AxisListType.X, op), [o], [a])
-
-    def vtr(o, a):
-        run("v", lambda: g.vector.transpose(ap(o), ap(a)), [o], [a])
+        if plain(o, a):
+            lin(o, a)
+        else:
+            on_v(lambda: g.vector.tensor_copy(ap(o), ap(a)), o, [a], cost(o, [a]))
 
     def scan(o, a, b, init, op0, op1):
-        run("v", lambda: g.vector.tensor_tensor_scan(ap(o), ap(a), ap(b), s_(init), op0, op1), [o], [a, b, init])
+        on_v(lambda: g.vector.tensor_tensor_scan(ap(o), ap(a), ap(b), ap(init), op0, op1), o, [a, b, init], cost(o, [a, b]))
 
     def ms(o, c):
-        run("v", lambda: g.vector.memset(ap(o), c), [o], [])
+        on_v(lambda: g.vector.memset(ap(o), c), o, [], cost(o, [o]))
 
-    def act(o, a, f=AF.Copy, bias=0.0, scale=1.0):
-        run("a", lambda: g.scalar.activation(ap(o), ap(a), f, s_(bias), s_(scale)), [o], [a, bias, scale])
+    def c_act(a):
+        return 80 + GA * width(a) if a[0] == "IND" else max(64, width(a))
 
-    def mm(o, l, x, start=True, stop=True):
-        run("t", lambda: g.tensor.matmul(ap(o), ap(l), ap(x), start, stop), [o], [l, x])
+    def act(o, a, f=AF.Copy, bias=0.0, scale=1.0, acc=None):
+        step({"a": (lambda: [g.scalar.activation(ap(o), ap(a), f, ap(bias), ap(scale), accum_out=ap(acc))], c_act(a))}, [o] + ([acc] if acc else []), [a, bias, scale])
+
+    def lin(o, a, scale=None, bias=None):
+        if scale is None and bias is None:
+            fv = lambda: g.vector.tensor_copy(ap(o), ap(a))
+        else:
+            fv = f_ts(o, a, 1.0 if scale is None else scale, OP.mult, 0.0 if bias is None else bias, OP.add)
+        fa = lambda: g.scalar.activation(ap(o), ap(a), AF.Copy if bias is None else AF.Identity, 0.0 if bias is None else ap(bias), 1.0 if scale is None else ap(scale))
+        step({"v": (lambda: [fv()], cost(o, [a])), "a": (lambda: [fa()], c_act(a))}, [o], [a, scale, bias])
+
+    def mm(*ms_, acc=False):
+        c = sum(max(min(64, width(x[1])), width(x[2])) / 2 for x in ms_)
+        step({"t": (lambda: [g.tensor.matmul(ap(o), ap(l), ap(x), s0, s1) for o, l, x, s0, s1 in ms_], c)}, [x[0] for x in ms_], [y for x in ms_ for y in x[1:3]], acc)
 
     def iota(o, pat, base=0, ch=0):
-        run("g", lambda: g.iota(ap(o), pat, base, ch, allow_small_or_imprecise_dtypes=True), [o], [])
+        step({"g": (lambda: [g.iota(ap(o), pat, base, ch, allow_small_or_imprecise_dtypes=True)], 160 + 2 * width(o))}, [o], [])
 
-    def dma(q, o, a):
-        s = "d%d" % ndma[0]
+    def fill(o, c):
+        step({"g": (lambda: [g.iota(ap(o), [[0, width(o)]], c, 0, allow_small_or_imprecise_dtypes=True)], 160 + 2 * width(o)),
+              "v": (lambda: [g.vector.memset(ap(o), c)], cost(o, [o]))}, [o], [])
+
+    def dma(q, pairs, lat=DMA):
         ndma[0] += 1
-        run(q, lambda: (g.sync if q == "s" else g.scalar).dma_start(ap(o), ap(a)), [o], [a], s, 16)
+        step({q: (lambda: [E[q].dma_start(ap(o), ap(a)) for o, a in pairs], 60 * len(pairs))}, [o for o, a in pairs], [a for o, a in pairs], sem="d%d" % (ndma[0] - 1), lat=lat)
 
-    direct, rel = plan(r, T, topo)
-    last, on = masks_c(r, T, topo)
-    nls = [0]
+    direct, rel, off, on = plan(r, T, topo)
+    cnt = {"ls": 0}
 
-    def bcast(ex, x):
-        waits("g", deps("g", [], [x]))
-        rs = [c for c, q in rel]
-        if rs:
-            es = topo.engines(core, rs[0])
-            g.remote_dma_fused([RemoteDMATransfer(dst_ids=[dst(topo, c, core) for c in rs], dma_engine_mask=bits(es), remote_sem=T.sem["r" + ex], srcs=[ap(x)], dsts=[ap(x) for c in rs])], local_sem=T.sem.ls)
-            nls[0] += len(es)
-        if direct:
-            es = topo.engines(core, T.cores[direct[0]])
-            g.remote_dma_fused([RemoteDMATransfer(dst_ids=[dst(topo, T.cores[d], core) for d in direct], dma_engine_mask=bits(es), remote_sem=T.sem["y" + ex], srcs=[ap(x)], dsts=[ap(x) for d in direct])], local_sem=T.sem.ls)
-            nls[0] += len(es)
-
-    def movers(t):
-        ex, nm = "c%d" % t, "MV%d" % t
-        waits("g", deps("g", [], [v(nm)]))
-        x_ = [RemoteDMATransfer(dst_ids=[dst(topo, x, core)], dma_engine_mask=bits(on[d]), remote_sem=T.sem["r" + ex], src=T[nm][:, 16 * d:16 * d + 16], dst=T[nm][:, 16 * d:16 * d + 16]) for x, q in rel for d in q]
-        if x_:
-            g.remote_dma_fused(x_, local_sem=T.sem.ls)
-            nls[0] += sum(len(e) for e in on.values())
-        x_ = [RemoteDMATransfer(dst_ids=[dst(topo, T.cores[d], core)], dma_engine_mask=bits(last[d]), remote_sem=T.sem["y" + ex], src=T[nm][:, 16 * d:16 * d + 16], dst=spot(T, r, d, t)) for d in direct]
-        if x_:
-            g.remote_dma_fused(x_, local_sem=T.sem.ls)
-            nls[0] += sum(len(last[d]) for d in direct)
-
-    def arrive(ex, regions):
-        n = 0
-        for q in range(N):
-            if q != r:
-                dq, rq = plan(q, T, topo)
-                if ex[0] == "c":
-                    n += len(masks_c(q, T, topo)[0][r])
-                elif r in dq:
-                    n += len(topo.engines(T.cores[q], T.cores[dq[0]]))
-                else:
-                    x, k = [(x, k) for x, k in rq if r in k][0]
-                    n += len(topo.engines(x, T.cores[k[0]]))
-        cnt["y" + ex] = n
-        for x in regions:
-            hist.setdefault(x[0], []).append({"a": x[1], "b": x[2], "st": x[3], "w": True, "e": "net", "s": "y" + ex, "n": n, "k": {}})
+    def exchange(ex, x, lands):
+        if ex[0] == "c":
+            ds = [(c, d) for c, q in rel for d in q]
+            tr = [RemoteDMATransfer(dst_ids=[dst(topo, c, core)], dma_engine_mask=bits(es), remote_sem=T.sem["r" + ex], src=message(ex, r, d, T)[0], dst=message(ex, r, d, T)[0])
+                  for (c, d), es in zip(ds, parts(on, len(ds)))]
+        else:
+            tr = [RemoteDMATransfer(dst_ids=[dst(topo, c, core) for c, q in rel], dma_engine_mask=bits(on), remote_sem=T.sem["r" + ex], srcs=[ap(x)], dsts=[ap(x) for c in rel])]
+        tr += onward(ex, r, direct, core, T, topo)
+        cnt["ls"] += len(on) + len(off)
+        s = step({"g": (lambda: [g.remote_dma_fused(tr, local_sem=T.sem.ls)][1:], 400)}, [], [x], lat=NET * (2 if ex == "a0" else 1))
+        cnt["y" + ex] = sum(len(engines_to(ex, q, r, T, topo)) for q in range(N) if q != r)
+        ops[step({"n": (None, 1)}, lands, [], sem="y" + ex, lat=HOP)]["pre"].append(s)
 
     def col(i):
         return v("COL", i, i + 1)
 
-    (P_, M_, G_, G15, ODD, EVN, C13, K14, K15, C16_, UHC, WCC, R15, F15, I0, BC, LT8, GE8, K16, AR_, SAW, SBW, WBC, WAC, WVC, UCC, P1_, G14, WO, WO1, H18, H19) = range(32)
+    (P_, M_, G_, G15, C13, K14, K15, K45, UHC, UCC, C16_, CN16, R15, I0, BC, B255, LT8, GE8, MH, RNC, K256, F15, H18, H19, WC0) = range(25)
     TQ, TQB = 32, 40
     AS = AF.Identity
-
-    dma("s", v("POI"), v("post"))
-    dma("s", v("X0", 0, 1792), v("rec", 0, 1792))
-    dma("a", v("X0", 1792, 3584), v("rec", 1792, 3584))
-    dma("s", v("ABI"), v("absorb"))
-    dma("a", v("CEN"), v("cen"))
-    dma("s", v("XB"), v("rec"))
-    dma("s", v("NEI", 0, 288), v("near"))
-    ic = [v("IC", i, i + 1) for i in range(4)]
-    iota(ic[0], [[0, 1]], 0, 1)
-    iota(v("IOT"), [[1, 256]])
-    iota(v("IOS"), [[16, 288]])
-    iota(v("G1"), [[1, 8], [0, 16]])
-    for q in range(8):
-        iota(v("RM", 128 * q, 128 * q + 128), [[16, 8], [8, 2], [0, 8]], q)
-    iota(v("I16"), [[1, 16]])
-    iota(v("EO"), [[1, 2], [0, 16]])
-    iota(v("C31"), [[-1, 16]], 31)
-    iota(v("C16"), [[-1, 16]], 16)
-    iota(v("C16k"), [[16, 16]])
-    iota(v("E"), [[1, 128], [0, 16]])
-    iota(v("TAB0"), [[0, 2688]], 4096)
-    ts(ic[1], ic[0], 15, OP.bitwise_and)
-    ts(ic[2], ic[0], 4, OP.arith_shift_right)
-    ts(ic[3], ic[2], 1, OP.bitwise_and)
-    for i in range(3):
-        tc(col(i), ic[i])
-    tc(col(ODD), ic[3])
-    ts(col(G15), col(G_), 16, OP.mult, 15, OP.add)
-    ts(col(EVN), col(ODD), -1, OP.mult, 1, OP.add)
-    ts(col(C13), col(M_), 14, OP.is_lt)
-    ts(col(K14), col(M_), 14, OP.is_equal)
-    ts(col(K15), col(M_), 15, OP.is_equal)
-    ts(col(UHC), col(K14), 256, OP.mult, col(K15), OP.add)
-    ts(v("UH"), v("IOT", 0, 144), col(G15), OP.is_equal, col(UHC), OP.mult)
-    ts(v("ID"), v("IOT", 0, 128), col(P_), OP.is_equal)
-    ts(v("BO"), v("G1"), col(G_), OP.is_equal)
-    ts(v("TRI"), v("IOT", 0, 128), col(P_), OP.is_ge)
-    tt(v("TRI"), v("TRI"), v("BO"), OP.mult)
-    tc(v("PU", 0, 288), v("POI"))
-    for a, b in ((0, 96), (96, 208)):
-        act(v("H", 16 * a, 16 * b), ind(v("X0", 0, 3584), v("PU", a, b)))
-    ms(v("X0", 3584, 3808), 0)
-    ms(v("X1", 3584, 3808), 0)
-    ms(v("PIf", 288, 320), 0)
-    ms(v("CPf", 288, 320), 0)
-    ms(v("L"), 0)
-    ms(v("CE", 288, 320), 0)
-    tc(v("PIf", 0, 288), v("POI"))
-    ts(v("SLOT"), v("IOS"), col(M_), OP.add)
-    tc(v("H", 16 * 208, 4608), ind(v("X0", 0, 3584), v("PU", 208, 288)))
-    tc(v("ABU"), v("ABI", 0, 224))
-    for a, b in ((0, 96), (96, 208), (208, 288)):
-        for m in range(16):
-            mm(v("PA", a, b), v("UH", 15 - m, 143 - m), v("H", 16 * a + m, 16 * b, 16), m == 0, m == 15)
-    ts(col(SAW), col(K14), 8, OP.mult, col(C13), OP.add)
-    ts(col(SBW), col(K14), 16, OP.mult, col(C13), OP.add)
-    ts(col(G14), col(G15), -1, OP.add)
-    ts(col(P1_), col(P_), 1, OP.add)
-    ts(v("TA"), v("ID"), col(C13), OP.mult)
-    for nm, rr, wc in (("SA", G14, SAW), ("SB1", G15, SBW)):
-        ts(v(nm), v("IOT", 0, 128), col(rr), OP.is_equal, col(wc), OP.mult)
-        tt(v(nm), v(nm), v("TA"), OP.add)
-    ts(v("TB2"), v("IOT", 0, 128), col(P1_), OP.is_equal)
-    tt(v("TB2"), v("ID"), v("TB2"), OP.subtract)
-    ts(v("SB2"), v("TB2"), col(K14), OP.mult)
-    ms(v("ZER"), 0)
-    ms(v("F0", 288, 304), 1)
-    ms(v("F1", 304, 320), 1)
-    ms(v("VS", 256, 272), 0)
-    ts(col(R15), col(M_), 16, OP.mult, 15, OP.add)
-    ts(col(C16_), col(C13), 16, OP.mult)
-    act(v("CE", 0, 288), v("CEN"), AS, col(K14), col(C13))
-    for a, b in ((0, 112), (112, 224)):
-        tt(v("X1", 16 * a, 16 * b), ind(v("X0", 0, 3808), v("ABU", a, b)), v("XB", 16 * a, 16 * b), OP.max)
-
-    def sums(src, w, mid, out, b1, b2):
-        mm(v(b1, 0, w), v("SA"), v(src, 0, w))
-        act(v(mid, 0, w), v(b1, 0, w))
-        mm(v(b2, 0, w), v("SB1"), v(src, 0, w), True, False)
-        mm(v(b2, 0, w), v("SB2"), v(mid, 0, w), False, True)
-        act(v(out, 0, w), v(b2, 0, w))
 
     def nbs(t):
         return [128, 128, 32 + 16 * t]
 
-    def centres(t):
-        sums("CE", 288 + 16 * t, "CX1", "CEX", "PM0", "PM1")
-        nb = nbs(t)
-        for b in range(3):
-            mm(v("PM0", 128 * b, 128 * b + 128, 1, 0, nb[b]), v("CEX", 128 * b, 128 * b + nb[b]), v("ID"))
-        act(v("CXT", 0, 256), v("PM0", 0, 256))
-        act(v("CXT", 256, 384, 1, 0, nb[2]), v("PM0", 256, 384, 1, 0, nb[2]))
+    def chunks(a, b, n=CH):
+        return [(x, min(b, x + n)) for x in range(a, b, n)]
 
-    centres(0)
+    def phase(k, fn, xs):
+        i, w = len(ops), 0
+        for x in xs:
+            fn(*x)
+        for o in ops[:i - 1:-1]:
+            if "t" not in o["alt"]:
+                o["more"] = w
+                w += min(c for f, c in o["alt"].values()) / k
 
-    def rows_open():
-        ts(col(LT8), col(M_), 8, OP.is_lt)
-        ts(col(GE8), col(M_), 8, OP.is_ge)
-        ts(v("AI"), v("ABI", 224, 448), 255, OP.bitwise_and)
-        tc(v("AL"), v("AI"))
-        tt(v("AH"), v("ABI", 224, 448), v("AI"), OP.subtract)
-        act(v("S1"), v("ID"), AF.Copy, 0.0, col(LT8))
-        act(v("S4"), v("ID"), AF.Copy, 0.0, col(GE8))
-        ts(v("S2"), v("IOT", 0, 128), -8, OP.add, col(P_), OP.is_equal)
-        ts(v("S2"), v("S2"), col(LT8), OP.mult)
-        ts(v("S3"), v("IOT", 0, 128), 8, OP.add, col(P_), OP.is_equal)
-        ts(v("S3"), v("S3"), col(GE8), OP.mult)
-        ts(v("RM"), v("RM"), col(P_), OP.is_equal)
-        mm(v("PC", 0, 224), v("S1"), v("AH"), True, False)
-        mm(v("PC", 0, 224), v("S2"), v("AL"), False, True)
-        mm(v("PD", 0, 224), v("S3"), v("AH"), True, False)
-        mm(v("PD", 0, 224), v("S4"), v("AL"), False, True)
-        act(v("DA"), v("PC", 0, 224))
-        act(v("DB"), v("PD", 0, 224))
-
-    def rows(i, bank):
-        for j in range(2):
-            q = 2 * i + j
-            mm(v(bank, 224 * j, 224 * j + 224), v("RM", 128 * (q % 8), 128 * (q % 8) + 128), v("DA" if q < 8 else "DB"))
-        act(v("AR", 448 * i, 448 * i + 448), v(bank, 0, 448))
-
-    def vgather(t, b):
-        o = v("VW"[t], 2048 * b, 2048 * b + 16 * nbs(t)[b])
-        if t == 0:
-            act(o, ind(v("X1", 0, 3584), v("PU", 128 * b, 128 * b + nbs(t)[b])), AS, col(K14), col(C13))
-        else:
-            tt(o, ind(v("X1", 0, 3808), v("CU", 128 * b, 128 * b + nbs(t)[b])), v("V", 2048 * b, 2048 * b + 16 * nbs(t)[b]), OP.max)
-
-    def count(t, a, b, fresh):
-        Ft, P = "F%d" % t, 288 + 16 * t
-        e = min(b, P)
-        mm(v("PA", a, e), v("BO"), v("L", a, e))
-        mm(v("PB", a, b), v("TRI"), v("L", a, b))
-        ts(v(Ft, a, e), v("PA", a, e), 12, OP.is_ge)
-        act(v("Z", a, b), v("PB", a, b), AF.Relu, 1.0, -1.0)
-        mm(v("PB", a, b), v("BO"), v("Z", a, b))
-        act(v("MA", a, b), v("PB", a, b))
-        scan(v("INC", a, b), v(Ft, a, b), v("ZER", a, b), 0.0 if fresh else v("INC", a - 1, a), OP.add, OP.add)
-        ts(v("LE", a, b), v("INC", a, b), col(M_), OP.is_le)
-        tr(v("pk", 0, 1) if fresh else v("pk", 1, 2), v("LE", a, b), OP.add)
-        if not fresh:
-            tt(v("pk", 0, 1), v("pk", 0, 1), v("pk", 1, 2), OP.add)
-
-    def numbers(t):
-        P, k1 = 288 + 16 * t, v("pk", 0, 1)
-        ts(v("pk2"), v("ZER", 0, 2), k1, OP.add)
-        tc(v("SPu"), ind(v("PIf"), v("pk2", 0, 1)))
-        if t == 1:
-            tc(v("CSu"), ind(v("CPf"), v("pk2", 0, 1)))
-        ts(v("t2"), k1, P, OP.is_ge, 2560 + 16 * r - 320 * r - P, OP.mult)
-        ts(v("NL%d" % t, 4 * r, 4 * r + 1), v("t2"), k1, OP.add, 320 * r, OP.add)
-        bcast("a%d" % t, v("NL%d" % t, 4 * r, 4 * r + 1))
-
-    def kp(bank, x):
-        mm(v(bank, 0, 16), v("ID"), v("C31"), True, False)
-        for k in range(16):
-            mm(v(bank, 0, 16), v("U16", 15 - k, 143 - k), v(x, 16 * k, 16 * k + 16), False, k == 15)
-
-    def split_a(t):
-        P, pk1 = 288 + 16 * t, v("pk2", 0, 1)
-        if t == 0:
-            act(v("VS", 0, 256), ind(v("X1", 0, 3584), v("SPu")), AS, col(K14), col(C13))
-            tc(v("VSc"), ind(v("X1", 0, 3584), v("SPu")))
-        else:
-            act(v("VSa"), ind(v("X1", 0, 3808), v("SPu")), AS, col(K14), col(C13))
-        tt(v("LAf"), ind(v("MA", 0, P + 16), pk1), v("C16k"), OP.add)
-        tc(v("LAu"), v("LAf"))
-        tt(v("LS2"), ind(v("L", 0, 320), v("pk2")), v("EO"), OP.mult)
-        vtr(v("LT"), v("LS2"))
-        tt(v("LK"), v("LT", 0, 16), v("LT", 16, 32), OP.add)
-        if t == 1:
-            tt(v("VS", 0, 256), ind(v("X1", 0, 3808), v("CSu")), v("VSa"), OP.max)
-            tc(v("VSc"), v("VS", 0, 256))
-        tt(v("AD"), ind(v("VS"), v("LAu")), v("VSc"), OP.subtract)
-        tc(v("LO", 0, P), v("L", 0, P))
-        tc(ind(v("LO", 0, P + 16), pk1), v("ZER", 0, 16))
-
-    def split_b(t):
-        tt(v("KL"), v("PC", 0, 16), v("LK"), OP.mult)
-        tr(v("kx"), v("KL"), OP.max)
-        ts(v("kr"), v("kx"), 15, OP.bitwise_and)
-        ts(v("obu", 0, 1), v("kr"), -1, OP.mult, col(R15), OP.add)
-        bt = v("BT%d" % t, 16 * r, 16 * r + 16)
-        tc(bt, ind(v("VS"), v("obu", 0, 1)))
-        bcast("b%d" % t, bt)
-
-    def split_c(t):
-        ts(v("obf"), v("kr"), -1, OP.mult, col(R15), OP.add)
-        ts(v("RB"), v("I16"), v("obf"), OP.mult)
-        mm(v("PD", 0, 16), v("BO"), v("RB"))
-        tc(v("LBu"), v("PD", 0, 16))
-        tt(v("BD"), ind(v("VS"), v("LBu")), v("VSc"), OP.subtract)
-        act(v("KA"), v("PC", 0, 16))
-        act(v("BA"), v("BD"), AF.Abs)
-        kp("PD", "BA")
-
-    def split_g():
-        tt(v("g1"), v("PD", 0, 16), v("KA"), OP.is_lt)
-        tt(v("GO"), v("g1"), v("LK"), OP.mult)
-
-    def split_d(t):
-        P, pk1 = 288 + 16 * t, v("pk2", 0, 1)
-        tc(v("SPf"), ind(v("PIf"), pk1))
-        act(v("GE", 0, 16), v("GO"), AF.Copy, 0.0, col(EVN))
-        act(v("GE", 16, 32), v("GO"), AF.Copy, 0.0, col(ODD))
-        vtr(v("GT"), v("GE"))
-        tt(v("GS"), v("GT", 0, 16), v("GT", 16, 32), OP.add)
-        tt(v("g1"), v("GO"), v("C16"), OP.mult)
-        tt(v("KL"), v("C16"), v("g1"), OP.subtract)
-        tr(v("mx"), v("KL"), OP.max)
-        ts(v("RO", 0, 16), v("KL"), v("mx"), OP.is_equal, col(EVN), OP.mult)
-        ts(v("RO", 16, 32), v("KL"), v("mx"), OP.is_equal, col(ODD), OP.mult)
-        ts(v("obf"), v("mx"), -1, OP.mult, col(K16), OP.add)
-        act(v("RB2"), v("I16"), AF.Copy, 0.0, v("obf"))
-        mm(v("PC", 0, 16), v("BO"), v("RB2"))
-        act(v("FV"), v("PC", 0, 16), AS, col(H18 + t), col(K15))
-        act(v("MVV%d" % t, 16 * r, 16 * r + 16), v("FV"))
-        tt(v("GLf"), v("SPf"), v("DGO"), OP.subtract)
-        tt(v("GLf"), v("GLf"), v("GS"), OP.mult)
-        tt(v("GLf"), v("GLf"), v("DGO"), OP.add)
-        tc(v("GLu"), v("GLf"))
-        if t == 0:
-            tt(v("LS16"), ind(v("L", 0, 320), pk1), v("GS"), OP.subtract)
-            tc(ind(v("L", 0, 320), pk1), v("LS16"))
-            tt(v("RB"), v("AD", 0, 256, 16), v("VSc", 0, 256, 16), OP.add)
-            tc(ind(v("CE"), pk1), v("RB"))
-            tc(v("CE", P, P + 16), v("BT%d" % t, 16 * r, 16 * r + 16))
-            tc(v("NU", P, P + 16), ind(v("NEI"), pk1))
-
-    def go_homes(t):
-        tc(ind(v("X0"), v("GLu")), v("HV%d" % t))
-
-    def mcent(t, b, js=(0, 1, 2, 3)):
-        nb = nbs(t)
-        for j in js:
-            n = min(512, 16 * nb[b] - 512 * j)
-            if n > 0:
-                c = 2048 * b + 512 * j
-                pm = "PM%d" % (j % 2)
-                kk = 128 if b < 2 else nb[b]
-                mm(v(pm, 0, n), v("CXT", 128 * b, 128 * b + 128, 1, 0, kk), v("E", 512 * j, 512 * j + n, 1, 0, kk), True, b != 1)
-                if b == 1:
-                    mm(v(pm, 0, n), v("NID"), v("VW"[t], c, c + n), False, True)
-                    act(v("MC", c, c + n), v(pm, 0, n), AF.Abs)
-                else:
-                    tt(v("MC", c, c + n), v(pm, 0, n), v("VW"[t], c, c + n), OP.max)
-
-    def by_slot(bank, x, w, t, b):
-        nb = nbs(t)
-        for m in range(16):
-            mm(v(bank, 24 * m + b, 24 * m + b + 22, 3, 0, nb[b]), v(x, 2048 * b + m, 2048 * b + 16 * nb[b], 16), v(w), False, False)
-
-    def gain_open(t):
-        nb = nbs(t)
-        mm(v("PG", 0, 384), v("FST"), v("C15"), True, False)
-        for b in range(3):
-            for m in range(16):
-                mm(v("PG", 24 * m + b, 24 * m + b + 22, 3, 0, nb[b]), v("LO", 128 * b, 128 * b + nb[b]), v("LW", 8 * m, 8 * m + 8), False, False)
-
-    def close(bank):
-        mm(v(bank, 0, 384), v("FST"), v("ZER"), False, True)
-
-    def tree(bank, op, out):
-        tc(v("T1"), v(bank, 192, 384))
-        tt(v("T2"), v(bank, 0, 192), v("T1"), op)
-        tt(v("T3"), v("T2", 0, 96), v("T2", 96, 192), op)
-        tt(v("T4"), v("T3", 0, 48), v("T3", 48, 96), op)
-        tt(out, v("T4", 0, 24), v("T4", 24, 48), op)
-
-    def turn(x, n, out):
-        for b in range(3):
-            mm(v("PA", 128 * b, 128 * b + 128, 1, 0, n), v(x, b, 3 * n, 3), v("ID"))
-        tc(v(out, 0, 384, 1, 0, n), v("PA", 0, 384, 1, 0, n))
-
-    def table(t):
-        arrive("a%d" % t, [v("NL%d" % t)])
-        tc(v("NLu"), v("NL%d" % t, 0, 32, 4))
-        tc(ind(v("TAB%d" % t), v("NLu")), v("IOB"))
-
-    def near(t, b, vec=False):
-        o, i = v("TN", 2048 * b, 2048 * b + 16 * nbs(t)[b]), ind(v("TAB%d" % t), v("NU", 128 * b, 128 * b + nbs(t)[b]))
-        if vec:
-            tc(o, i)
-        else:
-            act(o, i)
-
-    def near_sums(t, bs):
-        mm(v("PN", 0, 384), v("FST"), v("C128"), True, False)
-        for b in bs:
-            by_slot("PN", "TN", "SEL", t, b)
-        close("PN")
-
-    def targets(t):
-        P = 288 + 16 * t
-        tree("PN", OP.min, v("ki"))
-        ts(v("Ti"), v("ki"), 127, OP.bitwise_and)
-        tc(v("TB"), v("Ti"))
-        sums("BT%d" % t, 128, "BX1", "BTX", "PC", "PD")
-        turn("TB", 8, "T8")
-        mm(v("PB", 0, P), v("RP", 0, 128, 1, 0, 8), v("T8", 0, P, 1, 0, 8))
-        tc(v("TLu", 0, P), v("PB", 0, P))
-
-    def far(t):
-        nb = nbs(t)
-        V = "VW"[t]
-        by_slot("PG", "MC", "WV", t, 1)
-        for j in range(5):
-            if j < 4:
-                c, br, pm = 2048 + 512 * j, "BR%d" % (j % 2), "PM%d" % (j % 2)
-                act(v(br), ind(v("BTX"), v("TLu", 128 + 32 * j, 160 + 32 * j)))
-                mm(v(pm), v("ID"), v(br), True, False)
-                mm(v(pm), v("NID"), v(V, c, c + 512), False, True)
-            if j > 0:
-                c, pm = 1536 + 512 * j, "PM%d" % ((j - 1) % 2)
-                act(v("MB", c, c + 512), v(pm), AF.Abs)
-        for b in (2, 0):
-            c, n = 2048 * b, 16 * nb[b]
-            tt(v("MB", c, c + n), ind(v("BTX"), v("TLu", 128 * b, 128 * b + nb[b])), v(V, c, c + n), OP.max)
-            if b == 2:
-                ts(v("hs"), v("ki"), 4096, OP.is_lt)
-                ts(v("ok"), v("TB"), -255, OP.add)
-                tt(v("TH"), v("ok"), v("hs"), OP.mult)
-        if t == 0:
-            by_slot("PG", "MC", "WC", t, 2)
-        by_slot("PG", "MB", "WB", t, 2)
-        by_slot("PG", "MB", "WB", t, 0)
-        by_slot("PG", "MB", "WA", t, 1)
-        close("PG")
-
-    def pick(t):
-        P = 288 + 16 * t
-        tree("PG", OP.max, v("ki"))
-        ts(v("ok"), v("ki"), 262160, OP.is_ge)
-        ts(v("lo"), v("ki"), 15, OP.bitwise_and)
-        tt(v("X48", 24, 48), v("ok"), v("TH"), OP.mult)
-        tc(v("X48", 0, 24), v("lo"))
-        turn("X48", 16, "XT")
-        mm(v("PB", 0, 304), v("RP", 128, 256, 1, 0, 16), v("XT", 0, 304, 1, 0, 16))
-        act(v("TS"), v("PB", 0, 304))
-        tt(v("Y"), ind(v("X48", 0, 24), v("L8u")), v("MKU"), OP.mult)
-        mm(v("PD", 0, 24), v("ID"), v("C256"), True, False)
-        for q in range(8):
-            mm(v("PD", 0, 24), v("ZW", 112 - 16 * q, 240 - 16 * q), v("Y", 24 * q, 24 * q + 24), False, q == 7)
-        mm(v("PC", 0, 304), v("RP", 0, 128, 1, 0, 16), v("XT", 0, 304, 1, 0, 16))
-        ts(v("VLu"), v("PD", 0, 24), col(R15), OP.add)
-        for q in range(6, 8):
-            act(v("ZQ", 304 * q, 304 * q + 304), v("TS"), AF.Abs, col(TQB + q), 1000.0)
-        act(v("VB", 0, P), ind(v("VW"[t], 0, 16 * P), v("VLu", 0, P // 16)))
-        for q in range(6):
-            ts(v("ZQ", 304 * q, 304 * q + 304), v("TS"), col(TQ + q), OP.not_equal, 1000, OP.mult)
-        scan(v("SC"), v("D0"), v("ZQ"), 1000.0, OP.add, OP.min)
-        ts(v("QTu"), v("SC", 303, 2432, 304), 303, OP.add, 304, OP.min)
-        tc(v("MV%d" % t), ind(v("VB"), v("QTu")))
-        act(v("LOS", 0, 304), v("PC", 0, 304))
-        movers(t)
-
-    def own(t):
-        ex, x = v("W8", 0, 8), v("W8", 24, 32)
-        ts(ex, v("SC", 303, 2432, 304), 0, OP.is_le)
-        ts(v("OHm"), ind(v("LOS"), v("QTu")), col(F15), OP.is_equal)
-        tt(v("PGm", 0, 128), ind(v("PIf"), v("QTu")), v("OHm"), OP.mult)
-        if t == 0:
-            ts(v("QTo", 0, 1), v("SC", 303 + 304 * r, 304 + 304 * r), 303, OP.add, 304, OP.min)
-            ts(v("OHn"), ind(v("LOS"), v("QTu")), col(F15), OP.not_equal)
-            tt(v("LN"), ind(v("L", 0, 320), v("QTu")), v("OHn"), OP.mult)
-            ts(x, v("SC", 303, 2432, 304), 303 + 3744, OP.add)
-            tt(x, x, v("DMV"), OP.subtract)
-            tt(x, x, ex, OP.mult)
-            tt(x, x, v("DMV"), OP.add)
-            ts(v("QLu"), x, -3744, OP.add)
-            tc(ind(v("L"), v("QLu")), v("LN"))
-        ox = v("W8", r, r + 1)
-        ts(v("sm", 0, 1), ox, -1, OP.mult, 1, OP.add)
-        tt(v("sm", 1, 2), ox, own1(0), OP.mult)
-
-    def own1(o):
-        src = v("PGm", o + 16 * r, o + 16 * r + 16)
-        ts(v("TT", 0, 16), src, col(EVN), OP.mult)
-        ts(v("TT", 16, 32), src, col(ODD), OP.mult)
-        vtr(v("TR", 0, 32), v("TT", 0, 32))
-        tt(v("OH"), v("TR", 0, 16), v("TR", 16, 32), OP.add)
-        tr(v("sm", 10, 11), v("OH"), OP.add)
-        return v("sm", 10, 11)
-
-    def own_c():
-        tt(v("PGm", 128 + 16 * r, 144 + 16 * r), ind(v("CPf"), v("QTo", 0, 1)), v("OHm", 16 * r, 16 * r + 16), OP.mult)
-        tt(v("sm", 8, 9), v("W8", r, r + 1), own1(128), OP.mult)
-
-    def own_ids():
-        for k in range(16):
-            mm(v("PA", 0, 8), v("UF", 15 - k, 143 - k), v("PGm", k, 128, 16), k == 0, k == 15)
-
-    def own2(t):
-        ex, x = v("W8", 0, 8), v("W8", 24, 32)
-        tc(v("W8", 8, 16), v("PA", 0, 8))
-        tt(x, v("W8", 8, 16), v("DMV"), OP.subtract)
-        tt(x, x, ex, OP.mult)
-        tt(x, x, v("DMV"), OP.add)
-        tc(v("MVL"), x)
-
-    def mv_homes(t):
-        tc(ind(v("X0"), v("MVL")), v("MVV%d" % t))
-
-    def land(t):
-        P = 288 + 16 * t
-        nx, a0 = ("XA", 0) if t else ("X1", 3584)
-        arrive("c%d" % t, [v(nx, a0, a0 + 112)])
-        for k in range(16):
-            mm(v("PC", 0, 7), v("U14", 15 - k, 143 - k), v(nx, a0 + k, a0 + 112, 16), k == 0, k == 15)
-        tt(v("kk"), v("PC", 0, 7), v("C7"), OP.mult)
-        km, hw, wo, w, wc = [v("sm", i, i + 1) for i in (2, 3, 4, 5, 9)]
-        nown, ido, ox = v("sm", 0, 1), v("sm", 1, 2), v("W8", r, r + 1)
-        tr(km, v("kk"), OP.max)
-        ts(hw, km, ox, OP.max, 0, OP.is_gt)
-        ts(v("TT", 0, 32), v("RO"), hw, OP.mult)
-        ts(wo, km, -16, OP.mult, col(WO + t), OP.add)
-        ts(w, wo, nown, OP.mult, ido, OP.add)
-        ts(v("TT", 32, 64), v("TT", 0, 32), w, OP.mult)
-        n = 64
-        if t == 0:
-            n = 96
-            ts(wc, wo, nown, OP.mult, v("sm", 8, 9), OP.add)
-            ts(v("TT", 64, 96), v("TT", 0, 32), wc, OP.mult)
-        vtr(v("TR", 0, n), v("TT", 0, n))
-        tt(v("OH"), v("TR", 0, 16), v("TR", 16, 32), OP.add)
-        if t == 0:
-            tt(v("L", P, P + 16), v("GS"), v("OH"), OP.add)
-        for nm, pf, o in (("SPf", "PIf", 32), ("CSf", "CPf", 64)):
-            if nm == "SPf" or t == 0:
-                tt(v("OW"), v("TR", o, o + 16), v("TR", o + 16, o + 32), OP.add)
-                tt(v("g1"), v(nm), v("OH"), OP.mult)
-                tt(v("OW"), v(nm), v("OW"), OP.add)
-                tt(v(pf, P, P + 16), v("OW"), v("g1"), OP.subtract)
-
-    def land_home(t):
-        hw, wo = v("sm", 3, 4), v("sm", 4, 5)
-        ts(v("sm", 6, 7), hw, v("sm", 0, 1), OP.mult)
-        tt(v("sm", 7, 8), wo, col(AR_), OP.subtract)
-        ts(v("ARu", 0, 1), v("sm", 7, 8), v("sm", 6, 7), OP.mult, col(AR_), OP.add)
-        tc(ind(v("X0"), v("ARu", 0, 1)), v("FV"))
-
-    tt(v("L", 0, 288), v("PA", 0, 288), v("SLOT"), OP.is_equal)
-    count(0, 0, 304, True)
-    ts(v("EO"), v("EO"), col(ODD), OP.is_equal)
-    numbers(0)
-    iota(v("IOB"), [[1, 128]])
-    iota(v("C128"), [[128, 16], [0, 24]])
-    iota(v("C15"), [[-1, 16], [0, 24]], 15)
-    iota(v("G2", 128, 136), [[1, 8]])
-    iota(v("G2", 0, 128), [[1, 16], [16, 8]])
-    iota(v("COL", TQ, TQ + 8), [[16, 8]], -255)
-    ts(v("E"), v("E"), col(P_), OP.is_equal)
-    ts(v("I16"), v("I16"), col(M_), OP.is_equal)
-    ts(v("U16"), v("IOT", 0, 144), col(G15), OP.is_equal, col(C16_), OP.mult)
-    split_a(0)
-    vgather(0, 0)
-    act(v("NID"), v("ID"), AF.Copy, 0.0, -1.0)
-    act(v("AA"), v("AD"), AF.Abs)
-    kp("PC", "AA")
-    ms(v("NEI", 288, 320), 0)
-    tc(v("NU", 0, 288), v("NEI", 0, 288))
-    ms(v("FST"), 0)
-    ms(v("FST", 0, 128, 1, 0, 1), 1)
-    mcent(0, 0)
-    split_b(0)
-    vgather(0, 1)
-    split_c(0)
+    dma("s", [(v("POI"), v("post"))])
+    dma("a", [(v("X0", 0, 1792), v("rec", 0, 1792))], 3500)
+    dma("s", [(v("X0", 1792, 3584), v("rec", 1792, 3584))], 3500)
+    dma("a", [(v("ABI"), v("absorb"))], 2200)
+    dma("s", [(v("XB", 0, 3584, 1, 16 * q, 16 * q + 14), v("rec", 0, 3584, 1, 16 * q, 16 * q + 14)) for q in range(8)], 5500)
+    dma("s", [(v("CE", 0, 288), v("cen")), (v("NEI", 0, 288), v("near"))], 5500)
+    for i in range(6):
+        ops[i]["more"] = 10 ** 6 * (6 - i)
+    ic = [v("IC", i, i + 1) for i in range(3)]
+    iota(ic[0], [[0, 1]], 0, 1)
+    iota(v("IOT"), [[1, 256]])
+    iota(v("IOS"), [[16, 288]])
+    iota(v("G1"), [[1, 8], [0, 16]])
+    iota(v("G2"), [[0, 8], [1, 16]])
+    iota(v("G3"), [[0, 24], [1, 8]])
+    iota(v("G8"), [[1, 8]])
+    iota(v("C15"), [[-1, 16]], 15)
+    iota(v("C16k"), [[16, 16]])
+    iota(v("C256"), [[256, 24]])
+    iota(v("SQ"), [[1, 8], [8, 3]])
+    iota(v("ZW"), [[1, 240]], -112)
+    iota(v("IOB", 0, 16), [[1, 16]], 16 * r)
+    for a, b, o in ((0, r, 0), (r, 7, 16)):
+        if b > a:
+            iota(v("IOB", 16 + 16 * a, 16 + 16 * b), [[1, 16 * (b - a)]], 16 * a + o)
+    ts(ic[1], ic[0], 15, OP.bitwise_and)
+    ts(ic[2], ic[0], 4, OP.arith_shift_right)
+    for i in range(3):
+        tc(col(i), ic[i])
+    ts(col(G15), col(G_), 16, OP.mult, 15, OP.add)
+    ts(col(C13), col(M_), 14, OP.is_lt)
+    ts(col(K14), col(M_), 14, OP.is_equal)
+    ts(col(K15), col(M_), 15, OP.is_equal)
+    ts(col(BC), col(M_), 14, OP.is_ge)
+    ts(col(B255), col(BC), 255, OP.mult)
+    ts(col(K256), col(BC), 256, OP.mult)
+    ts(col(UHC), col(K14), 256, OP.mult, col(K15), OP.add)
+    ts(col(UCC), col(K15), 1 / 256, OP.mult, col(K14), OP.add)
+    ts(col(RNC), col(K14), -16, OP.mult, col(K15), OP.add)
+    ts(col(C16_), col(C13), 16, OP.mult)
+    ts(col(CN16), col(C13), -16, OP.mult)
+    ts(col(R15), col(M_), 16, OP.mult, 15, OP.add)
     ts(col(I0), col(M_), 0, OP.is_equal)
-    ts(col(WCC), col(C13), 48, OP.mult, -16, OP.add)
-    ts(col(WBC), col(WCC), -1, OP.mult)
-    ts(col(WAC), col(C13), -16, OP.mult)
-    ts(col(WVC), col(C13), 16, OP.mult)
-    for nm, wc in (("WC", WCC), ("WB", WBC), ("WA", WAC), ("WV", WVC), ("SEL", I0)):
-        ts(v(nm), v("G2", 128, 136), col(G_), OP.is_equal, col(wc), OP.mult)
-    ts(v("LW"), v("G2", 0, 128), col(P_), OP.is_equal, 262144, OP.mult)
-    split_g()
-    rows_open()
-    vgather(0, 2)
-    for i in range(4):
-        rows(i, ("PN", "PG", "PC", "PD")[i])
-    table(0)
-    near(0, 1, True)
-    mcent(0, 2)
-    near(0, 0)
-    near(0, 2)
-    gain_open(0)
-    by_slot("PG", "MC", "WC", 0, 0)
-    near_sums(0, (1, 0, 2))
-    mcent(0, 1, (0, 1))
-    ts(v("PQ"), v("POI"), 15, OP.bitwise_and)
-    ts(v("PQ2"), v("POI"), 4, OP.arith_shift_right)
-    ts(v("PQ"), v("PQ"), 224, OP.mult)
-    tt(v("PQ"), v("PQ"), v("PQ2"), OP.add)
-    tc(v("PP"), v("PQ"))
+    ts(col(LT8), col(M_), 8, OP.is_lt)
+    ts(col(GE8), col(M_), 8, OP.is_ge)
+    ts(col(MH), col(M_), 0.5, OP.add)
+    ts(v("U1"), v("IOT", 0, 144), col(G15), OP.is_equal)
+    for nm, c in (("UH", UHC), ("UC", UCC), ("U16", C16_), ("UN16", CN16)):
+        ts(v(nm), v("U1"), col(c), OP.mult)
+    tc(v("UF"), v("U1"))
+    ts(v("ID"), v("IOT", 0, 128), col(P_), OP.is_equal)
+    for nm, w in (("NID", -1), ("IDL", 2 ** 23), ("IDh", 1)):
+        ts(v(nm), v("ID"), w, OP.mult)
+    ts(v("BO"), v("G1"), col(G_), OP.is_equal)
+    for nm, c in (("BOh", 1), ("RN", col(RNC)), ("RC", col(UCC))):
+        ts(v(nm), v("BO"), c, OP.mult)
+    ts(v("B15"), v("U1", 0, 128), col(M_), OP.mult)
+    step({"g": (lambda: [g.affine_select(ap(v("TRI")), ap(v("BO")), [[1, 128]], OP.is_ge, 0.0, 0, -1)], 460)}, [v("TRI")], [v("BO")])
     ts(v("RP", 0, 128), v("G1"), col(P_), OP.is_equal)
     ts(v("RP", 128, 256), v("G1"), 8, OP.add, col(P_), OP.is_equal)
-    arrive("b0", [v("BT0")])
-    targets(0)
-    mcent(0, 1, (2, 3))
-    for i in range(4, 8):
-        rows(i, ("PC", "PD")[i % 2])
-    iota(v("ZW"), [[1, 240]], -112)
-    iota(v("G3"), [[0, 24], [1, 8]])
-    iota(v("L8f"), [[2, 12]])
-    iota(v("C256"), [[256, 24]])
-    iota(v("DMV"), [[16, 8]], 4064)
-    iota(v("C7"), [[-1, 7]], 7)
-    iota(v("D0"), [[0, 2432]], -1)
-    iota(v("D0", 0, 2432, 304), [[0, 8]], 5000)
-    iota(v("VB"), [[0, 320]])
-    iota(v("LOS", 304, 320), [[0, 16]])
-    iota(v("MVV0"), [[0, 128]], 255)
-    iota(v("MVV1"), [[0, 128]], 255)
-    iota(v("TAB1"), [[0, 2688]], 4096)
-    far(0)
-    ts(col(K16), col(M_), 16, OP.mult, 16, OP.add)
-    for t in range(2):
-        ts(col(H18 + t), col(K14), 18 + t, OP.mult)
-        ts(col(WO + t), col(M_), 3584 + 112 * t + 112, OP.add)
-    ts(v("DGO"), v("C16k"), col(M_), OP.add, 3808, OP.add)
-    split_d(0)
+    ts(v("SLOT"), v("IOS"), col(M_), OP.add)
+    ts(v("I16"), v("IOT", 0, 16), col(M_), OP.is_equal)
+    ts(v("I17"), v("I16"), 2 ** 17, OP.mult)
+    ts(v("W8", 40, 48), v("BO", 0, 128, 16), col(C13), OP.mult)
+    for i, w in enumerate((4096, -4096, 2048, -2048)):
+        ts(v("W8", 8 * i, 8 * i + 8), v("W8", 40, 48), w, OP.mult)
+    ts(v("W8", 32, 40), v("BO", 0, 128, 16), col(I0), OP.mult)
+    for i, x in enumerate(MS):
+        if x:
+            ts(col(WC0 + i), col(C13), 2048 if i % 2 else -2048, OP.mult)
+            ts(v("CO%d" % i), v("BO"), col(WC0 + i), OP.mult)
+            step({"g": (lambda i=i, x=x: [g.affine_select(ap(v("CO%d" % i)), ap(v("CO%d" % i)), [[0, 8], [-1, 16]], OP.is_gt, 0.0, x, 0)], 460)}, [v("CO%d" % i)], [v("CO%d" % i)])
     ts(v("ZW"), v("ZW"), col(M_), OP.is_equal, -1, OP.mult)
     ts(v("MKU"), v("G3"), col(G_), OP.is_equal)
-    ts(v("L8u"), v("L8f"), col(GE8), OP.add)
-    ts(v("COL", TQ, TQ + 8), v("COL", TQ, TQ + 8), col(M_), OP.add)
+    ts(v("L8f"), v("SQ", 0, 24, 2), col(LT8), OP.mult)
+    ts(v("t24", 0, 12), v("SQ", 1, 24, 2), col(GE8), OP.mult)
+    tt(v("L8f"), v("L8f"), v("t24", 0, 12), OP.add)
+    tc(v("L8u"), v("L8f"))
+    ts(v("K86f"), v("G8"), 0, OP.mult, col(M_), OP.add)
+    tc(v("K7"), v("K86f"))
+    ts(v("K86"), v("K86f"), 8, OP.mult, 6, OP.add)
+    ts(v("COL", TQ, TQ + 8), v("C16k", 0, 8), 16, OP.add, col(M_), OP.add)
     ts(v("COL", TQB, TQB + 8), v("COL", TQ, TQ + 8), -1000, OP.mult)
+    ts(v("DGO"), v("C16k"), col(M_), OP.add, 3808, OP.add)
+    ts(v("DQ"), v("COL", TQ, TQ + 8), 304, OP.add)
+    ts(v("DM"), v("COL", TQ, TQ + 8), 3808 - 1904 - 16, OP.add)
+    for nm, c in (("ZER", 0), ("FST", 0), ("L", 0), ("D0", -1), ("D1", 1), ("DN", -128), ("DG", 1), ("CNG", -2 ** 23), ("MVV0", 255), ("MVV1", 255)):
+        fill(v(nm), c)
+    ms(v("FST", 0, 128, 1, 0, 1), 1)
+    ms(v("DN", 0, 384, 16), 2 ** 14)
+    ms(v("DG", 0, 384, 16), -2 ** 25)
+    ms(v("D1", 7, 128, 8), 0)
+    for x in (v("X0", 3584, 3808), v("X1", 3696, 3808), v("PIf", 288, 320), v("CPf", 288, 320), v("NEI", 288, 320), v("CE", 288, 320), v("VS", 256, 272), v("VB", 288, 320),
+              v("PIm", 288, 320), v("PN", 256, 384)):
+        ms(x, 0)
+    ms(v("LOS", 288, 320), 99)
     ts(col(F15), col(M_), -1, OP.mult, 15, OP.add)
-    act(v("YR", 0, 2048), ind(v("AR"), v("PP", 0, 128)))
-    pick(0)
-    act(v("YR", 2048, 4096), ind(v("AR"), v("PP", 128, 256)))
-    act(v("YR", 4096, 4608), ind(v("AR"), v("PP", 256, 288)))
-    act(v("X1", 0, 3584), v("X1", 0, 3584), AF.Copy, 0.0, col(C13))
-    ts(v("DMV"), v("DMV"), col(M_), OP.add)
+    ms(v("F0", 288, 304), 1)
+    ms(v("F1", 304, 320), 1)
     for t in range(2):
-        act(v("HV%d" % t), v("IOT"), AS, col(H18 + t), col(K15))
-    ts(col(UCC), col(I0), 8, OP.add)
-    ts(col(UCC), col(M_), col(UCC), OP.is_equal, col(I0), OP.add)
-    ts(v("UC"), v("IOT", 0, 144), col(G15), OP.is_equal, col(UCC), OP.mult)
-    ts(v("UF"), v("IOT", 0, 144), col(G15), OP.is_equal)
-    ts(v("U14"), v("IOT", 0, 144), col(G15), OP.is_equal, col(K14), OP.mult)
+        for a, b in chunks(0, 2688, 672):
+            fill(v("TAB%d" % t, a, b), 4096)
+        ts(col(H18 + t), col(K14), 18 + t, OP.mult)
+        lin(v("HV%d" % t), v("IOT"), col(K15), col(H18 + t))
+        iota(v("ZC%d" % t), [[1, 112]], 3584 + 112 * t - 4096)
+        x = v("PR%d" % t)
+        ts(x, v("G1"), r, OP.is_gt, -1, OP.mult)
+        ts(x, x, 33 - 7 * t - r, OP.add, col(K14), OP.mult)
+        ts(v("JK", 0, 128), v("G2"), col(K15), OP.mult)
+        tt(x, x, v("JK", 0, 128), OP.add)
+        ts(x, x, col(K256), OP.subtract, 256, OP.add)
+        ms(v("PR%d" % t, 16 * r, 16 * r + 16), 2 ** 20)
+
+    def by_row(bank, u, x, a, b):
+        mm(*[(v(bank, a, b), v(u, 15 - m, 143 - m), v(x, 16 * a + m, 16 * b, 16), m == 0, m == 15) for m in range(16)], acc=True)
+
+    def first_live(a, b):
+        mm((v("PB", a, b), v("TRI"), v("L", a, b), True, True))
+        act(v("Z", a, b), v("PB", a, b), AF.Relu, 1.0, -1.0)
+        mm((v("PB", a, b), v("BO"), v("Z", a, b), True, True))
+        lin(v("MA", a, b), v("PB", a, b))
+
+    def full(t, a, b):
+        mm((v("PC", a, b), v("BO"), v("L", a, b), True, True))
+        ts(v("F%d" % t, a, b), v("PC", a, b), 12, OP.is_ge)
+
+    def count(t, a, b, j):
+        scan(v("INC", a, b), v("F%d" % t, a, b), v("ZER", a, b), v("INC", a - 1, a) if a else 0.0, OP.add, OP.add)
+        act(v("JK", a, b), v("INC", a, b), AF.Sign, col(MH), -1.0, v("acc", j, j + 1))
+
+    def numbers(t, x, pre):
+        P, t1, t2 = 288 + 16 * t, v("t1", 0, 1), v("t1", 1, 2)
+        ts(t1, x, 0.5, OP.mult, pre, OP.add)
+        ts(t2, t1, P, OP.is_ge, 2560 + 16 * r - 320 * r - P, OP.mult)
+        ts(v("NO%d" % t, 0, 1), t1, t2, OP.add, 320 * r, OP.add)
+        ts(v("pk8"), v("ZER", 0, 8), t1, OP.add)
+        exchange("a%d" % t, v("NO%d" % t, 0, 1), [v("NL%d" % t, 0, 7)])
+
+    def split(t):
+        P, pk1, bt = 288 + 16 * t, v("pk8", 0, 1), v("BT%d" % t, 16 * r, 16 * r + 16)
+        tc(v("SPu"), ind(v("PIf"), pk1))
+        if t == 0:
+            lin(v("VS", 0, 256), ind(v("X1", 0, 3584), v("SPu")))
+            lin(v("VSc"), ind(v("X1", 0, 3584), v("SPu")))
+        else:
+            tc(v("CSu"), ind(v("CPf"), pk1))
+            lin(v("VSa"), ind(v("X1"), v("SPu")))
+            tt(v("VS", 0, 256), ind(v("X1"), v("CSu")), v("VSa"), OP.max)
+            tc(v("VSc"), v("VS", 0, 256))
+        tt(v("LAf"), ind(v("MA", 0, P + 16), pk1), v("C16k"), OP.add)
+        tc(v("LAu"), v("LAf"))
+        tt(v("LSE"), ind(v("L", 0, 320), v("pk8")), v("BO"), OP.mult)
+        tt(v("AD"), ind(v("VS"), v("LAu")), v("VSc"), OP.subtract)
+        act(v("AA"), v("AD"), AF.Abs)
+        mm((v("PC", 0, 16), v("ID"), v("C15"), True, False), (v("PC", 0, 16), v("LSE"), v("I17"), False, False))
+        mm(*[(v("PC", 0, 16), v("U16", 15 - k, 143 - k), v("AA", 16 * k, 16 * k + 16), False, k == 15) for k in range(16)])
+        on_v(lambda: g.vector.tensor_reduce(ap(v("kx")), ap(v("PC", 0, 16)), AxisListType.X, OP.max), v("kx"), [v("PC", 0, 16)], 64)
+        ts(v("kr"), v("kx"), 15, OP.bitwise_and)
+        ts(v("obu", 0, 1), v("kr"), -1, OP.mult, col(R15), OP.add)
+        tc(bt, ind(v("VS"), v("obu", 0, 1)))
+        exchange("b%d" % t, bt, [v("BT%d" % t, 0, 16 * r), v("BT%d" % t, 16 * r + 16, 128)])
+        tc(v("LO", 0, P), v("L", 0, P))
+        tc(ind(v("LO", 0, P + 16), pk1), v("ZER", 0, 16))
+        ts(v("t1", 2, 3), v("kr"), -1, OP.mult, col(R15), OP.add)
+        ts(v("RB"), v("I16"), v("t1", 2, 3), OP.mult)
+        mm((v("PC", 0, 16), v("BO"), v("RB"), True, True))
+        tc(v("LBu"), v("PC", 0, 16))
+        tt(v("BD"), ind(v("VS"), v("LBu")), v("VSc"), OP.subtract)
+        act(v("BA"), v("BD"), AF.Abs)
+        tc(v("LS"), ind(v("L", 0, 320), pk1))
+        tc(v("SPf"), ind(v("PIf"), pk1))
+        mm(*([(v("PC", 0, 16), v("IDL"), v("LS"), True, False)] + [(v("PC", 0, 16), v(u, 15 - m, 143 - m), v(x, m, 256, 16), False, x == "BA" and m == 15) for u, x in (("U16", "AA"), ("UN16", "BA")) for m in range(16)]))
+        ts(v("GS"), v("PC", 0, 16), 2 ** 23, OP.is_gt)
+        ts(v("NG"), v("PC", 0, 16), 2 ** 23, OP.is_le)
+        mm((v("PC", 0, 16), v("TRI"), v("NG"), True, True))
+        ts(v("g1"), v("PC", 0, 16), 1, OP.is_equal)
+        tt(v("RO"), v("g1"), v("NG"), OP.mult)
+        mm((v("PC", 0, 16), v("B15"), v("RO"), True, True))
+        tt(v("FV"), v("PC", 0, 16), v("HV%d" % t, 0, 256, 16), OP.add)
+        tc(v("MVV%d" % t, 16 * r, 16 * r + 16), v("FV"))
+        ts(v("FD"), ind(v("FV"), v("K7", 0, 7)), col(B255), OP.subtract)
+        ts(v("g1"), v("NG"), 8192, OP.mult)
+        tt(v("g1"), v("g1"), v("SPf"), OP.add)
+        tt(v("GLf"), v("g1"), v("DGO"), OP.min)
+        tc(v("GLu"), v("GLf"))
+        tc(ind(v("X0"), v("GLu")), v("HV%d" % t))
+        if t == 0:
+            tt(v("LS"), v("LS"), v("GS"), OP.subtract)
+            tc(ind(v("L", 0, 320), pk1), v("LS"))
+
+    def centres():
+        pk1 = v("pk8", 0, 1)
+        tt(v("RB"), v("AD", 0, 256, 16), v("VS", 0, 256, 16), OP.add)
+        tc(ind(v("CE"), pk1), v("RB"))
+        tc(v("CE", 288, 304), v("BT0", 16 * r, 16 * r + 16))
+        tc(v("NU", 288, 304), ind(v("NEI"), pk1))
+        tc(v("CSf"), ind(v("CPf"), pk1))
+
+    def by_posting(bank, x, m, w, t, acc_=True):
+        nb = nbs(t)
+        return [(v(bank, 128 * b + m, 128 * b + 128, 16, 0, nb[b]), x(b), v("W8", 8 * w, 8 * w + 8), not acc_, not acc_) for b in range(3)]
+
+    def listed(x, bank, t, first):
+        tt(v("Y"), ind(v(x), v("L8u")), v("MKU"), OP.mult)
+        mm(*(first + [(v(bank, 0, 24), v("ZW", 112 - 16 * q, 240 - 16 * q), v("Y", 24 * q, 24 * q + 24), q == 0 and not first, q == 7) for q in range(8)]))
+
+    def near(t):
+        P, nb, tab = 288 + 16 * t, nbs(t), v("TAB%d" % t)
+        tc(ind(tab, v("NO%d" % t, 0, 1)), v("IOB", 0, 16))
+        tc(ind(tab, v("NL%d" % t, 0, 7)), v("IOB", 16, 128))
+        phase(2, lambda a, b: lin(v("TN", 16 * a, 16 * b), ind(tab, v("NU", a, b))), chunks(0, P))
+        for b in range(3):
+            mm(*[(v("PN", 128 * b + m, 128 * b + 128, 16, 0, nb[b]), v("TN", 2048 * b + m, 2048 * b + 16 * nb[b], 16), v("W8", 32, 40), True, True) for m in range(16)], acc=True)
+        scan(v("kn"), v("DN"), v("PN", 0, 384), 0.0, OP.add, OP.min)
+        ts(v("Ti"), v("kn", 15, 384, 16), 127, OP.bitwise_and)
+        listed("Ti", "PC", t, [])
+        ts(v("TLu"), v("PC", 0, 24), -1, OP.mult)
+        lin(v("BQ", 0, P), ind(v("BT%d" % t), v("TLu", 0, P // 16)))
+        ts(v("hs"), v("kn", 15, 384, 16), 128, OP.is_lt)
+        ts(v("t24"), v("Ti"), 16, OP.add)
+        tt(v("TH"), v("t24"), v("hs"), OP.mult)
+
+    def gains(t, c, out, sign):
+        P, nb, V, k = 288 + 16 * t, nbs(t), "VW"[t], MS[2 * t + sign]
+        if k:
+            mm((v("PX", 0, P), v("ID"), v(c, 0, P), True, True))
+            mm(*[(v("PG", 128 * b, 128 * b + 128, 1, 0, nb[b]), v(c, 128 * b, 128 * b + nb[b]), v("CO%d" % (2 * t + sign)), False, False) for b in range(3)], acc=True)
+
+        def row(m):
+            o, x = v(out, 304 * m, 304 * m + P), v(V, m, 16 * P, 16)
+            if m < k:
+                tt(o, x, v("PX", 0, P), OP.max)
+                if m >= MS[2 * t + 1 - sign]:
+                    mm(*by_posting("PG", lambda b: v(V, 2048 * b + m, 2048 * b + 16 * nb[b], 16), m, 3 - sign, t), acc=True)
+            else:
+                pm = v("PM%d" % (m % 2), 0, P)
+                mm((pm, v("ID"), x, True, False), (pm, v("NID"), v(c, 0, P), False, True))
+                act(o, pm, AF.Abs)
+            mm(*by_posting("PG", lambda b: v(out, 304 * m + 128 * b, 304 * m + 128 * b + nb[b]), m, sign + (0 if m < k else 2), t), acc=True)
+        phase(2 if k else 1, row, [(m,) for m in sorted(range(16), key=lambda m: m / k if m < k else (m - k) / (16 - k))])
+
+    def absorb(out, win, lst, x, n, k):
+        def part(a, b):
+            o, w, y = v(out, 16 * a, 16 * b), ind(win, v(lst, a, b)), v(x, 16 * a, 16 * b)
+            if k and a // CH % k == k - 1:
+                h, pm = v("H", 16 * a, 16 * b), v("PM%d" % (a // CH // k % 2), 0, 16 * (b - a))
+                act(h, w)
+                mm((pm, v("ID"), h, True, True))
+                tt(o, pm, y, OP.max)
+            else:
+                tt(o, w, y, OP.max)
+        phase(1, part, chunks(0, n))
+
+    def keys_open(t):
+        nb = nbs(t)
+        mm((v("PG", 0, 384), v("FST"), v("CNG"), True, False))
+        mm(*[(v("PG", 128 * b, 128 * b + 128, 1, 0, nb[b]), v("LO", 128 * b, 128 * b + nb[b]), v("IDL"), False, False) for b in range(3)], acc=True)
+
+    def turn(x, out, banks, t):
+        P, nb = 288 + 16 * t, nbs(t)
+        mm(*[(v("PA", 128 * b, 128 * b + nb[b], 1, 0, 8), v(x, 8 * b, 8 * b + 8), v("ID", 0, nb[b]), True, True) for b in range(3)])
+        act(v(out, 0, P, 1, 0, 8), v("PA", 0, P, 1, 0, 8))
+        for bank in banks:
+            mm((v(bank, 0, P), v("RP", 0, 128, 1, 0, 8), v(out, 0, P, 1, 0, 8), True, True))
+
+    def pick(t):
+        P, last = 288 + 16 * t, v("SC", 287 + 16 * t, 2432, 304)
+        mm((v("PG", 0, 16), v("FST"), v("ZER", 0, 16), False, True))
+        scan(v("ki"), v("DG"), v("PG", 0, 384), 0.0, OP.add, OP.max)
+        tt(v("X24"), v("ki", 15, 384, 16), v("TH"), OP.min)
+        turn("X24", "T8", ("PM0", "PM1"), t)
+        ts(v("lo"), v("ki", 15, 384, 16), 15, OP.bitwise_and)
+        listed("lo", "PC", t, [(v("PC", 0, 24), v("ID"), v("C256"), True, False)])
+        ts(v("VLu"), v("PC", 0, 24), col(R15), OP.add)
+        lin(v("VB", 0, P), ind(v("VW"[t], 0, 16 * P), v("VLu", 0, P // 16)))
+        tc(v("TS", 0, P), v("PM1", 0, P))
+        for q in range(8):
+            z = v("ZQ", 304 * q, 304 * q + P)
+            if q < NACT:
+                act(z, v("PM0", 0, P), AF.Abs, col(TQB + q), 1000.0)
+            else:
+                ts(z, v("TS", 0, P), col(TQ + q), OP.not_equal, 1000, OP.mult)
+            scan(v("SC", 304 * q, 304 * q + P), v("D0", 0, P), z, 1000.0, OP.add, OP.min)
+        ts(v("QTu"), last, P - 1, OP.add, 304, OP.min)
+        tt(v("MV%d" % t), ind(v("VB"), v("QTu")), v("PR%d" % t), OP.min)
+        exchange("c%d" % t, v("MV%d" % t), [v("XA") if t else v("X1", 3584, 3696)])
+
+    def own(t):
+        P, last = 288 + 16 * t, v("SC", 287 + 16 * t, 2432, 304)
+        tc(v("L24"), v("lo"))
+        turn("L24", "L8", ("PX",), t)
+        act(v("LOS", 0, P), v("PX", 0, P))
+        ts(v("OHm"), ind(v("LOS"), v("QTu")), col(F15), OP.is_equal)
+        if t == 0:
+            ts(v("QLf"), last, P - 1, OP.add)
+            tt(v("QLf"), v("QLf"), v("DQ"), OP.min)
+            tc(v("QLu"), v("QLf"))
+            tt(v("LN"), ind(v("L", 0, 320), v("QTu")), v("OHm"), OP.subtract)
+            tc(ind(v("L"), v("QLu")), v("LN"))
+        lin(v("PIm", 0, P), v("PIf", 0, P), None, -1904.0)
+        tt(v("PGh"), ind(v("PIm"), v("QTu")), v("OHm"), OP.mult)
+        ts(v("t24", 0, 8), last, 0, OP.is_gt)
+        tt(v("DMh"), v("t24", 0, 8), v("DM"), OP.mult)
+        mm(*([(v("PB", 0, 8), v("IDh"), v("DMh"), True, False)] + [(v("PB", 0, 8), v("UF", 15 - k, 143 - k), v("PGh", k, 128, 16), False, k == 15) for k in range(16)]))
+        ts(v("MVL"), v("PB", 0, 8), 1904, OP.add)
+        tc(ind(v("X0"), v("MVL")), v("MVV%d" % t))
+        mm((v("PB", 0, 16), v("RC"), v("MV%d" % t, 16 * r, 16 * r + 16), True, True), (v("PB", 16, 32), v("BOh"), v("PGh", 16 * r, 16 * r + 16), True, True))
+        ts(v("exo"), v("PB", 0, 16), 0, OP.is_gt)
+        ts(v("D1", 6, 128, 8), v("PB", 0, 16), 0, OP.is_le)
+        tt(v("ROo"), v("RO"), v("exo"), OP.mult)
+        ts(v("g1"), v("SPf"), -1904, OP.add)
+        tt(v("g1"), v("PB", 16, 32), v("g1"), OP.subtract)
+        tt(v("g1"), v("g1"), v("ROo"), OP.mult)
+        tt(v("SPo"), v("g1"), v("SPf"), OP.add)
+        if t == 0:
+            ts(v("g2"), v("PB", 0, 16), -257, OP.add, 0, OP.max)
+            tt(v("g2"), v("g2"), v("CSf"), OP.subtract)
+            tt(v("g2"), v("g2"), v("RO"), OP.mult)
+            tt(v("CSo"), v("g2"), v("CSf"), OP.add)
+            tt(v("RB"), v("GS"), v("ROo"), OP.add)
+            mm((v("PB", 0, 16), v("BO"), v("RB"), True, True))
+            ts(v("T3"), v("PB", 0, 16), -11, OP.add, 8192, OP.mult)
+            tt(v("g3"), v("GS"), v("RO"), OP.add)
+            ts(v("g3"), v("g3"), -1, OP.add, 8192, OP.mult)
+            tt(v("T2"), v("g3"), v("RB"), OP.add)
+        ms(v("PX", 0, 128), 0)
+
+    def land(t):
+        P, n = 288 + 16 * t, v("nn", 6, 128, 8)
+        nx, a0 = ("XA", 0) if t else ("X1", 3584)
+        mm(*[(v("PX", o, 128, 8), v("RN"), v(nx, a0 + 16 * o, a0 + 16 * o + 16), True, True) for o in range(7)])
+        scan(v("nn"), v("PX", 0, 128), v("D1"), 0.0, OP.min, OP.mult)
+        if t == 0:
+            tt(v("F1", P, P + 16), n, v("T3"), OP.is_lt)
+            tt(v("L", P, P + 16), n, v("T2"), OP.is_lt)
+        ts(v("iw"), n, 4095, OP.bitwise_and)
+        tt(v("xw"), v("iw"), v("RO"), OP.mult)
+        tt(v("PIf", P, P + 16), v("xw"), v("SPo"), OP.max)
+        if t == 0:
+            tt(v("CPf", P, P + 16), v("xw"), v("CSo"), OP.add)
+        tt(v("WN"), ind(v("nn"), v("K86", 0, 7)), v("ZC%d" % t), OP.is_equal)
+        tt(v("WN"), v("WN"), v("FD"), OP.mult)
+
+    tc(v("PU", 0, 288), v("POI"))
+    tc(v("PIf", 0, 288), v("POI"))
+    tc(v("ABU"), v("ABI", 0, 224))
+    tc(v("NU", 0, 288), v("NEI", 0, 288))
+    phase(2, lambda a, b: lin(v("H", 16 * a, 16 * b), ind(v("X0", 0, 3584), v("PU", a, b))), chunks(0, 288, 24))
+    for a, b in chunks(0, 288, 72):
+        by_row("PA", "UH", "H", a, b)
+    tt(v("L", 0, 288), v("PA", 0, 288), v("SLOT"), OP.is_equal)
+    ts(v("AI"), v("ABI", 224, 448), 8, OP.arith_shift_right)
+    ts(v("AJ"), v("ABI", 224, 448), 255, OP.bitwise_and)
+    ts(v("A2", 0, 224), v("AI"), 1, OP.add, 256, OP.mult)
+    ts(v("A2", 224, 448), v("AJ"), 1, OP.add, 256, OP.mult)
+    mm(*[(v("PB", 64 * q + 16 * j, 64 * q + 16 * j + 16, 1, 0, 112), v("A2", j, 448, 4), v("ID", 16 * q, 16 * q + 16), True, True) for q in range(8) for j in range(4)])
+    lin(v("S3", 0, 512, 1, 0, 112), v("PB", 0, 512, 1, 0, 112))
+    dma("s", [(v("XB", 0, 3584, 1, 16 * q + 14, 16 * q + 16), v("S3", 64 * q, 64 * q + 64, 1, 0, 112)) for q in range(8)])
+    full(0, 0, 288)
+    count(0, 0, 304, 0)
+    numbers(0, v("acc", 0, 1), 152.0)
+    first_live(0, 304)
+    absorb("X1", v("X0", 0, 3808), "ABU", "XB", 224, KA[0])
+    split(0)
+    phase(2, lambda a, b: lin(v("V", 16 * a, 16 * b), ind(v("X1", 0, 3584), v("PU", a, b))), chunks(0, 288))
+    keys_open(0)
+    gains(0, "CE", "MC", 0)
+    near(0)
+    gains(0, "BQ", "MB", 1)
+    for a, b in chunks(0, 288, 96):
+        by_row("PA", "UC", "V", a, b)
+    ts(v("CPf", 0, 288), v("PA", 0, 288), -257, OP.add)
+    ts(v("CU", 0, 288), v("PA", 0, 288), -257, OP.add)
+    centres()
+    pick(0)
     own(0)
-    for a, b in ((0, 128), (128, 288)):
-        for m in range(16):
-            mm(v("PN", a, b), v("UC", 15 - m, 143 - m), v("YR", 16 * a + m, 16 * b, 16), m == 0, m == 15)
-    tc(v("CPf", 0, 288), v("PN", 0, 288))
-    tc(v("CSf"), ind(v("CPf"), v("pk2", 0, 1)))
-    count(1, 0, 288, True)
-    own_c()
-    tc(v("CU", 0, 288), v("CPf", 0, 288))
+    full(1, 0, 288)
+    count(1, 0, 288, 1)
+    ts(v("acc", 2, 3), v("acc", 1, 2), 0.5, OP.mult, 160, OP.add)
+    first_live(0, 288)
     land(0)
-    count(1, 288, 320, False)
-    numbers(1)
+    ts(v("X0", 3584, 3696), v("WN"), col(B255), OP.add)
+    count(1, 288, 320, 3)
+    numbers(1, v("acc", 3, 4), v("acc", 2, 3))
+    first_live(288, 320)
     tc(v("PU", 288, 304), v("PIf", 288, 304))
-    split_a(1)
-    act(v("AA"), v("AD"), AF.Abs)
-    kp("PC", "AA")
-    centres(1)
     tc(v("CU", 288, 304), v("CPf", 288, 304))
-    act(v("V", 4608, 4864), ind(v("X1", 0, 3808), v("PU", 288, 304)), AS, col(K14), col(C13))
-    dma("s", v("ypost", 0, 304), v("PIf", 0, 304))
-    split_b(1)
-    split_c(1)
-    vgather(1, 0)
-    mcent(1, 0)
-    own_ids()
-    split_g()
-    table(1)
-    for b in range(3):
-        near(1, b)
-    vgather(1, 1)
-    vgather(1, 2)
-    mcent(1, 2)
-    gain_open(1)
-    by_slot("PG", "MC", "WC", 1, 0)
-    by_slot("PG", "MC", "WC", 1, 2)
-    near_sums(1, (0, 1, 2))
-    mcent(1, 1, (0, 1))
-    ts(col(AR_), col(M_), 4192, OP.add)
-    ms(v("X0", 3584, 3808), 255)
-    own2(0)
-    go_homes(0)
-    mv_homes(0)
-    land_home(0)
-    arrive("b1", [v("BT1")])
-    targets(1)
-    mcent(1, 1, (2, 3))
-    far(1)
-    split_d(1)
-    go_homes(1)
+    dma("s", [(v("ypost", 0, 304), v("PIf", 0, 304))])
+    split(1)
+    lin(v("V", 4608, 4864), ind(v("X1"), v("PU", 288, 304)), None, col(K256))
+    absorb("W", v("X1"), "CU", "V", 304, KA[1])
+    keys_open(1)
+    gains(1, "CE", "MC", 0)
+    near(1)
+    gains(1, "BQ", "MB", 1)
     pick(1)
     own(1)
-    own_ids()
-    own2(1)
-    mv_homes(1)
-    dma("s", v("yh", 0, 3584, 1, 0, 16, 2), v("X0", 0, 3584, 1, 14, 128, 16))
-    dma("a", v("yh", 0, 3584, 1, 1, 16, 2), v("X0", 0, 3584, 1, 15, 128, 16))
-    ts(col(BC), col(C13), -1, OP.mult, 1, OP.add)
+    dma("s", [(v("yh", 0, 3584, 1, 0, 16, 2), v("X0", 0, 3584, 1, 14, 128, 16))])
+    dma("a", [(v("yh", 0, 3584, 1, 1, 16, 2), v("X0", 0, 3584, 1, 15, 128, 16))])
+    ts(v("YB"), v("X0", 3584, 3696), col(BC), OP.mult)
+    ts(v("XM"), v("X1", 3584, 3696), col(C13), OP.mult)
+    tt(v("YA", 0, 112), v("XM"), v("YB"), OP.add)
+    dma("s", [(v("ya", 0, 112), v("YA", 0, 112))])
+    lin(v("XM"), v("XA"), col(C13), col(B255))
     land(1)
-    dma("s", v("ypost", 304, 320), v("PIf", 304, 320))
-    land_home(1)
-    ts(v("YA", 0, 112), v("X1", 3584, 3696), col(C13), OP.mult)
-    ts(v("YA", 112, 224), v("XA"), col(C13), OP.mult)
-    ts(v("YB"), v("X0", 3584, 3808), col(BC), OP.mult)
-    tt(v("YA"), v("YA"), v("YB"), OP.add)
-    dma("a", v("ya"), v("YA"))
-    cnt["ls"] = nls[0]
-    waits("g", {s: (n, {}) for s, n in cnt.items() if n})
+    dma("s", [(v("ypost", 304, 320), v("PIf", 304, 320))])
+    tt(v("YA", 112, 224), v("XM"), v("WN"), OP.add)
+    dma("a", [(v("ya", 112, 224), v("YA", 112, 224))])
+
+    for i in range(len(ops) - 1, -1, -1):
+        o = ops[i]
+        o["rank"] = o.get("rank", 0) + min(c for f, c in o["alt"].values()) + o["lat"] + o.get("more", 0)
+        for p in o["pre"]:
+            ops[p]["rank"] = max(ops[p].get("rank", 0), o["rank"])
+    free, left, nxt = {e: 0 for e in "vatgsn"}, [len(o["pre"]) for o in ops], [[] for o in ops]
+    for i, o in enumerate(ops):
+        for p in o["pre"]:
+            nxt[p].append(i)
+    ready = {}
+
+    def enter(i):
+        ready[i] = {e: max([0] + [ops[p]["end"] + (0 if e == "t" == ops[p]["eng"] else ops[p]["lat"]) for p in ops[i]["pre"]]) for e in ops[i]["alt"]}
+
+    for i, n in enumerate(left):
+        if not n:
+            enter(i)
+    while ready:
+        t0, e = min((max(t, free[e]), e) for x in ready.values() for e, t in x.items())
+        mine = sorted((PEN * (e == "v" and len(x) > 1) - ops[i]["rank"], x[e], i) for i, x in ready.items() if e in x)
+        go = [i for w, t, i in mine if t <= t0 and not any(w2 + MARG < w and t0 < t2 < t0 + ops[i]["alt"][e][1] - SLK for w2, t2, j in mine)]
+        if not go:
+            free[e] = min(t for w, t, i in mine if t > t0)
+            continue
+        o = ops[go[0]]
+        o["start"], o["end"], o["eng"] = t0, t0 + o["alt"][e][1], e
+        free[e] = o["end"]
+        del ready[go[0]]
+        for j in nxt[go[0]]:
+            left[j] -= 1
+            if not left[j]:
+                enter(j)
+    know = {e: {} for e in E}
+
+    def waits(e, need):
+        for s, n, k in sorted(need, key=lambda z: -len(z[2])):
+            if know[e].get(s, 0) < n:
+                E[e].wait_ge(T.sem[s], n)
+                for a, b in list(k.items()) + [(s, n)]:
+                    know[e][a] = max(know[e].get(a, 0), b)
+
+    for o in sorted(ops, key=lambda z: z["start"]):
+        e = o["eng"]
+        if e == "n":
+            o["done"] = (o["sem"], cnt[o["sem"]], {})
+            continue
+        waits(e, [ops[p]["done"] for p in o["pre"] if not e == "t" == ops[p]["eng"]])
+        s = o["sem"] or "c" + e
+        for x in o["alt"][e][0]():
+            x.then_inc(T.sem[s], 16 if o["sem"] else 1)
+            cnt[s] = cnt.get(s, 0) + (16 if o["sem"] else 1)
+        o["done"] = (s, cnt.get(s, 0), dict(know[e]))
+    waits("g", [(s, n, {}) for s, n in cnt.items() if n])

@@ -5,7 +5,7 @@ F, B, I, U, H16 = "float32", "bfloat16", "int32", "uint16", "float16"
 _W = {
     B: "X0 4064 XB 3584 X1 3808 XA 112 H 4864 V 4864 W 4864 MC 4864 MB 4864 TN 4864 CE 320 TAB0 2688 TAB1 2688 L 448 LO 320 LB 320 F0 320 F1 320 INC 320 JK 320 ZER 384 Z 320 "
        "BT0 128 BT1 128 MV0 128 MV1 128 BQ 304 VS 272 VSa 256 VSc 256 AD 256 BD 256 AA 256 BA 256 LSE 128 LS 16 GS 16 NG 16 RO 16 RB 16 A2 448 S3 512 TS 304 ZQ 2432 D0 304 Y 192 VB 320 LN 128 FV 16 FD 112 WN 112 "
-       "MVV0 128 MVV1 128 YA 224 YB 112 BO 128 TRI 128 ID 128 NID 128 IDL 128 U16 144 UN16 144 UH 144 UC 144 W8 48 ZW 240 MKU 192 I16 16 I17 16 C15 16 IOB 128 C256 24 HV0 256 HV1 256 FST 128 "
+       "MVV0 128 MVV1 128 YA 224 YB 112 BO 128 TRI 128 ID 128 NID 128 IDL 128 U16 144 UN16 144 UH 144 UC 144 W8 48 ZW 240 MKU 192 I16 16 I17 16 C15 16 IOB 144 C256 24 HV0 256 HV1 256 FST 128 "
        "CNG 384 U1 144 RP 256 X24 24 L24 24 T8 304 L8 304 LOS 320 OHm 128 DN 384 DG 384 CO0 128 CO1 128 CO2 128 CO3 128 RN 128 RC 128 B15 128 PR0 128 PR1 128 D1 128 XM 112 TH 24",
     F: "PIf 320 PIm 320 PB_ 320 CPf 320 SLOT 288 MA 320 acc 4 t1 4 SPf 16 CSf 16 LAf 16 g1 16 g2 16 g3 16 exo 16 ROo 16 SPo 16 CSo 16 T2 16 T3 16 xw 16 hs 24 t24 24 GLf 16 QLf 8 COL 64 "
        "IOT 256 IOS 288 G1 128 G2 128 G3 192 G8 8 SQ 24 L8f 12 C16k 16 DGO 16 DQ 8 DM 8 ZC0 112 ZC1 112 X15f 24 K86f 8",
@@ -33,12 +33,13 @@ for _k in _PS:
     SCRATCH[_k] = ("psum", [128, 512], F)
 _EX = ["a0", "b0", "c0", "a1", "b1", "c1"]
 SEMAPHORES = ["cv", "ca", "ct", "cg"] + ["r" + e for e in _EX] + ["y" + e for e in _EX] + ["ls"] + ["d%d" % i for i in range(16)]
-MS = (4, 8, 4, 8)
-KA = (2, 2)
-PEN, MARG, SLK = 3000, 500, 100
+MS = (8, 8, 8, 8)
+KA = ((1, 3, 5), (1, 3, 5, 7, 9))
+PEN, NIT, NIN = 500, 6, 6
+_ORDER = {}
 CH = 32
 NACT = 5
-GA, SCA, HOP, NET, DMA = 1.6, 3.8, 130, 3000, 1800
+GA, SCA, HOP, NET, DMA = 1.56, 3.8, 185, 3200, 1800
 
 
 def bits(es):
@@ -277,13 +278,11 @@ def rank_program(g, core, T, topo):
                 w += min(c for f, c in o["alt"].values()) / k
 
     dma("s", [(v("POI"), v("post"))])
-    dma("a", [(v("X0", 0, 1792), v("rec", 0, 1792))], 3500)
-    dma("s", [(v("X0", 1792, 3584), v("rec", 1792, 3584))], 3500)
     dma("a", [(v("ABI"), v("absorb"))], 2200)
+    dma("a", [(v("X0", 0, 1792), v("rec", 0, 1792))], 3800)
+    dma("s", [(v("X0", 1792, 3584), v("rec", 1792, 3584))], 3800)
     dma("s", [(v("XB", 0, 3584, 1, 16 * q, 16 * q + 14), v("rec", 0, 3584, 1, 16 * q, 16 * q + 14)) for q in range(8)], 5500)
     dma("s", [(v("CE", 0, 288), v("cen")), (v("NEI", 0, 288), v("near"))], 5500)
-    for i in range(6):
-        ops[i]["more"] = 10 ** 6 * (6 - i)
     ic = [v("IC", i, i + 1) for i in range(3)]
     iota(ic[0], [[0, 1]], 0, 1)
     iota(v("IOT"), [[1, 256]])
@@ -297,10 +296,9 @@ def rank_program(g, core, T, topo):
     iota(v("C256"), [[256, 24]])
     iota(v("SQ"), [[1, 8], [8, 3]])
     iota(v("ZW"), [[1, 240]], -112)
-    iota(v("IOB", 0, 16), [[1, 16]], 16 * r)
-    for a, b, o in ((0, r, 0), (r, 7, 16)):
-        if b > a:
-            iota(v("IOB", 16 + 16 * a, 16 + 16 * b), [[1, 16 * (b - a)]], 16 * a + o)
+    iota(v("IOB", 0, 16 * r + 16), [[1, 16 * r + 16]])
+    iota(v("IOB", 16 * r, 128), [[1, 128 - 16 * r]], 16 * r + 16)
+    iota(v("IOB", 128, 144), [[1, 16]], 16 * r)
     ts(ic[1], ic[0], 15, OP.bitwise_and)
     ts(ic[2], ic[0], 4, OP.arith_shift_right)
     for i in range(3):
@@ -439,22 +437,27 @@ def rank_program(g, core, T, topo):
         exchange("b%d" % t, bt, [v("BT%d" % t, 0, 16 * r), v("BT%d" % t, 16 * r + 16, 128)])
         tc(v("LO", 0, P), v("L", 0, P))
         tc(ind(v("LO", 0, P + 16), pk1), v("ZER", 0, 16))
+
+    def parted(t):
+        pk1 = v("pk8", 0, 1)
         ts(v("t1", 2, 3), v("kr"), -1, OP.mult, col(R15), OP.add)
         ts(v("RB"), v("I16"), v("t1", 2, 3), OP.mult)
-        mm((v("PC", 0, 16), v("BO"), v("RB"), True, True))
-        tc(v("LBu"), v("PC", 0, 16))
+        pb = v("PB", 0, 16)
+        mm((pb, v("BO"), v("RB"), True, True))
+        tc(v("LBu"), pb)
         tt(v("BD"), ind(v("VS"), v("LBu")), v("VSc"), OP.subtract)
         act(v("BA"), v("BD"), AF.Abs)
         tc(v("LS"), ind(v("L", 0, 320), pk1))
         tc(v("SPf"), ind(v("PIf"), pk1))
-        mm(*([(v("PC", 0, 16), v("IDL"), v("LS"), True, False)] + [(v("PC", 0, 16), v(u, 15 - m, 143 - m), v(x, m, 256, 16), False, x == "BA" and m == 15) for u, x in (("U16", "AA"), ("UN16", "BA")) for m in range(16)]))
-        ts(v("GS"), v("PC", 0, 16), 2 ** 23, OP.is_gt)
-        ts(v("NG"), v("PC", 0, 16), 2 ** 23, OP.is_le)
-        mm((v("PC", 0, 16), v("TRI"), v("NG"), True, True))
-        ts(v("g1"), v("PC", 0, 16), 1, OP.is_equal)
+        for u, x in (("U16", "AA"), ("UN16", "BA")):
+            mm(*([(pb, v("IDL"), v("LS"), True, False)][:x == "AA"] + [(pb, v(u, 15 - m, 143 - m), v(x, m, 256, 16), False, x == "BA" and m == 15) for m in range(16)]))
+        ts(v("GS"), pb, 2 ** 23, OP.is_gt)
+        ts(v("NG"), pb, 2 ** 23, OP.is_le)
+        mm((pb, v("TRI"), v("NG"), True, True))
+        ts(v("g1"), pb, 1, OP.is_equal)
         tt(v("RO"), v("g1"), v("NG"), OP.mult)
-        mm((v("PC", 0, 16), v("B15"), v("RO"), True, True))
-        tt(v("FV"), v("PC", 0, 16), v("HV%d" % t, 0, 256, 16), OP.add)
+        mm((pb, v("B15"), v("RO"), True, True))
+        tt(v("FV"), pb, v("HV%d" % t, 0, 256, 16), OP.add)
         tc(v("MVV%d" % t, 16 * r, 16 * r + 16), v("FV"))
         ts(v("FD"), ind(v("FV"), v("K7", 0, 7)), col(B255), OP.subtract)
         ts(v("g1"), v("NG"), 8192, OP.mult)
@@ -484,8 +487,8 @@ def rank_program(g, core, T, topo):
 
     def near(t):
         P, nb, tab = 288 + 16 * t, nbs(t), v("TAB%d" % t)
-        tc(ind(tab, v("NO%d" % t, 0, 1)), v("IOB", 0, 16))
-        tc(ind(tab, v("NL%d" % t, 0, 7)), v("IOB", 16, 128))
+        tc(ind(tab, v("NO%d" % t, 0, 1)), v("IOB", 128, 144))
+        tc(ind(tab, v("NL%d" % t, 0, 7)), v("IOB", 0, 112))
         phase(2, lambda a, b: lin(v("TN", 16 * a, 16 * b), ind(tab, v("NU", a, b))), chunks(0, P))
         for b in range(3):
             mm(*[(v("PN", 128 * b + m, 128 * b + 128, 16, 0, nb[b]), v("TN", 2048 * b + m, 2048 * b + 16 * nb[b], 16), v("W8", 32, 40), True, True) for m in range(16)], acc=True)
@@ -511,7 +514,7 @@ def rank_program(g, core, T, topo):
                 if m >= MS[2 * t + 1 - sign]:
                     mm(*by_posting("PG", lambda b: v(V, 2048 * b + m, 2048 * b + 16 * nb[b], 16), m, 3 - sign, t), acc=True)
             else:
-                pm = v("PM%d" % (m % 2), 0, P)
+                pm = v(("PM0", "PM1", "PA", "PN")[m % (3 + sign)], 0, P)
                 mm((pm, v("ID"), x, True, False), (pm, v("NID"), v(c, 0, P), False, True))
                 act(o, pm, AF.Abs)
             mm(*by_posting("PG", lambda b: v(out, 304 * m + 128 * b, 304 * m + 128 * b + nb[b]), m, sign + (0 if m < k else 2), t), acc=True)
@@ -520,14 +523,14 @@ def rank_program(g, core, T, topo):
     def absorb(out, win, lst, x, n, k):
         def part(a, b):
             o, w, y = v(out, 16 * a, 16 * b), ind(win, v(lst, a, b)), v(x, 16 * a, 16 * b)
-            if k and a // CH % k == k - 1:
-                h, pm = v("H", 16 * a, 16 * b), v("PM%d" % (a // CH // k % 2), 0, 16 * (b - a))
+            if a // 32 in k:
+                h, pm = v("H", 16 * a, 16 * b), v("PM%d" % (k.index(a // 32) % 2), 0, 16 * (b - a))
                 act(h, w)
                 mm((pm, v("ID"), h, True, True))
                 tt(o, pm, y, OP.max)
             else:
                 tt(o, w, y, OP.max)
-        phase(1, part, chunks(0, n))
+        phase(1, part, chunks(0, n, 32))
 
     def keys_open(t):
         nb = nbs(t)
@@ -641,14 +644,15 @@ def rank_program(g, core, T, topo):
     absorb("X1", v("X0", 0, 3808), "ABU", "XB", 224, KA[0])
     split(0)
     phase(2, lambda a, b: lin(v("V", 16 * a, 16 * b), ind(v("X1", 0, 3584), v("PU", a, b))), chunks(0, 288))
+    for a, b in chunks(0, 288, 96):
+        by_row("PB", "UC", "V", a, b)
+    ts(v("CPf", 0, 288), v("PB", 0, 288), -257, OP.add)
+    tc(v("CU", 0, 288), v("CPf", 0, 288))
+    parted(0)
     keys_open(0)
     gains(0, "CE", "MC", 0)
     near(0)
     gains(0, "BQ", "MB", 1)
-    for a, b in chunks(0, 288, 96):
-        by_row("PA", "UC", "V", a, b)
-    ts(v("CPf", 0, 288), v("PA", 0, 288), -257, OP.add)
-    ts(v("CU", 0, 288), v("PA", 0, 288), -257, OP.add)
     centres()
     pick(0)
     own(0)
@@ -665,6 +669,7 @@ def rank_program(g, core, T, topo):
     tc(v("CU", 288, 304), v("CPf", 288, 304))
     dma("s", [(v("ypost", 0, 304), v("PIf", 0, 304))])
     split(1)
+    parted(1)
     lin(v("V", 4608, 4864), ind(v("X1"), v("PU", 288, 304)), None, col(K256))
     absorb("W", v("X1"), "CU", "V", 304, KA[1])
     keys_open(1)
@@ -690,33 +695,37 @@ def rank_program(g, core, T, topo):
         o["rank"] = o.get("rank", 0) + min(c for f, c in o["alt"].values()) + o["lat"] + o.get("more", 0)
         for p in o["pre"]:
             ops[p]["rank"] = max(ops[p].get("rank", 0), o["rank"])
-    free, left, nxt = {e: 0 for e in "vatgsn"}, [len(o["pre"]) for o in ops], [[] for o in ops]
+    nxt = [[] for o in ops]
     for i, o in enumerate(ops):
         for p in o["pre"]:
             nxt[p].append(i)
-    ready = {}
 
-    def enter(i):
-        ready[i] = {e: max([0] + [ops[p]["end"] + (0 if e == "t" == ops[p]["eng"] else ops[p]["lat"]) for p in ops[i]["pre"]]) for e in ops[i]["alt"]}
+    def place(key, back):
+        busy, at = {e: [] for e in "vatgsn"}, [None] * len(ops)
+        for i in sorted(range(len(ops)), key=lambda j: key[j] if back or j >= NIN else j - 10 ** 9):
+            best = None
+            for e, (f, c) in ops[i]["alt"].items():
+                t0 = max([ops[i]["lat"] if back else 0] + [at[p][1] + (0 if e == "t" == at[p][2] else ops[i if back else p]["lat"]) for p in (nxt[i] if back else ops[i]["pre"])])
+                for x, y in busy[e]:
+                    if t0 + c <= x:
+                        break
+                    t0 = max(t0, y)
+                if best is None or t0 + c + PEN * (e == "v") < best[0]:
+                    best = (t0 + c + PEN * (e == "v"), t0, t0 + c, e)
+            at[i] = best[1:]
+            busy[best[3]].append(best[1:3])
+            busy[best[3]].sort()
+        return at
 
-    for i, n in enumerate(left):
-        if not n:
-            enter(i)
-    while ready:
-        t0, e = min((max(t, free[e]), e) for x in ready.values() for e, t in x.items())
-        mine = sorted((PEN * (e == "v" and len(x) > 1) - ops[i]["rank"], x[e], i) for i, x in ready.items() if e in x)
-        go = [i for w, t, i in mine if t <= t0 and not any(w2 + MARG < w and t0 < t2 < t0 + ops[i]["alt"][e][1] - SLK for w2, t2, j in mine)]
-        if not go:
-            free[e] = min(t for w, t, i in mine if t > t0)
-            continue
-        o = ops[go[0]]
-        o["start"], o["end"], o["eng"] = t0, t0 + o["alt"][e][1], e
-        free[e] = o["end"]
-        del ready[go[0]]
-        for j in nxt[go[0]]:
-            left[j] -= 1
-            if not left[j]:
-                enter(j)
+    key, shape = [-o["rank"] for o in ops], tuple(tuple(o["pre"]) for o in ops)
+    for n in range(0 if shape in _ORDER else NIT):
+        at = place(key, False)
+        end = max(x[1] + o["lat"] for x, o in zip(at, ops))
+        if n == 0 or end < _ORDER[shape][0]:
+            _ORDER[shape] = (end, at)
+        key = [-x[1] for x in place([-x[1] for x in at], True)]
+    for o, x in zip(ops, _ORDER[shape][1]):
+        o["start"], o["eng"] = x[0], x[2]
     know = {e: {} for e in E}
 
     def waits(e, need):

@@ -3,14 +3,14 @@ from concourse.mybir import AluOpType as OP, AxisListType, ActivationFunctionTyp
 
 F, B, I, U, H16 = "float32", "bfloat16", "int32", "uint16", "float16"
 _W = {
-    B: "X0 4064 XB 3584 X1 3808 XA 112 H 4864 V 4864 W 4864 MC 4864 MB 4864 TN 4864 CE 320 TAB0 2688 TAB1 2688 L 448 LO 320 LB 320 F0 320 F1 320 INC 320 JK 320 ZER 384 Z 320 "
-       "BT0 128 BT1 128 MV0 128 MV1 128 BQ 304 VS 272 VSa 256 VSc 256 AD 256 BD 256 AA 256 BA 256 LSE 128 LS 16 GS 16 NG 16 RO 16 RB 16 A2 448 S3 512 TS 304 ZQ 2432 D0 304 Y 192 VB 320 LN 128 FV 16 FD 112 WN 112 "
-       "MVV0 128 MVV1 128 YA 224 YB 112 BO 128 TRI 128 ID 128 NID 128 IDL 128 U16 144 UN16 144 UH 144 UC 144 W8 48 ZW 240 MKU 192 I16 16 I17 16 C15 16 IOB 144 C256 24 HV0 256 HV1 256 FST 128 "
-       "CNG 384 U1 144 RP 256 X24 24 L24 24 T8 304 L8 304 LOS 320 OHm 128 DN 384 DG 384 CO0 128 CO1 128 CO2 128 CO3 128 RN 128 RC 128 B15 128 PR0 128 PR1 128 D1 128 XM 112 TH 24",
-    F: "PIf 320 PIm 320 PB_ 320 CPf 320 SLOT 288 MA 320 acc 4 t1 4 SPf 16 CSf 16 LAf 16 g1 16 g2 16 g3 16 exo 16 ROo 16 SPo 16 CSo 16 T2 16 T3 16 xw 16 hs 24 t24 24 GLf 16 QLf 8 COL 64 "
-       "IOT 256 IOS 288 G1 128 G2 128 G3 192 G8 8 SQ 24 L8f 12 C16k 16 DGO 16 DQ 8 DM 8 ZC0 112 ZC1 112 X15f 24 K86f 8",
+    B: "X0 4064 XB 3584 X1 3808 XA 112 H 4864 V 4864 W 4864 MC 4864 MB 4864 MC2 4864 MB2 4864 TN 4864 CE 320 TAB0 2688 TAB1 2688 L 448 SF0 320 SF1 320 OHB 320 F0 320 F1 320 INC 320 JK 320 ZER 16 ONE 384 Z 16 "
+       "BT0 128 BT1 128 MV0 128 MV1 128 BQ 304 VS 272 VSa 256 AD 256 BD 256 AA 256 BA 256 LSE 128 LS 16 GS 16 NG 16 RO 16 ROo 16 BV 16 A2 448 S3 512 ZQ 2432 D0 608 Y 192 VB 320 LN 128 FV 16 FD 112 WN 112 "
+       "MVV0 128 MVV1 128 YA 224 BO 128 TRI 128 ID 128 NID 128 IDL 128 U16 144 UN16 144 UH 144 UC 144 W8 40 ZW 240 MKU 192 I16 16 I17 16 C15 16 IOB 144 C256 24 C16b 16 HV0 256 HV1 256 FST 128 "
+       "U1 144 RP 128 X24 24 T8 304 OHm 128 DN 384 DG 384 CO0 128 CO1 128 CO2 128 CO3 128 RN 128 RC 128 B15 128 PR0 128 PR1 128 D1 128 XM 112 TH 24",
+    F: "PIf 320 PIm 320 PRa 128 CPf 320 SLOT 288 acc 4 t1 4 pre 10 CSf 16 SPf 16 g1 16 exo 16 CSo 16 SPo 16 E32 32 T2 16 T3 16 xw 16 hs 24 t24 24 GLf 16 QLf 8 COL 64 "
+       "IOT 256 IOS 288 G1 128 G2 128 SQ 24 L8f 12 C16k 16 DGO 16 DQ 8 DM 8 ZC0 112 ZC1 112",
     I: "POI 288 ABI 448 NEI 320 kx 1 kr 1 kn 384 ki 384 Ti 24 lo 24 IC 4 AI 224 AJ 224 nn 128 iw 16",
-    U: "PU 304 ABU 224 NU 304 pk8 8 NO0 2 NO1 2 NL0 8 NL1 8 SPu 16 CSu 16 LAu 16 obu 2 LBu 16 TLu 24 QTu 8 VLu 24 QLu 8 MVL 8 GLu 16 L8u 12 CU 304 X15 24 XS 24 K86 8 K7 8",
+    U: "PU 304 ABU 224 NU 304 pk8 8 NO0 2 NO1 2 NL0 8 NL1 8 SPu 16 CSu 16 LAu 16 obu 2 K16 16 TLu 24 QTu 8 VLu 24 MLu 24 QLu 8 MVL 8 GLu 16 L8u 12 CU 304 K86 8 K7 8",
     H16: "SC 2432 PGh 128 UF 144 BOh 128 IDh 128 DMh 8",
 }
 _S = {}
@@ -19,7 +19,8 @@ for _d, _t in _W.items():
     for _i in range(0, len(_t), 2):
         _S[_t[_i]] = (int(_t[_i + 1]), _d)
 _PS = ["PA", "PB", "PC", "PX", "PN", "PG", "PM0", "PM1"]
-_OWN = ("X0 XB X1 XA H V W MC MB TN CE TAB0 TAB1 L LO LOS BT0 BT1 MV0 MV1 VS S3 ZQ VB FV YA PIf PIm CPf MA POI ABI NEI kn ki Ti lo nn SC").split()
+_WHOLE = ["BT0", "BT1", "IOB"]
+_OWN = "X0 XB X1 XA H V W MC MB MC2 MB2 TN CE TAB0 TAB1 L SF0 SF1 OHB BV I16 MV0 MV1 VS S3 ZQ VB FV YA PIf PIm CPf POI ABI NEI kn ki Ti lo nn SC".split() + _WHOLE
 SCRATCH, _PACK, _n = {}, {}, {}
 for _k, (_w, _d) in _S.items():
     if _k in _OWN or _d == U:
@@ -32,14 +33,21 @@ for _d in _n:
 for _k in _PS:
     SCRATCH[_k] = ("psum", [128, 512], F)
 _EX = ["a0", "b0", "c0", "a1", "b1", "c1"]
-SEMAPHORES = ["cv", "ca", "ct", "cg"] + ["r" + e for e in _EX] + ["y" + e for e in _EX] + ["ls"] + ["d%d" % i for i in range(16)]
-MS = (8, 8, 8, 8)
-KA = ((1, 3, 5), (1, 3, 5, 7, 9))
-PEN, NIT, NIN = 500, 6, 6
-_ORDER = {}
+SEMAPHORES = ["cv", "ca", "ct", "cg"] + ["r" + e for e in _EX] + ["y" + e for e in _EX] + ["ls"] + ["d%d" % i for i in range(20)]
+MS = (8, 8, 4, 8)
+KA = ((1, 3, 5), (0, 1))
 CH = 32
-NACT = 5
-GA, SCA, HOP, NET, DMA = 1.56, 3.8, 185, 3200, 1800
+CHH = 36
+TF = 5
+QUAD = (0, 0, 1, 0)
+NAB, DS3 = 4000, 3000
+SCANS = ((2, 4), (0, 2), (4, 6), (6, 8))
+NACT = (0, 1, 4, 5, 6)
+GA, SCA, HOP, NET, DMA = 1.56, 3.8, 225, 3400, 1900
+PEN, NIT, NIN = (100, 200, 350, 500, 700, 1000, 1500), 6, 5
+GX, GL = 1.4, 400
+NSW, TOL, SEED = 20000, 400, 1
+_ORDER = {}
 
 
 def bits(es):
@@ -68,19 +76,23 @@ def plan(r, T, topo):
 
 def engines_to(ex, r, d, T, topo):
     direct, rel, off, on = plan(r, T, topo)
-    q, es = [(direct, off)] + [(q, topo.engines(x, T.cores[d])) for x, q in rel if d in q], None
-    q, es = q[-1]
+    q, es = ([(direct, off)] + [(q, topo.engines(x, T.cores[d])) for x, q in rel if d in q])[-1]
     return parts(es, len(q))[q.index(d)] if ex[0] == "c" else es
 
 
-def message(ex, r, d, T):
+def order(r, T, topo):
+    direct, rel, off, on = plan(r, T, topo)
+    return [d for x, q in rel for d in q] + direct + [r]
+
+
+def message(ex, r, d, T, topo):
     t, o = ex[1], r if r < d else r - 1
     if ex[0] == "a":
         return T["NO" + t][:, 0:1], T["NL" + t][:, o:o + 1]
     if ex[0] == "b":
         return T["BT" + t][:, 16 * r:16 * r + 16], T["BT" + t][:, 16 * r:16 * r + 16]
-    a = 16 * o + (3584 if t == "0" else 0)
-    return T["MV" + t][:, 16 * d:16 * d + 16], T["X1" if t == "0" else "XA"][:, a:a + 16]
+    a, p = 16 * o + (3584 if t == "0" else 0), 16 * order(r, T, topo).index(d)
+    return T["MV" + t][:, p:p + 16], T["X1" if t == "0" else "XA"][:, a:a + 16]
 
 
 def dst(topo, x, c):
@@ -91,9 +103,9 @@ def dst(topo, x, c):
 def onward(ex, r, q, core, T, topo):
     if ex[0] == "c":
         return [RemoteDMATransfer(dst_ids=[dst(topo, T.cores[d], core)], dma_engine_mask=bits(engines_to(ex, r, d, T, topo)), remote_sem=T.sem["y" + ex],
-                                  src=message(ex, r, d, T)[0], dst=message(ex, r, d, T)[1]) for d in q]
+                                  src=message(ex, r, d, T, topo)[0], dst=message(ex, r, d, T, topo)[1]) for d in q]
     return [RemoteDMATransfer(dst_ids=[dst(topo, T.cores[d], core) for d in q], dma_engine_mask=bits(engines_to(ex, r, q[0], T, topo)), remote_sem=T.sem["y" + ex],
-                              srcs=[message(ex, r, q[0], T)[0]], dsts=[message(ex, r, d, T)[1] for d in q])]
+                              srcs=[message(ex, r, q[0], T, topo)[0]], dsts=[message(ex, r, d, T, topo)[1] for d in q])]
 
 
 def relay_program(g, core, T, topo):
@@ -107,6 +119,125 @@ def relay_program(g, core, T, topo):
                     g.remote_dma_fused(onward(ex, r, q, core, T, topo), local_sem=T.sem.ls)
                     n += len(topo.engines(core, T.cores[q[0]]))
                 g.wait_ge(T.sem.ls, n)
+
+
+def arrange(pre, lat, alt, more):
+    n = len(pre)
+    nxt = [[] for i in range(n)]
+    rank = [0] * n
+    for i in range(n - 1, -1, -1):
+        rank[i] += min(alt[i].values()) + lat[i] + more[i]
+        for p in pre[i]:
+            nxt[p].append(i)
+            rank[p] = max(rank[p], rank[i])
+
+    def place(key, alt, back=False, pen=0):
+        busy, at = {e: [] for e in "vatgsn"}, [None] * n
+        for i in sorted(range(n), key=lambda j: key[j] if back or j >= NIN else j - 10 ** 9):
+            best = None
+            for e, c in alt[i].items():
+                t0 = lat[i] if back else 0
+                for p in (nxt[i] if back else pre[i]):
+                    t0 = max(t0, at[p][1] + (0 if e == "t" == at[p][2] else lat[i if back else p]))
+                q = busy[e]
+                k = len(q)
+                while k and q[k - 1][1] > t0:
+                    k -= 1
+                while k < len(q) and t0 + c > q[k][0]:
+                    t0, k = max(t0, q[k][1]), k + 1
+                if best is None or t0 + c + pen * (e == "v") < best[0]:
+                    best = (t0 + c + pen * (e == "v"), t0, t0 + c, e, k)
+            at[i] = best[1:4]
+            busy[best[3]].insert(best[4], best[1:3])
+        return at
+
+    def end(at):
+        return max(x[1] + y for x, y in zip(at, lat))
+
+    at = None
+    for pen in PEN:
+        key = [-x for x in rank]
+        for k in range(NIT):
+            a = place(key, alt, False, pen)
+            if at is None or end(a) < end(at):
+                at = a
+            key = [-x[1] for x in place([-x[1] for x in a], alt, True, pen)]
+    marks, seed = [i for i in range(n) if "n" in alt[i]], [SEED]
+
+    def pick(xs):
+        seed[0] = (seed[0] * 1103515245 + 12345) % 2 ** 31
+        return xs[(seed[0] >> 8) % len(xs)]
+
+    def worth(at):
+        return end(at) + 0.2 * sum(at[i][1] for i in marks) + 0.05 * sum(x[1] for x in at) / n
+
+    gap = [[(p, 0 if "t" in alt[i] and "t" in alt[p] else lat[p]) for p in pre[i]] for i in range(n)]
+
+    def again(key, one, old, seq0, j0):
+        seq = sorted(range(n), key=lambda j: key[j])
+        f = 0
+        while f < n and seq[f] == seq0[f] != j0:
+            f += 1
+        busy, at = {e: [] for e in "vatgsn"}, list(old)
+        for x in sorted(at[i] for i in seq[:f]):
+            busy[x[2]].append(x)
+        for i in seq[f:]:
+            e, t0 = one[i], 0
+            c, q = alt[i][e], busy[e]
+            for p, d in gap[i]:
+                if at[p][1] + d > t0:
+                    t0 = at[p][1] + d
+            k = m = len(q)
+            while k and q[k - 1][1] > t0:
+                k -= 1
+            while k < m and t0 + c > q[k][0]:
+                if q[k][1] > t0:
+                    t0 = q[k][1]
+                k += 1
+            at[i] = (t0, t0 + c, e)
+            q.insert(k, at[i])
+        return at, seq
+
+    key, one, kept = [x[0] if i >= NIN else i - 10 ** 9 for i, x in enumerate(at)], [x[2] for x in at], at
+    at, seq = again(key, one, at, [-1] * n, -1)
+    now, paths = worth(at), {}
+    for k in range(NSW):
+        if paths.get("at") is not at:
+            paths = {"at": at, "before": {x[1:]: j for j, x in enumerate(at)}, "last": max(range(n), key=lambda j: at[j][1] + lat[j])}
+        i = pick(marks + [paths["last"]] * 3)
+        if i not in paths:
+            pairs = paths[i] = []
+            while i is not None:
+                c = [p for p, d in gap[i] if at[p][1] + d == at[i][0]]
+                j = pick(c) if c else paths["before"].get((at[i][0], at[i][2]))
+                if not c and j is not None:
+                    pairs.append((j, i))
+                i = j
+        else:
+            pairs = paths[i]
+        if not pairs:
+            continue
+        (a, b), how, key2, one2 = pick(pairs), pick((0, 1, 2)), list(key), list(one)
+        free, j0 = [j for j in (a, b) if len(alt[j]) > 1], -1
+        if how == 0 and free:
+            j0 = pick(free)
+            one2[j0] = [e for e in alt[j0] if e != one[j0]][0]
+        elif a >= NIN:
+            d, todo = (-1, [b]) if how < 2 else (1, [a])
+            key2[todo[0]] = (min if d < 0 else max)(key[a], key[b]) + d * pick((1, 1, 300, 1000, 3000))
+            while todo:
+                j = todo.pop()
+                for p in (pre[j] if d < 0 else nxt[j]):
+                    if d * key2[p] <= d * key2[j]:
+                        key2[p] = key2[j] + d * 0.01
+                        todo.append(p)
+        a, seq2 = again(key2, one2, at, seq, j0)
+        w = worth(a)
+        if w <= now + pick(range(1 + TOL * (NSW - k) // NSW)):
+            at, key, one, now, seq = a, key2, one2, w, seq2
+            if end(at) < end(kept):
+                kept = at
+    return kept
 
 
 def rank_program(g, core, T, topo):
@@ -138,7 +269,7 @@ def rank_program(g, core, T, topo):
         return T[n][p0:p1, a:b] if st == 1 else T[n][p0:p1, a:b:st]
 
     def regs(xs):
-        return [y for x in xs if isinstance(x, tuple) for y in (x[1:] if x[0] == "IND" else [x])]
+        return [v(y[0]) if y[0] in _WHOLE else y for x in xs if isinstance(x, tuple) for y in (x[1:] if x[0] == "IND" else [x])]
 
     def width(x):
         return 16 * (x[2][2] - x[2][1]) if x[0] == "IND" else (x[2] - x[1] + x[3] - 1) // x[3]
@@ -151,8 +282,7 @@ def rank_program(g, core, T, topo):
         me, pre, one = len(ops), {}, list(alt)[0] if len(alt) == 1 else None
         for w, xs in ((True, o), (False, i)):
             for x in xs:
-                hs = hist.setdefault(x[0], [])
-                for h in hs:
+                for h in hist.setdefault(x[0], []):
                     y = h[0]
                     if x[0] in _PS:
                         if (acc and w and h[3]) or (not w and not h[1] and one and ops[h[2]]["one"] == one):
@@ -176,7 +306,7 @@ def rank_program(g, core, T, topo):
         if xs[0][0] == "IND":
             return 60 + GA * n
         n = width(xs[0])
-        return max(64, 2 * n if two and not any(x[0] in _PS for x in xs) else (n / 2 if not two and short(o) and all(short(x) for x in xs) else n))
+        return 60 + (2 * n if two and not any(x[0] in _PS for x in xs) else (n / 2 if not two and short(o) and all(short(x) for x in xs) else n))
 
     def on_v(fn, o, xs, c):
         return step({"v": (lambda: [fn()], c)}, [o], xs)
@@ -189,11 +319,11 @@ def rank_program(g, core, T, topo):
             return lambda: g.vector.tensor_scalar(ap(o), ap(a), ap(s1), None, op0)
         return lambda: g.vector.tensor_scalar(ap(o), ap(a), ap(s1), ap(s2), op0, op1)
 
-    def plain(*xs):
-        return all(not isinstance(x, tuple) or (x[0] != "IND" or x is not xs[0]) and all(y[0] in _PS or SCRATCH[y[0]][2] in (F, B) for y in regs([x])[:1]) for x in xs)
+    def plain(o, a):
+        return o[0] != "IND" and all(y[0] in _PS or SCRATCH[y[0]][2] in (F, B) for y in (o, regs([a])[0]))
 
     def ts(o, a, s1, op0, s2=None, op1=None):
-        if plain(o, a) and not any(x[0] in _PS for x in regs([s1, s2])) and (op0, op1) in ((OP.mult, None), (OP.add, None), (OP.mult, OP.add)):
+        if plain(o, a) and (op0, op1) in ((OP.mult, None), (OP.add, None), (OP.mult, OP.add)):
             lin(o, a, None if op0 == OP.add else s1, s1 if op0 == OP.add else s2)
         else:
             on_v(f_ts(o, a, s1, op0, s2, op1), o, [a, s1, s2], cost(o, [a]))
@@ -211,7 +341,7 @@ def rank_program(g, core, T, topo):
         on_v(lambda: g.vector.memset(ap(o), c), o, [], cost(o, [o]))
 
     def c_act(a):
-        return 80 + GA * width(a) if a[0] == "IND" else max(64, width(a))
+        return 80 + GA * width(a) if a[0] == "IND" else 80 + width(a)
 
     def act(o, a, f=AF.Copy, bias=0.0, scale=1.0, acc=None):
         step({"a": (lambda: [g.scalar.activation(ap(o), ap(a), f, ap(bias), ap(scale), accum_out=ap(acc))], c_act(a))}, [o] + ([acc] if acc else []), [a, bias, scale])
@@ -225,14 +355,21 @@ def rank_program(g, core, T, topo):
         step({"v": (lambda: [fv()], cost(o, [a])), "a": (lambda: [fa()], c_act(a))}, [o], [a, scale, bias])
 
     def mm(*ms_, acc=False):
-        c = sum(max(min(64, width(x[1])), width(x[2])) / 2 for x in ms_)
+        c = sum(max(min(64, width(x[1])), width(x[2])) / 2 + TF for x in ms_)
         step({"t": (lambda: [g.tensor.matmul(ap(o), ap(l), ap(x), s0, s1) for o, l, x, s0, s1 in ms_], c)}, [x[0] for x in ms_], [y for x in ms_ for y in x[1:3]], acc)
 
+    def long(*ms_, n=8):
+        for i in range(0, len(ms_), n):
+            mm(*ms_[i:i + n])
+
     def iota(o, pat, base=0, ch=0):
-        step({"g": (lambda: [g.iota(ap(o), pat, base, ch, allow_small_or_imprecise_dtypes=True)], 160 + 2 * width(o))}, [o], [])
+        step({"g": (lambda: [g.iota(ap(o), pat, base, ch, allow_small_or_imprecise_dtypes=True)], GX * (160 + 2 * width(o)))}, [o], [], lat=GL)
+
+    def select(o, a, pat, op, c, base, ch):
+        step({"g": (lambda: [g.affine_select(ap(o), ap(a), pat, op, float(c), base, ch)], GX * (210 + 2 * width(o)))}, [o], [a], lat=GL)
 
     def fill(o, c):
-        step({"g": (lambda: [g.iota(ap(o), [[0, width(o)]], c, 0, allow_small_or_imprecise_dtypes=True)], 160 + 2 * width(o)),
+        step({"g": (lambda: [g.iota(ap(o), [[0, width(o)]], c, 0, allow_small_or_imprecise_dtypes=True)], GX * (160 + 2 * width(o))),
               "v": (lambda: [g.vector.memset(ap(o), c)], cost(o, [o]))}, [o], [])
 
     def dma(q, pairs, lat=DMA):
@@ -240,27 +377,27 @@ def rank_program(g, core, T, topo):
         step({q: (lambda: [E[q].dma_start(ap(o), ap(a)) for o, a in pairs], 60 * len(pairs))}, [o for o, a in pairs], [a for o, a in pairs], sem="d%d" % (ndma[0] - 1), lat=lat)
 
     direct, rel, off, on = plan(r, T, topo)
-    cnt = {"ls": 0}
+    cnt, seg = {"ls": 0}, order(r, T, topo)
 
     def exchange(ex, x, lands):
+        last = onward(ex, r, direct, core, T, topo)
         if ex[0] == "c":
-            ds = [(c, d) for c, q in rel for d in q]
-            tr = [RemoteDMATransfer(dst_ids=[dst(topo, c, core)], dma_engine_mask=bits(es), remote_sem=T.sem["r" + ex], src=message(ex, r, d, T)[0], dst=message(ex, r, d, T)[0])
-                  for (c, d), es in zip(ds, parts(on, len(ds)))]
+            w = [T["MV" + ex[1]][:, 16 * seg.index(q[0]):16 * seg.index(q[-1]) + 16] for c, q in rel]
+            calls = [([RemoteDMATransfer(dst_ids=[dst(topo, c, core)], dma_engine_mask=bits(es), remote_sem=T.sem["r" + ex], src=y, dst=y)
+                       for (c, q), y, es in zip(rel, w, parts(on, len(rel)))], x[0], NET - 500), (last, x[1], NET - 1500)]
         else:
-            tr = [RemoteDMATransfer(dst_ids=[dst(topo, c, core) for c, q in rel], dma_engine_mask=bits(on), remote_sem=T.sem["r" + ex], srcs=[ap(x)], dsts=[ap(x) for c in rel])]
-        tr += onward(ex, r, direct, core, T, topo)
+            calls = [([RemoteDMATransfer(dst_ids=[dst(topo, c, core) for c, q in rel], dma_engine_mask=bits(on), remote_sem=T.sem["r" + ex], srcs=[ap(x)], dsts=[ap(x) for c in rel])] + last,
+                      x, NAB + 3000 * (ex == "a0"))]
         cnt["ls"] += len(on) + len(off)
-        s = step({"g": (lambda: [g.remote_dma_fused(tr, local_sem=T.sem.ls)][1:], 400)}, [], [x], lat=NET * (2 if ex == "a0" else 1))
+        s = [step({"g": (lambda tr=tr: [g.remote_dma_fused(tr, local_sem=T.sem.ls)][1:], 400)}, [], [y], lat=lat) for tr, y, lat in calls]
         cnt["y" + ex] = sum(len(engines_to(ex, q, r, T, topo)) for q in range(N) if q != r)
-        ops[step({"n": (None, 1)}, lands, [], sem="y" + ex, lat=HOP)]["pre"].append(s)
+        ops[step({"n": (None, 1)}, lands, [], sem="y" + ex, lat=HOP)]["pre"] += s
 
     def col(i):
         return v("COL", i, i + 1)
 
-    (P_, M_, G_, G15, C13, K14, K15, K45, UHC, UCC, C16_, CN16, R15, I0, BC, B255, LT8, GE8, MH, RNC, K256, F15, H18, H19, WC0) = range(25)
+    (P_, M_, G_, G15, C13, K14, K15, UHC, UCC, C16_, CN16, R15, I0, BC, B255, LT8, GE8, MH, RNC, K256, H18, H19, N255, C256_, K7N, CP_, CN_) = range(27)
     TQ, TQB = 32, 40
-    AS = AF.Identity
 
     def nbs(t):
         return [128, 128, 32 + 16 * t]
@@ -278,24 +415,21 @@ def rank_program(g, core, T, topo):
                 w += min(c for f, c in o["alt"].values()) / k
 
     dma("s", [(v("POI"), v("post"))])
-    dma("a", [(v("ABI"), v("absorb"))], 2200)
+    dma("a", [(v("ABI", 224, 448), v("absorb", 224, 448))], 1900)
     dma("a", [(v("X0", 0, 1792), v("rec", 0, 1792))], 3800)
     dma("s", [(v("X0", 1792, 3584), v("rec", 1792, 3584))], 3800)
-    dma("s", [(v("XB", 0, 3584, 1, 16 * q, 16 * q + 14), v("rec", 0, 3584, 1, 16 * q, 16 * q + 14)) for q in range(8)], 5500)
-    dma("s", [(v("CE", 0, 288), v("cen")), (v("NEI", 0, 288), v("near"))], 5500)
+    dma("s", [(v("XB", 0, 3584, 1, 16 * q, 16 * q + 14), v("rec", 0, 3584, 1, 16 * q, 16 * q + 14)) for q in range(8)] + [(v("ABI", 0, 224), v("absorb", 0, 224))], 5500)
     ic = [v("IC", i, i + 1) for i in range(3)]
     iota(ic[0], [[0, 1]], 0, 1)
     iota(v("IOT"), [[1, 256]])
     iota(v("IOS"), [[16, 288]])
     iota(v("G1"), [[1, 8], [0, 16]])
     iota(v("G2"), [[0, 8], [1, 16]])
-    iota(v("G3"), [[0, 24], [1, 8]])
-    iota(v("G8"), [[1, 8]])
     iota(v("C15"), [[-1, 16]], 15)
     iota(v("C16k"), [[16, 16]])
+    iota(v("C16b"), [[16, 16]])
     iota(v("C256"), [[256, 24]])
     iota(v("SQ"), [[1, 8], [8, 3]])
-    iota(v("ZW"), [[1, 240]], -112)
     iota(v("IOB", 0, 16 * r + 16), [[1, 16 * r + 16]])
     iota(v("IOB", 16 * r, 128), [[1, 128 - 16 * r]], 16 * r + 16)
     iota(v("IOB", 128, 144), [[1, 16]], 16 * r)
@@ -304,22 +438,12 @@ def rank_program(g, core, T, topo):
     for i in range(3):
         tc(col(i), ic[i])
     ts(col(G15), col(G_), 16, OP.mult, 15, OP.add)
-    ts(col(C13), col(M_), 14, OP.is_lt)
-    ts(col(K14), col(M_), 14, OP.is_equal)
-    ts(col(K15), col(M_), 15, OP.is_equal)
-    ts(col(BC), col(M_), 14, OP.is_ge)
-    ts(col(B255), col(BC), 255, OP.mult)
-    ts(col(K256), col(BC), 256, OP.mult)
-    ts(col(UHC), col(K14), 256, OP.mult, col(K15), OP.add)
-    ts(col(UCC), col(K15), 1 / 256, OP.mult, col(K14), OP.add)
-    ts(col(RNC), col(K14), -16, OP.mult, col(K15), OP.add)
-    ts(col(C16_), col(C13), 16, OP.mult)
-    ts(col(CN16), col(C13), -16, OP.mult)
-    ts(col(R15), col(M_), 16, OP.mult, 15, OP.add)
-    ts(col(I0), col(M_), 0, OP.is_equal)
-    ts(col(LT8), col(M_), 8, OP.is_lt)
-    ts(col(GE8), col(M_), 8, OP.is_ge)
-    ts(col(MH), col(M_), 0.5, OP.add)
+    for c, x, op in ((C13, 14, OP.is_lt), (K14, 14, OP.is_equal), (K15, 15, OP.is_equal), (I0, 0, OP.is_equal), (GE8, 8, OP.is_ge)):
+        ts(col(c), col(M_), x, op)
+    for c, x, a, b in ((BC, C13, -1, 1), (B255, C13, -255, 255), (N255, C13, 255, -255), (K256, C13, -256, 256), (C256_, C13, 256, 0), (UHC, K14, 256, col(K15)), (UCC, K15, 1 / 256, col(K14)),
+                       (RNC, K14, -16, col(K15)), (C16_, C13, 16, 0), (CN16, C13, -16, 0), (R15, M_, 16, 15), (LT8, GE8, -1, 1), (MH, M_, 2, 1), (H18, K14, 18, 0),
+                       (H19, K14, 19, 0), (K7N, K14, -7, 0), (CP_, C13, 2048, 0), (CN_, C13, -2048, 0)):
+        ts(col(c), col(x), a, OP.mult, b, OP.add)
     ts(v("U1"), v("IOT", 0, 144), col(G15), OP.is_equal)
     for nm, c in (("UH", UHC), ("UC", UCC), ("U16", C16_), ("UN16", CN16)):
         ts(v(nm), v("U1"), col(c), OP.mult)
@@ -331,135 +455,127 @@ def rank_program(g, core, T, topo):
     for nm, c in (("BOh", 1), ("RN", col(RNC)), ("RC", col(UCC))):
         ts(v(nm), v("BO"), c, OP.mult)
     ts(v("B15"), v("U1", 0, 128), col(M_), OP.mult)
-    step({"g": (lambda: [g.affine_select(ap(v("TRI")), ap(v("BO")), [[1, 128]], OP.is_ge, 0.0, 0, -1)], 460)}, [v("TRI")], [v("BO")])
-    ts(v("RP", 0, 128), v("G1"), col(P_), OP.is_equal)
-    ts(v("RP", 128, 256), v("G1"), 8, OP.add, col(P_), OP.is_equal)
+    select(v("TRI"), v("BO"), [[1, 128]], OP.is_ge, 0, 0, -1)
     ts(v("SLOT"), v("IOS"), col(M_), OP.add)
     ts(v("I16"), v("IOT", 0, 16), col(M_), OP.is_equal)
     ts(v("I17"), v("I16"), 2 ** 17, OP.mult)
-    ts(v("W8", 40, 48), v("BO", 0, 128, 16), col(C13), OP.mult)
-    for i, w in enumerate((4096, -4096, 2048, -2048)):
-        ts(v("W8", 8 * i, 8 * i + 8), v("W8", 40, 48), w, OP.mult)
-    ts(v("W8", 32, 40), v("BO", 0, 128, 16), col(I0), OP.mult)
+    for i, (c, w) in enumerate(((CP_, 2), (CN_, 2), (CP_, 1), (CN_, 1), (I0, 1))):
+        ts(v("W8", 8 * i, 8 * i + 8), v("BO", 0, 128, 16), col(c), OP.mult, w, OP.mult)
     for i, x in enumerate(MS):
-        if x:
-            ts(col(WC0 + i), col(C13), 2048 if i % 2 else -2048, OP.mult)
-            ts(v("CO%d" % i), v("BO"), col(WC0 + i), OP.mult)
-            step({"g": (lambda i=i, x=x: [g.affine_select(ap(v("CO%d" % i)), ap(v("CO%d" % i)), [[0, 8], [-1, 16]], OP.is_gt, 0.0, x, 0)], 460)}, [v("CO%d" % i)], [v("CO%d" % i)])
-    ts(v("ZW"), v("ZW"), col(M_), OP.is_equal, -1, OP.mult)
-    ts(v("MKU"), v("G3"), col(G_), OP.is_equal)
+        if x and (i < 2 or x != MS[i - 2]):
+            ts(v("CO%d" % i), v("BO"), col(CP_ if i % 2 else CN_), OP.mult)
+            select(v("CO%d" % i), v("CO%d" % i), [[0, 8], [-1, 16]], OP.is_gt, 0, x, 0)
+    for x, c in ((v("ZER"), 0), (v("ONE"), 1), (v("DN"), -128), (v("D0"), -1), (v("MVV0"), 255), (v("FST"), -2 ** 17), (v("TAB0", 0, 896), 4096)):
+        ms(x, c)
+    ms(v("DN", 0, 384, 16), 2 ** 14)
+    ms(v("D0", 304, 305), 2000)
+    select(v("RP"), v("ONE", 0, 128), [[-1, 8], [0, 16]], OP.is_equal, 0, 0, 1)
+    select(v("MKU"), v("ONE", 0, 192), [[0, 24], [-16, 8]], OP.is_ge, 0, 0, 1)
+    select(v("MKU"), v("MKU"), [[0, 24], [16, 8]], OP.is_ge, 0, 15, -1)
+
+    for x in (v("X0", 3584, 3808), v("X1", 3696, 3808), v("L", 288, 448), v("CE", 288, 320), v("VS", 256, 272), v("VB", 288, 320), v("OHB", 288, 320), v("ZW")):
+        fill(x, 0)
+    for x in (v("F0", 288, 304), v("F1", 304, 320), v("SF0"), v("SF1"), v("D1"), v("DG")):
+        fill(x, 1)
+    fill(v("MVV1"), 255)
+    ms(v("DG", 0, 384, 16), -2 ** 25)
+    ms(v("D1", 7, 128, 8), 0)
+    ts(v("ZW", 112, 128), v("I16"), -1, OP.mult)
     ts(v("L8f"), v("SQ", 0, 24, 2), col(LT8), OP.mult)
     ts(v("t24", 0, 12), v("SQ", 1, 24, 2), col(GE8), OP.mult)
     tt(v("L8f"), v("L8f"), v("t24", 0, 12), OP.add)
     tc(v("L8u"), v("L8f"))
-    ts(v("K86f"), v("G8"), 0, OP.mult, col(M_), OP.add)
-    tc(v("K7"), v("K86f"))
-    ts(v("K86"), v("K86f"), 8, OP.mult, 6, OP.add)
-    ts(v("COL", TQ, TQ + 8), v("C16k", 0, 8), 16, OP.add, col(M_), OP.add)
+    ts(v("K7"), v("IOT", 0, 8), 0, OP.mult, col(M_), OP.add)
+    ts(v("K86"), v("K7"), 8, OP.mult, 6, OP.add)
+    for i, d in enumerate(seg):
+        fill(v("PRa", 16 * i, 16 * i + 16), 16 * d + 16)
+    ts(v("COL", TQ, TQ + 8), v("PRa", 0, 128, 16), col(M_), OP.add)
+    ts(v("PRa"), v("PRa"), 16 * r + 16, OP.is_le, 32 - r, OP.add)
     ts(v("COL", TQB, TQB + 8), v("COL", TQ, TQ + 8), -1000, OP.mult)
     ts(v("DGO"), v("C16k"), col(M_), OP.add, 3808, OP.add)
-    ts(v("DQ"), v("COL", TQ, TQ + 8), 304, OP.add)
+    ts(v("DQ"), v("COL", TQ, TQ + 8), 304 - 287, OP.add)
     ts(v("DM"), v("COL", TQ, TQ + 8), 3808 - 1904 - 16, OP.add)
-    for nm, c in (("ZER", 0), ("FST", 0), ("L", 0), ("D0", -1), ("D1", 1), ("DN", -128), ("DG", 1), ("CNG", -2 ** 23), ("MVV0", 255), ("MVV1", 255)):
-        fill(v(nm), c)
-    ms(v("FST", 0, 128, 1, 0, 1), 1)
-    ms(v("DN", 0, 384, 16), 2 ** 14)
-    ms(v("DG", 0, 384, 16), -2 ** 25)
-    ms(v("D1", 7, 128, 8), 0)
-    for x in (v("X0", 3584, 3808), v("X1", 3696, 3808), v("PIf", 288, 320), v("CPf", 288, 320), v("NEI", 288, 320), v("CE", 288, 320), v("VS", 256, 272), v("VB", 288, 320),
-              v("PIm", 288, 320), v("PN", 256, 384)):
-        ms(x, 0)
-    ms(v("LOS", 288, 320), 99)
-    ts(col(F15), col(M_), -1, OP.mult, 15, OP.add)
-    ms(v("F0", 288, 304), 1)
-    ms(v("F1", 304, 320), 1)
+    for x in (v("PIf", 288, 320), v("CPf", 288, 320), v("NEI", 288, 320), v("PIm", 288, 320)):
+        fill(x, 0)
+    ms(v("PN", 256, 384), 0)
+    tc(v("K16"), v("IOT", 0, 16))
+    ts(v("PRa"), v("PRa"), col(K14), OP.mult, col(C256_), OP.add)
+    ts(v("JK", 0, 128), v("G2"), col(K15), OP.mult)
+    tt(v("PR0"), v("PRa"), v("JK", 0, 128), OP.add)
+    ts(v("PR1"), v("PR0"), col(K7N), OP.add)
     for t in range(2):
-        for a, b in chunks(0, 2688, 672):
-            fill(v("TAB%d" % t, a, b), 4096)
-        ts(col(H18 + t), col(K14), 18 + t, OP.mult)
         lin(v("HV%d" % t), v("IOT"), col(K15), col(H18 + t))
         iota(v("ZC%d" % t), [[1, 112]], 3584 + 112 * t - 4096)
-        x = v("PR%d" % t)
-        ts(x, v("G1"), r, OP.is_gt, -1, OP.mult)
-        ts(x, x, 33 - 7 * t - r, OP.add, col(K14), OP.mult)
-        ts(v("JK", 0, 128), v("G2"), col(K15), OP.mult)
-        tt(x, x, v("JK", 0, 128), OP.add)
-        ts(x, x, col(K256), OP.subtract, 256, OP.add)
-        ms(v("PR%d" % t, 16 * r, 16 * r + 16), 2 ** 20)
+        fill(v("PR%d" % t, 112, 128), 2 ** 20)
 
     def by_row(bank, u, x, a, b):
         mm(*[(v(bank, a, b), v(u, 15 - m, 143 - m), v(x, 16 * a + m, 16 * b, 16), m == 0, m == 15) for m in range(16)], acc=True)
 
-    def first_live(a, b):
-        mm((v("PB", a, b), v("TRI"), v("L", a, b), True, True))
-        act(v("Z", a, b), v("PB", a, b), AF.Relu, 1.0, -1.0)
-        mm((v("PB", a, b), v("BO"), v("Z", a, b), True, True))
-        lin(v("MA", a, b), v("PB", a, b))
-
     def full(t, a, b):
         mm((v("PC", a, b), v("BO"), v("L", a, b), True, True))
-        ts(v("F%d" % t, a, b), v("PC", a, b), 12, OP.is_ge)
+        act(v("F%d" % t, a, b), v("PC", a, b), AF.Sign, -11.5)
 
-    def count(t, a, b, j):
-        scan(v("INC", a, b), v("F%d" % t, a, b), v("ZER", a, b), v("INC", a - 1, a) if a else 0.0, OP.add, OP.add)
+    def count(t, a, b, j, one):
+        scan(v("INC", a, b), v("F%d" % t, a, b), v(one, a, b), v("INC", a - 1, a) if a else 0.0, OP.add, OP.add)
         act(v("JK", a, b), v("INC", a, b), AF.Sign, col(MH), -1.0, v("acc", j, j + 1))
 
     def numbers(t, x, pre):
         P, t1, t2 = 288 + 16 * t, v("t1", 0, 1), v("t1", 1, 2)
-        ts(t1, x, 0.5, OP.mult, pre, OP.add)
-        ts(t2, t1, P, OP.is_ge, 2560 + 16 * r - 320 * r - P, OP.mult)
-        ts(v("NO%d" % t, 0, 1), t1, t2, OP.add, 320 * r, OP.add)
-        ts(v("pk8"), v("ZER", 0, 8), t1, OP.add)
+        ts(v("pre", 0, 8), v("IOT", 0, 8), 0.0, OP.mult, pre, OP.add)
+        ts(v("pre", 8, 9), v("pre", 0, 1), -1, OP.mult, 2 * P, OP.add)
+        ts(v("pre", 9, 10), v("pre", 0, 1), 0.5, OP.mult, 320 * r, OP.add)
+        ts(v("pk8"), v("pre", 0, 8), x, OP.add, 0.5, OP.mult)
+        ts(t1, x, 0.5, OP.mult, v("pre", 9, 10), OP.add)
+        ts(t2, x, v("pre", 8, 9), OP.is_ge, 2560 + 16 * r - 320 * r - P, OP.mult)
+        ts(v("NO%d" % t, 0, 1), t1, t2, OP.add)
         exchange("a%d" % t, v("NO%d" % t, 0, 1), [v("NL%d" % t, 0, 7)])
 
+    def apart(win, lst, x, out, bank):
+        lin(v(x), ind(v(win), v(lst)))
+        mm((bank, v("NID"), v("VS", 0, 256), True, False))
+        mm((bank, v("ID"), v(x), False, True))
+        act(v(out), bank, AF.Abs)
+
     def split(t):
-        P, pk1, bt = 288 + 16 * t, v("pk8", 0, 1), v("BT%d" % t, 16 * r, 16 * r + 16)
+        P, pk1, bt, pc = 288 + 16 * t, v("pk8", 0, 1), v("BT%d" % t, 16 * r, 16 * r + 16), v("PC", 0, 16)
         tc(v("SPu"), ind(v("PIf"), pk1))
         if t == 0:
             lin(v("VS", 0, 256), ind(v("X1", 0, 3584), v("SPu")))
-            lin(v("VSc"), ind(v("X1", 0, 3584), v("SPu")))
         else:
             tc(v("CSu"), ind(v("CPf"), pk1))
             lin(v("VSa"), ind(v("X1"), v("SPu")))
             tt(v("VS", 0, 256), ind(v("X1"), v("CSu")), v("VSa"), OP.max)
-            tc(v("VSc"), v("VS", 0, 256))
-        tt(v("LAf"), ind(v("MA", 0, P + 16), pk1), v("C16k"), OP.add)
-        tc(v("LAu"), v("LAf"))
+        tc(v("LS"), ind(v("L", 0, 320), pk1))
+        mm((pc, v("TRI"), v("LS"), True, True))
+        act(v("Z"), pc, AF.Relu, 1.0, -1.0)
+        mm((pc, v("ID"), v("C16b"), True, False), (pc, v("BO"), v("Z"), False, True))
+        tc(v("LAu"), pc)
         tt(v("LSE"), ind(v("L", 0, 320), v("pk8")), v("BO"), OP.mult)
-        tt(v("AD"), ind(v("VS"), v("LAu")), v("VSc"), OP.subtract)
-        act(v("AA"), v("AD"), AF.Abs)
-        mm((v("PC", 0, 16), v("ID"), v("C15"), True, False), (v("PC", 0, 16), v("LSE"), v("I17"), False, False))
-        mm(*[(v("PC", 0, 16), v("U16", 15 - k, 143 - k), v("AA", 16 * k, 16 * k + 16), False, k == 15) for k in range(16)])
-        on_v(lambda: g.vector.tensor_reduce(ap(v("kx")), ap(v("PC", 0, 16)), AxisListType.X, OP.max), v("kx"), [v("PC", 0, 16)], 64)
+        apart("VS", "LAu", "AD", "AA", v("PX", 0, 256))
+        mm((pc, v("ID"), v("C15"), True, False), (pc, v("LSE"), v("I17"), False, False))
+        mm(*[(pc, v("U16", 15 - k, 143 - k), v("AA", 16 * k, 16 * k + 16), False, k == 15) for k in range(16)])
+        on_v(lambda: g.vector.tensor_reduce(ap(v("kx")), ap(pc), AxisListType.X, OP.max), v("kx"), [pc], 64)
         ts(v("kr"), v("kx"), 15, OP.bitwise_and)
         ts(v("obu", 0, 1), v("kr"), -1, OP.mult, col(R15), OP.add)
         tc(bt, ind(v("VS"), v("obu", 0, 1)))
-        exchange("b%d" % t, bt, [v("BT%d" % t, 0, 16 * r), v("BT%d" % t, 16 * r + 16, 128)])
-        tc(v("LO", 0, P), v("L", 0, P))
-        tc(ind(v("LO", 0, P + 16), pk1), v("ZER", 0, 16))
+        exchange("b%d" % t, bt, [v("BT%d" % t)])
+        tc(ind(v("SF%d" % t), pk1), v("ZER", 0, 16))
 
     def parted(t):
-        pk1 = v("pk8", 0, 1)
-        ts(v("t1", 2, 3), v("kr"), -1, OP.mult, col(R15), OP.add)
-        ts(v("RB"), v("I16"), v("t1", 2, 3), OP.mult)
-        pb = v("PB", 0, 16)
-        mm((pb, v("BO"), v("RB"), True, True))
-        tc(v("LBu"), pb)
-        tt(v("BD"), ind(v("VS"), v("LBu")), v("VSc"), OP.subtract)
-        act(v("BA"), v("BD"), AF.Abs)
-        tc(v("LS"), ind(v("L", 0, 320), pk1))
+        pk1, pb = v("pk8", 0, 1), v("PB", 0, 16)
+        tc(v("BV"), ind(v("VS"), v("obu", 0, 1)))
+        apart("BV", "K16", "BD", "BA", v("PB", 0, 256))
         tc(v("SPf"), ind(v("PIf"), pk1))
         for u, x in (("U16", "AA"), ("UN16", "BA")):
-            mm(*([(pb, v("IDL"), v("LS"), True, False)][:x == "AA"] + [(pb, v(u, 15 - m, 143 - m), v(x, m, 256, 16), False, x == "BA" and m == 15) for m in range(16)]))
+            long(*([(pb, v("IDL"), v("LS"), True, False)][:x == "AA"] + [(pb, v(u, 15 - m, 143 - m), v(x, m, 256, 16), False, x == "BA" and m == 15) for m in range(16)]))
         ts(v("GS"), pb, 2 ** 23, OP.is_gt)
-        ts(v("NG"), pb, 2 ** 23, OP.is_le)
-        mm((pb, v("TRI"), v("NG"), True, True))
-        ts(v("g1"), pb, 1, OP.is_equal)
-        tt(v("RO"), v("g1"), v("NG"), OP.mult)
-        mm((pb, v("B15"), v("RO"), True, True))
-        tt(v("FV"), pb, v("HV%d" % t, 0, 256, 16), OP.add)
-        tc(v("MVV%d" % t, 16 * r, 16 * r + 16), v("FV"))
-        ts(v("FD"), ind(v("FV"), v("K7", 0, 7)), col(B255), OP.subtract)
+        ts(v("NG"), v("GS"), -1, OP.mult, 1, OP.add)
+        mm((pb, v("IDL"), v("GS"), True, False), (pb, v("TRI"), v("NG"), False, True))
+        ts(v("RO"), pb, 1, OP.is_equal)
+        mm((pb, v("ID"), v("HV%d" % t, 0, 256, 16), True, False), (pb, v("B15"), v("RO"), False, True))
+        tc(v("FV"), pb)
+        tc(v("MVV%d" % t, 112, 128), v("FV"))
+        lin(v("FD"), ind(v("FV"), v("K7", 0, 7)), None, col(N255))
         ts(v("g1"), v("NG"), 8192, OP.mult)
         tt(v("g1"), v("g1"), v("SPf"), OP.add)
         tt(v("GLf"), v("g1"), v("DGO"), OP.min)
@@ -471,30 +587,29 @@ def rank_program(g, core, T, topo):
 
     def centres():
         pk1 = v("pk8", 0, 1)
-        tt(v("RB"), v("AD", 0, 256, 16), v("VS", 0, 256, 16), OP.add)
-        tc(ind(v("CE"), pk1), v("RB"))
+        tc(ind(v("CE"), pk1), v("AD", 0, 256, 16))
         tc(v("CE", 288, 304), v("BT0", 16 * r, 16 * r + 16))
         tc(v("NU", 288, 304), ind(v("NEI"), pk1))
         tc(v("CSf"), ind(v("CPf"), pk1))
 
-    def by_posting(bank, x, m, w, t, acc_=True):
-        nb = nbs(t)
-        return [(v(bank, 128 * b + m, 128 * b + 128, 16, 0, nb[b]), x(b), v("W8", 8 * w, 8 * w + 8), not acc_, not acc_) for b in range(3)]
+    def by_posting(xs, w, t):
+        mm(*[(v("PG", 128 * b + m, 128 * b + 128, 16, 0, nbs(t)[b]), x, v("W8", 8 * w, 8 * w + 8), False, False) for m, b, x in xs], acc=True)
 
-    def listed(x, bank, t, first):
+    def listed(x, first):
         tt(v("Y"), ind(v(x), v("L8u")), v("MKU"), OP.mult)
-        mm(*(first + [(v(bank, 0, 24), v("ZW", 112 - 16 * q, 240 - 16 * q), v("Y", 24 * q, 24 * q + 24), q == 0 and not first, q == 7) for q in range(8)]))
+        for o, x in ([(24, first)] if first else []) + [(0, [])]:
+            mm(*(x + [(v("PC", o, o + 24), v("ZW", 112 - 16 * q, 240 - 16 * q), v("Y", 24 * q, 24 * q + 24), q == 0 and not x, q == 7) for q in range(8)]))
 
     def near(t):
         P, nb, tab = 288 + 16 * t, nbs(t), v("TAB%d" % t)
         tc(ind(tab, v("NO%d" % t, 0, 1)), v("IOB", 128, 144))
         tc(ind(tab, v("NL%d" % t, 0, 7)), v("IOB", 0, 112))
-        phase(2, lambda a, b: lin(v("TN", 16 * a, 16 * b), ind(tab, v("NU", a, b))), chunks(0, P))
+        phase(2, lambda a, b: lin(v("TN", 16 * a, 16 * b), ind(tab, v("NU", a, b))), chunks(0, 256) + chunks(256, P, 16))
         for b in range(3):
             mm(*[(v("PN", 128 * b + m, 128 * b + 128, 16, 0, nb[b]), v("TN", 2048 * b + m, 2048 * b + 16 * nb[b], 16), v("W8", 32, 40), True, True) for m in range(16)], acc=True)
         scan(v("kn"), v("DN"), v("PN", 0, 384), 0.0, OP.add, OP.min)
         ts(v("Ti"), v("kn", 15, 384, 16), 127, OP.bitwise_and)
-        listed("Ti", "PC", t, [])
+        listed("Ti", [])
         ts(v("TLu"), v("PC", 0, 24), -1, OP.mult)
         lin(v("BQ", 0, P), ind(v("BT%d" % t), v("TLu", 0, P // 16)))
         ts(v("hs"), v("kn", 15, 384, 16), 128, OP.is_lt)
@@ -503,22 +618,36 @@ def rank_program(g, core, T, topo):
 
     def gains(t, c, out, sign):
         P, nb, V, k = 288 + 16 * t, nbs(t), "VW"[t], MS[2 * t + sign]
+        first = [len(ops)][:k]
         if k:
             mm((v("PX", 0, P), v("ID"), v(c, 0, P), True, True))
-            mm(*[(v("PG", 128 * b, 128 * b + 128, 1, 0, nb[b]), v(c, 128 * b, 128 * b + nb[b]), v("CO%d" % (2 * t + sign)), False, False) for b in range(3)], acc=True)
+            mm(*[(v("PG", 128 * b, 128 * b + 128, 1, 0, nb[b]), v(c, 128 * b, 128 * b + nb[b]), v("CO%d" % (sign + 2 * (k != MS[sign]))), False, False) for b in range(3)], acc=True)
 
         def row(m):
-            o, x = v(out, 304 * m, 304 * m + P), v(V, m, 16 * P, 16)
-            if m < k:
-                tt(o, x, v("PX", 0, P), OP.max)
-                if m >= MS[2 * t + 1 - sign]:
-                    mm(*by_posting("PG", lambda b: v(V, 2048 * b + m, 2048 * b + 16 * nb[b], 16), m, 3 - sign, t), acc=True)
-            else:
-                pm = v(("PM0", "PM1", "PA", "PN")[m % (3 + sign)], 0, P)
-                mm((pm, v("ID"), x, True, False), (pm, v("NID"), v(c, 0, P), False, True))
-                act(o, pm, AF.Abs)
-            mm(*by_posting("PG", lambda b: v(out, 304 * m + 128 * b, 304 * m + 128 * b + nb[b]), m, sign + (0 if m < k else 2), t), acc=True)
-        phase(2 if k else 1, row, [(m,) for m in sorted(range(16), key=lambda m: m / k if m < k else (m - k) / (16 - k))])
+            tt(v(out, 304 * m, 304 * m + P), v(V, m, 16 * P, 16), v("PX", 0, P), OP.max)
+            if m >= MS[2 * t + 1 - sign]:
+                by_posting([(m, b, v(V, 2048 * b + m, 2048 * b + 16 * nb[b], 16)) for b in range(3)], 3 - sign, t)
+            by_posting([(m, b, v(out, 304 * m + 128 * b, 304 * m + 128 * b + nb[b])) for b in range(3)], sign, t)
+
+        def rows(i, b, ms_):
+            n, bank, o = nb[b], ("PM0", "PM1", "PA", "PN")[i % (3 + sign)], 2048 * b + nb[b] * ms_[0]
+            mm(*[(v(bank, n * j, n * j + n), v("ID"), v(V, 2048 * b + m, 2048 * b + 16 * n, 16), j == 0, False) for j, m in enumerate(ms_)])
+            mm(*[(v(bank, n * j, n * j + n), v("NID"), v(c, 128 * b, 128 * b + n), False, m == ms_[-1]) for j, m in enumerate(ms_)])
+            ops[-1]["pre"] += first
+            act(v(out + "2", o, o + n * len(ms_)), v(bank, 0, n * len(ms_)), AF.Abs)
+            by_posting([(m, b, v(out + "2", o + n * j, o + n * j + n)) for j, m in enumerate(ms_)], sign + 2, t)
+        phase(1, row, [(m,) for m in range(k)])
+        def arow(m):
+            o, x, pm = v(out, 304 * m, 304 * m + P), v(V, m, 16 * P, 16), v(("PM0", "PM1", "PA", "PN")[m % (3 + sign)], 0, P)
+            mm((pm, v("ID"), x, True, False))
+            mm((pm, v("NID"), v(c, 0, P), False, True))
+            ops[-1]["pre"] += first
+            act(o, pm, AF.Abs)
+            by_posting([(m, b, v(out, 304 * m + 128 * b, 304 * m + 128 * b + nb[b])) for b in range(3)], sign + 2, t)
+        if QUAD[2 * t + sign]:
+            phase(1, rows, [(i, b, range(x, y)) for i, (b, x, y) in enumerate((b, x, y) for b in range(3) for x, y in chunks(k, 16, 512 // nb[b]))])
+        else:
+            phase(1, arow, [(m,) for m in range(k, 16)])
 
     def absorb(out, win, lst, x, n, k):
         def part(a, b):
@@ -530,80 +659,80 @@ def rank_program(g, core, T, topo):
                 tt(o, pm, y, OP.max)
             else:
                 tt(o, w, y, OP.max)
-        phase(1, part, chunks(0, n, 32))
+        cut = [a for a in range(0, n, 32) if a // 32 in k or a // 32 - 1 in k or a % CH == 0] + [n]
+        phase(1, part, zip(cut, cut[1:]))
 
     def keys_open(t):
         nb = nbs(t)
-        mm((v("PG", 0, 384), v("FST"), v("CNG"), True, False))
-        mm(*[(v("PG", 128 * b, 128 * b + 128, 1, 0, nb[b]), v("LO", 128 * b, 128 * b + nb[b]), v("IDL"), False, False) for b in range(3)], acc=True)
+        mm((v("PG", 0, 384), v("FST"), v("ONE"), True, False))
+        for x in ("L", "SF%d" % t):
+            mm(*[(v("PG", 128 * b, 128 * b + 128, 1, 0, nb[b]), v(x, 128 * b, 128 * b + nb[b]), v("IDL"), False, False) for b in range(3)], acc=True)
 
-    def turn(x, out, banks, t):
+    def turn(x, pa, out, banks, t):
         P, nb = 288 + 16 * t, nbs(t)
-        mm(*[(v("PA", 128 * b, 128 * b + nb[b], 1, 0, 8), v(x, 8 * b, 8 * b + 8), v("ID", 0, nb[b]), True, True) for b in range(3)])
-        act(v(out, 0, P, 1, 0, 8), v("PA", 0, P, 1, 0, 8))
+        mm(*[(v(pa, 128 * b, 128 * b + nb[b], 1, 0, 8), v(x, 8 * b, 8 * b + 8), v("ID", 0, nb[b]), True, True) for b in range(3)])
+        lin(v(out, 0, P, 1, 0, 8), v(pa, 0, P, 1, 0, 8))
         for bank in banks:
             mm((v(bank, 0, P), v("RP", 0, 128, 1, 0, 8), v(out, 0, P, 1, 0, 8), True, True))
 
     def pick(t):
-        P, last = 288 + 16 * t, v("SC", 287 + 16 * t, 2432, 304)
+        P = 288 + 16 * t
         mm((v("PG", 0, 16), v("FST"), v("ZER", 0, 16), False, True))
         scan(v("ki"), v("DG"), v("PG", 0, 384), 0.0, OP.add, OP.max)
         tt(v("X24"), v("ki", 15, 384, 16), v("TH"), OP.min)
-        turn("X24", "T8", ("PM0", "PM1"), t)
+        turn("X24", "PA", "T8", ("PM0", "PM1"), t)
         ts(v("lo"), v("ki", 15, 384, 16), 15, OP.bitwise_and)
-        listed("lo", "PC", t, [(v("PC", 0, 24), v("ID"), v("C256"), True, False)])
-        ts(v("VLu"), v("PC", 0, 24), col(R15), OP.add)
+        listed("lo", [(v("PC", 24, 48), v("ID"), v("C256"), True, False)])
+        ts(v("VLu"), v("PC", 24, 48), col(R15), OP.add)
+        ts(v("MLu"), v("PC", 0, 24), 15, OP.add)
         lin(v("VB", 0, P), ind(v("VW"[t], 0, 16 * P), v("VLu", 0, P // 16)))
-        tc(v("TS", 0, P), v("PM1", 0, P))
         for q in range(8):
-            z = v("ZQ", 304 * q, 304 * q + P)
-            if q < NACT:
+            z = v("ZQ", P * q, P * q + P)
+            if q in NACT:
                 act(z, v("PM0", 0, P), AF.Abs, col(TQB + q), 1000.0)
             else:
-                ts(z, v("TS", 0, P), col(TQ + q), OP.not_equal, 1000, OP.mult)
-            scan(v("SC", 304 * q, 304 * q + P), v("D0", 0, P), z, 1000.0, OP.add, OP.min)
-        ts(v("QTu"), last, P - 1, OP.add, 304, OP.min)
-        tt(v("MV%d" % t), ind(v("VB"), v("QTu")), v("PR%d" % t), OP.min)
-        exchange("c%d" % t, v("MV%d" % t), [v("XA") if t else v("X1", 3584, 3696)])
+                ts(z, v("PM1", 0, P), col(TQ + q), OP.not_equal, 1000, OP.mult)
+        for a, b in SCANS:
+            scan(v("SC", P * a, P * b), v("D0", 304 - P, 304 + P), v("ZQ", P * a, P * b), 1000.0, OP.add, OP.min)
+        h = N - 1 - len(direct)
+        for a, b in ((0, h), (h, N)):
+            ts(v("QTu", a, b), v("SC", P * a + P - 1, P * b, P), P - 1, OP.add, 304, OP.min)
+            tt(v("MV%d" % t, 16 * a, 16 * b), ind(v("VB"), v("QTu", a, b)), v("PR%d" % t, 16 * a, 16 * b), OP.min)
+        exchange("c%d" % t, [v("MV%d" % t, 0, 16 * h), v("MV%d" % t, 16 * h, 128)], [v("XA") if t else v("X1", 3584, 3696)])
 
     def own(t):
-        P, last = 288 + 16 * t, v("SC", 287 + 16 * t, 2432, 304)
-        tc(v("L24"), v("lo"))
-        turn("L24", "L8", ("PX",), t)
-        act(v("LOS", 0, P), v("PX", 0, P))
-        ts(v("OHm"), ind(v("LOS"), v("QTu")), col(F15), OP.is_equal)
+        P = 288 + 16 * t
+        last = v("SC", P - 1, 8 * P, P)
+        tc(v("OHB", 0, P), ind(v("I16"), v("MLu", 0, P // 16)))
+        tc(v("OHm"), ind(v("OHB"), v("QTu")))
         if t == 0:
-            ts(v("QLf"), last, P - 1, OP.add)
-            tt(v("QLf"), v("QLf"), v("DQ"), OP.min)
-            tc(v("QLu"), v("QLf"))
+            tt(v("QLf"), last, v("DQ"), OP.min)
+            ts(v("QLu"), v("QLf"), P - 1, OP.add)
             tt(v("LN"), ind(v("L", 0, 320), v("QTu")), v("OHm"), OP.subtract)
             tc(ind(v("L"), v("QLu")), v("LN"))
-        lin(v("PIm", 0, P), v("PIf", 0, P), None, -1904.0)
+        lin(v("PIm", 288 * t, P), v("PIf", 288 * t, P), None, -1904.0)
         tt(v("PGh"), ind(v("PIm"), v("QTu")), v("OHm"), OP.mult)
         ts(v("t24", 0, 8), last, 0, OP.is_gt)
         tt(v("DMh"), v("t24", 0, 8), v("DM"), OP.mult)
         mm(*([(v("PB", 0, 8), v("IDh"), v("DMh"), True, False)] + [(v("PB", 0, 8), v("UF", 15 - k, 143 - k), v("PGh", k, 128, 16), False, k == 15) for k in range(16)]))
         ts(v("MVL"), v("PB", 0, 8), 1904, OP.add)
         tc(ind(v("X0"), v("MVL")), v("MVV%d" % t))
-        mm((v("PB", 0, 16), v("RC"), v("MV%d" % t, 16 * r, 16 * r + 16), True, True), (v("PB", 16, 32), v("BOh"), v("PGh", 16 * r, 16 * r + 16), True, True))
-        ts(v("exo"), v("PB", 0, 16), 0, OP.is_gt)
-        ts(v("D1", 6, 128, 8), v("PB", 0, 16), 0, OP.is_le)
-        tt(v("ROo"), v("RO"), v("exo"), OP.mult)
-        ts(v("g1"), v("SPf"), -1904, OP.add)
-        tt(v("g1"), v("PB", 16, 32), v("g1"), OP.subtract)
-        tt(v("g1"), v("g1"), v("ROo"), OP.mult)
-        tt(v("SPo"), v("g1"), v("SPf"), OP.add)
+        mm((v("PB", 0, 16), v("RC"), v("MV%d" % t, 112, 128), True, True), (v("PB", 16, 32), v("BOh"), v("PGh", 112, 128), True, True))
+        a = 16 * t
+        act(v("exo"), v("PB", 0, 16), AF.Sign)
         if t == 0:
-            ts(v("g2"), v("PB", 0, 16), -257, OP.add, 0, OP.max)
-            tt(v("g2"), v("g2"), v("CSf"), OP.subtract)
-            tt(v("g2"), v("g2"), v("RO"), OP.mult)
-            tt(v("CSo"), v("g2"), v("CSf"), OP.add)
-            tt(v("RB"), v("GS"), v("ROo"), OP.add)
-            mm((v("PB", 0, 16), v("BO"), v("RB"), True, True))
-            ts(v("T3"), v("PB", 0, 16), -11, OP.add, 8192, OP.mult)
-            tt(v("g3"), v("GS"), v("RO"), OP.add)
-            ts(v("g3"), v("g3"), -1, OP.add, 8192, OP.mult)
-            tt(v("T2"), v("g3"), v("RB"), OP.add)
+            act(v("E32", 0, 16), v("PB", 0, 16), AF.Relu, -257.0)
+        act(v("E32", 16, 32), v("PB", 16, 32), AF.Identity, 1904.0)
+        ts(v("D1", 6, 128, 8), v("exo"), -1, OP.mult, 1, OP.add)
+        tt(v("ROo"), v("RO"), v("exo"), OP.mult)
+        tt(v("E32", a, 32), v("E32", a, 32), v("CSf", a, 32), OP.subtract)
+        tt(v("E32", a, 32), v("E32", a, 32), v("RO", a, 32), OP.mult)
+        tt(v("CSo", a, 32), v("E32", a, 32), v("CSf", a, 32), OP.add)
+        if t == 0:
+            mm(*[(v("PB", 0, 16), v("BO"), v(x), x == "GS", x == "ROo") for x in ("GS", "ROo")],
+               *[(v("PB", 16, 32), v(w), v(x), i == 0, i == 3) for i, (w, x) in enumerate((("IDL", "GS"), ("IDL", "RO"), ("ID", "GS"), ("ID", "ROo")))])
+            act(v("T3"), v("PB", 0, 16), AF.Identity, -11.0 * 8192, 8192.0)
+            act(v("T2"), v("PB", 16, 32), AF.Identity, -2.0 ** 23)
         ms(v("PX", 0, 128), 0)
 
     def land(t):
@@ -625,9 +754,8 @@ def rank_program(g, core, T, topo):
     tc(v("PU", 0, 288), v("POI"))
     tc(v("PIf", 0, 288), v("POI"))
     tc(v("ABU"), v("ABI", 0, 224))
-    tc(v("NU", 0, 288), v("NEI", 0, 288))
-    phase(2, lambda a, b: lin(v("H", 16 * a, 16 * b), ind(v("X0", 0, 3584), v("PU", a, b))), chunks(0, 288, 24))
-    for a, b in chunks(0, 288, 72):
+    phase(2, lambda a, b: lin(v("H", 16 * a, 16 * b), ind(v("X0", 0, 3584), v("PU", a, b))), chunks(0, 288, CHH))
+    for a, b in ((0, 144), (144, 216), (216, 288)):
         by_row("PA", "UH", "H", a, b)
     tt(v("L", 0, 288), v("PA", 0, 288), v("SLOT"), OP.is_equal)
     ts(v("AI"), v("ABI", 224, 448), 8, OP.arith_shift_right)
@@ -636,38 +764,41 @@ def rank_program(g, core, T, topo):
     ts(v("A2", 224, 448), v("AJ"), 1, OP.add, 256, OP.mult)
     mm(*[(v("PB", 64 * q + 16 * j, 64 * q + 16 * j + 16, 1, 0, 112), v("A2", j, 448, 4), v("ID", 16 * q, 16 * q + 16), True, True) for q in range(8) for j in range(4)])
     lin(v("S3", 0, 512, 1, 0, 112), v("PB", 0, 512, 1, 0, 112))
-    dma("s", [(v("XB", 0, 3584, 1, 16 * q + 14, 16 * q + 16), v("S3", 64 * q, 64 * q + 64, 1, 0, 112)) for q in range(8)])
+    dma("s", [(v("XB", 0, 3584, 1, 16 * q + 14, 16 * q + 16), v("S3", 64 * q, 64 * q + 64, 1, 0, 112)) for q in range(8)], DS3)
+    i = len(ops) - 2
+    for x in ([(v("CE", 0, 288), v("cen")), (v("NEI", 0, 288), v("near"))], [(v("TAB0", a, b), v("TAB0", 0, 896)) for a, b in chunks(896, 2688, 896)],
+              [(v("TAB1", a, b), v("TAB0", 0, 896)) for a, b in chunks(0, 2688, 896)]):
+        dma("s", x, 4000)
+        ops[-1]["pre"].append(i)
+    tc(v("NU", 0, 288), v("NEI", 0, 288))
     full(0, 0, 288)
-    count(0, 0, 304, 0)
-    numbers(0, v("acc", 0, 1), 152.0)
-    first_live(0, 304)
+    count(0, 0, 304, 0, "ONE")
+    numbers(0, v("acc", 0, 1), 304.0)
     absorb("X1", v("X0", 0, 3808), "ABU", "XB", 224, KA[0])
     split(0)
     phase(2, lambda a, b: lin(v("V", 16 * a, 16 * b), ind(v("X1", 0, 3584), v("PU", a, b))), chunks(0, 288))
-    for a, b in chunks(0, 288, 96):
-        by_row("PB", "UC", "V", a, b)
-    ts(v("CPf", 0, 288), v("PB", 0, 288), -257, OP.add)
-    tc(v("CU", 0, 288), v("CPf", 0, 288))
-    parted(0)
     keys_open(0)
+    parted(0)
     gains(0, "CE", "MC", 0)
     near(0)
     gains(0, "BQ", "MB", 1)
+    long(*[(v("PN", 0, 288), v("UC", 15 - m, 143 - m), v("V", m, 4608, 16), m == 0, m == 15) for m in range(16)], n=2)
+    ts(v("CPf", 0, 288), v("PN", 0, 288), -257, OP.add)
+    tc(v("CU", 0, 288), v("CPf", 0, 288))
     centres()
     pick(0)
     own(0)
     full(1, 0, 288)
-    count(1, 0, 288, 1)
-    ts(v("acc", 2, 3), v("acc", 1, 2), 0.5, OP.mult, 160, OP.add)
-    first_live(0, 288)
+    count(1, 0, 288, 1, "ONE")
+    ts(v("acc", 2, 3), v("acc", 1, 2), 320, OP.add)
     land(0)
     ts(v("X0", 3584, 3696), v("WN"), col(B255), OP.add)
-    count(1, 288, 320, 3)
+    count(1, 288, 320, 3, "F1")
     numbers(1, v("acc", 3, 4), v("acc", 2, 3))
-    first_live(288, 320)
     tc(v("PU", 288, 304), v("PIf", 288, 304))
     tc(v("CU", 288, 304), v("CPf", 288, 304))
     dma("s", [(v("ypost", 0, 304), v("PIf", 0, 304))])
+    dma("s", [(v("ya", 0, 112), v("X1", 3584, 3696))])
     split(1)
     parted(1)
     lin(v("V", 4608, 4864), ind(v("X1"), v("PU", 288, 304)), None, col(K256))
@@ -680,51 +811,17 @@ def rank_program(g, core, T, topo):
     own(1)
     dma("s", [(v("yh", 0, 3584, 1, 0, 16, 2), v("X0", 0, 3584, 1, 14, 128, 16))])
     dma("a", [(v("yh", 0, 3584, 1, 1, 16, 2), v("X0", 0, 3584, 1, 15, 128, 16))])
-    ts(v("YB"), v("X0", 3584, 3696), col(BC), OP.mult)
-    ts(v("XM"), v("X1", 3584, 3696), col(C13), OP.mult)
-    tt(v("YA", 0, 112), v("XM"), v("YB"), OP.add)
-    dma("s", [(v("ya", 0, 112), v("YA", 0, 112))])
+    dma("s", [(v("ya", 0, 112, 1, i, 128, 16), v("X0", 3584, 3696, 1, i, 128, 16)) for i in (14, 15)])
     lin(v("XM"), v("XA"), col(C13), col(B255))
     land(1)
     dma("s", [(v("ypost", 304, 320), v("PIf", 304, 320))])
     tt(v("YA", 112, 224), v("XM"), v("WN"), OP.add)
     dma("a", [(v("ya", 112, 224), v("YA", 112, 224))])
 
-    for i in range(len(ops) - 1, -1, -1):
-        o = ops[i]
-        o["rank"] = o.get("rank", 0) + min(c for f, c in o["alt"].values()) + o["lat"] + o.get("more", 0)
-        for p in o["pre"]:
-            ops[p]["rank"] = max(ops[p].get("rank", 0), o["rank"])
-    nxt = [[] for o in ops]
-    for i, o in enumerate(ops):
-        for p in o["pre"]:
-            nxt[p].append(i)
-
-    def place(key, back):
-        busy, at = {e: [] for e in "vatgsn"}, [None] * len(ops)
-        for i in sorted(range(len(ops)), key=lambda j: key[j] if back or j >= NIN else j - 10 ** 9):
-            best = None
-            for e, (f, c) in ops[i]["alt"].items():
-                t0 = max([ops[i]["lat"] if back else 0] + [at[p][1] + (0 if e == "t" == at[p][2] else ops[i if back else p]["lat"]) for p in (nxt[i] if back else ops[i]["pre"])])
-                for x, y in busy[e]:
-                    if t0 + c <= x:
-                        break
-                    t0 = max(t0, y)
-                if best is None or t0 + c + PEN * (e == "v") < best[0]:
-                    best = (t0 + c + PEN * (e == "v"), t0, t0 + c, e)
-            at[i] = best[1:]
-            busy[best[3]].append(best[1:3])
-            busy[best[3]].sort()
-        return at
-
-    key, shape = [-o["rank"] for o in ops], tuple(tuple(o["pre"]) for o in ops)
-    for n in range(0 if shape in _ORDER else NIT):
-        at = place(key, False)
-        end = max(x[1] + o["lat"] for x, o in zip(at, ops))
-        if n == 0 or end < _ORDER[shape][0]:
-            _ORDER[shape] = (end, at)
-        key = [-x[1] for x in place([-x[1] for x in at], True)]
-    for o, x in zip(ops, _ORDER[shape][1]):
+    shape = tuple(tuple(o["pre"]) for o in ops)
+    if shape not in _ORDER:
+        _ORDER[shape] = arrange([o["pre"] for o in ops], [o["lat"] for o in ops], [{e: c for e, (f, c) in o["alt"].items()} for o in ops], [o.get("more", 0) for o in ops])
+    for o, x in zip(ops, _ORDER[shape]):
         o["start"], o["eng"] = x[0], x[2]
     know = {e: {} for e in E}
 

from concourse.bass import DstId, RemoteDMATransfer
from concourse.mybir import AluOpType as OP, AxisListType, ActivationFunctionType as AF

F, B, I, U, H16 = "float32", "bfloat16", "int32", "uint16", "float16"
_W = {
    B: "X0 4064 XB 3584 X1 3808 XA 112 H 4864 V 4864 W 4864 MC 4864 MB 4864 MC2 4864 MB2 4864 TN 4864 CE 320 TAB0 2688 TAB1 2688 L 448 SF0 320 SF1 320 OHB 320 F0 320 F1 320 INC 320 JK 320 ZER 16 ONE 384 Z 16 "
       "BT0 128 BT1 128 MV0 128 MV1 128 BQ 304 VS 272 VSa 256 AD 256 BD 256 AA 256 BA 256 LSE 128 LS 16 GS 16 NG 16 RO 16 ROo 16 BV 16 A2 448 S3 512 ZQ 2432 D0 608 Y 192 VB 320 LN 128 FV 16 FD 112 WN 112 "
       "MVV0 128 MVV1 128 YA 224 BO 128 TRI 128 ID 128 NID 128 IDL 128 U16 144 UN16 144 UH 144 UC 144 W8 40 ZW 240 MKU 192 I16 16 I17 16 C15 16 IOB 144 C256 24 C16b 16 HV0 256 HV1 256 FST 128 "
       "U1 144 RP 128 X24 24 T8 304 OHm 128 DN 384 DG 384 CO0 128 CO1 128 CO2 128 CO3 128 RN 128 RC 128 B15 128 PR0 128 PR1 128 D1 128 XM 112 TH 24",
    F: "PIf 320 PIm 320 PRa 128 CPf 320 SLOT 288 acc 4 t1 4 pre 10 CSf 16 SPf 16 g1 16 exo 16 CSo 16 SPo 16 E32 32 T2 16 T3 16 xw 16 hs 24 t24 24 GLf 16 QLf 8 COL 64 "
       "IOT 256 IOS 288 G1 128 G2 128 SQ 24 L8f 12 C16k 16 DGO 16 DQ 8 DM 8 ZC0 112 ZC1 112",
    I: "POI 288 ABI 448 NEI 320 kx 1 kr 1 kn 384 ki 384 Ti 24 lo 24 IC 4 AI 224 AJ 224 nn 128 iw 16",
    U: "PU 304 ABU 224 NU 304 pk8 8 NO0 2 NO1 2 NL0 8 NL1 8 SPu 16 CSu 16 LAu 16 obu 2 K16 16 TLu 24 QTu 8 VLu 24 MLu 24 QLu 8 MVL 8 GLu 16 L8u 12 CU 304 K86 8 K7 8",
    H16: "SC 2432 PGh 128 UF 144 BOh 128 IDh 128 DMh 8",
}
_S = {}
for _d, _t in _W.items():
    _t = _t.split()
    for _i in range(0, len(_t), 2):
        _S[_t[_i]] = (int(_t[_i + 1]), _d)
_PS = ["PA", "PB", "PC", "PX", "PN", "PG", "PM0", "PM1"]
_WHOLE = ["BT0", "BT1", "IOB"]
_OWN = "X0 XB X1 XA H V W MC MB MC2 MB2 TN CE TAB0 TAB1 L SF0 SF1 OHB BV I16 MV0 MV1 VS S3 ZQ VB FV YA PIf PIm CPf POI ABI NEI kn ki Ti lo nn SC".split() + _WHOLE
SCRATCH, _PACK, _n = {}, {}, {}
for _k, (_w, _d) in _S.items():
    if _k in _OWN or _d == U:
        SCRATCH[_k] = ("sbuf", [128, _w], _d)
    else:
        _PACK[_k] = ("PK" + _d, _n.get(_d, 0))
        _n[_d] = _n.get(_d, 0) + (_w + 15) // 16 * 16
for _d in _n:
    SCRATCH["PK" + _d] = ("sbuf", [128, _n[_d]], _d)
for _k in _PS:
    SCRATCH[_k] = ("psum", [128, 512], F)
_EX = ["a0", "b0", "c0", "a1", "b1", "c1"]
SEMAPHORES = ["cv", "ca", "ct", "cg"] + ["r" + e for e in _EX] + ["y" + e for e in _EX] + ["ls"] + ["d%d" % i for i in range(20)]
MS = (8, 8, 4, 8)
KA = ((1, 3, 5), (0, 1))
CH = 32
CHH = 36
TF = 5
QUAD = (0, 0, 1, 0)
NAB, DS3 = 4000, 3000
SCANS = ((2, 4), (0, 2), (4, 6), (6, 8))
NACT = (0, 1, 4, 5, 6)
GA, SCA, HOP, NET, DMA = 1.56, 3.8, 225, 3400, 1900
PEN, NIT, NIN = (100, 200, 350, 500, 700, 1000, 1500), 6, 5
GX, GL = 1.4, 400
NSW, TOL, SEED = 20000, 400, 1
_ORDER = {}


def bits(es):
    return sum(1 << e for e in es)


def parts(es, n):
    out, left = [], list(es)
    for i in range(n):
        k, s = n - i, 1
        while s * 2 <= (len(left) + k - 1) // k and s * 2 + (k - 1) <= len(left):
            s *= 2
        out.append(left[:s])
        left = left[s:]
    return out


def plan(r, T, topo):
    c = T.cores[r]
    direct = [d for d in range(len(T.cores)) if d != r and topo.may_write(c, T.cores[d])]
    cross = [d for d in range(len(T.cores)) if d != r and d not in direct]
    rel = [x for x in topo.cores_of(c) if x != c and topo.die(x) == topo.die(c) and T.rank_of(x) is None and all(topo.may_write(x, T.cores[d]) for d in cross)][:2]
    off = topo.engines(c, T.cores[direct[0]])
    return direct, [(x, cross[i::len(rel)]) for i, x in enumerate(rel)], off, [e for e in topo.engines(c, rel[0]) if e not in off]


def engines_to(ex, r, d, T, topo):
    direct, rel, off, on = plan(r, T, topo)
    q, es = ([(direct, off)] + [(q, topo.engines(x, T.cores[d])) for x, q in rel if d in q])[-1]
    return parts(es, len(q))[q.index(d)] if ex[0] == "c" else es


def order(r, T, topo):
    direct, rel, off, on = plan(r, T, topo)
    return [d for x, q in rel for d in q] + direct + [r]


def message(ex, r, d, T, topo):
    t, o = ex[1], r if r < d else r - 1
    if ex[0] == "a":
        return T["NO" + t][:, 0:1], T["NL" + t][:, o:o + 1]
    if ex[0] == "b":
        return T["BT" + t][:, 16 * r:16 * r + 16], T["BT" + t][:, 16 * r:16 * r + 16]
    a, p = 16 * o + (3584 if t == "0" else 0), 16 * order(r, T, topo).index(d)
    return T["MV" + t][:, p:p + 16], T["X1" if t == "0" else "XA"][:, a:a + 16]


def dst(topo, x, c):
    rid, pid = topo.addr(x, c)
    return DstId(rid=rid, pnc=pid)


def onward(ex, r, q, core, T, topo):
    if ex[0] == "c":
        return [RemoteDMATransfer(dst_ids=[dst(topo, T.cores[d], core)], dma_engine_mask=bits(engines_to(ex, r, d, T, topo)), remote_sem=T.sem["y" + ex],
                                  src=message(ex, r, d, T, topo)[0], dst=message(ex, r, d, T, topo)[1]) for d in q]
    return [RemoteDMATransfer(dst_ids=[dst(topo, T.cores[d], core) for d in q], dma_engine_mask=bits(engines_to(ex, r, q[0], T, topo)), remote_sem=T.sem["y" + ex],
                              srcs=[message(ex, r, q[0], T, topo)[0]], dsts=[message(ex, r, d, T, topo)[1] for d in q])]


def relay_program(g, core, T, topo):
    for r in range(len(T.cores)):
        direct, rel, off, on = plan(r, T, topo)
        for x, q in rel:
            if x == core:
                n = 0
                for ex in _EX:
                    g.wait_ge(T.sem["r" + ex], len(on) // len(rel) if ex[0] == "c" else len(on))
                    g.remote_dma_fused(onward(ex, r, q, core, T, topo), local_sem=T.sem.ls)
                    n += len(topo.engines(core, T.cores[q[0]]))
                g.wait_ge(T.sem.ls, n)


def arrange(pre, lat, alt, more):
    n = len(pre)
    nxt = [[] for i in range(n)]
    rank = [0] * n
    for i in range(n - 1, -1, -1):
        rank[i] += min(alt[i].values()) + lat[i] + more[i]
        for p in pre[i]:
            nxt[p].append(i)
            rank[p] = max(rank[p], rank[i])

    def place(key, alt, back=False, pen=0):
        busy, at = {e: [] for e in "vatgsn"}, [None] * n
        for i in sorted(range(n), key=lambda j: key[j] if back or j >= NIN else j - 10 ** 9):
            best = None
            for e, c in alt[i].items():
                t0 = lat[i] if back else 0
                for p in (nxt[i] if back else pre[i]):
                    t0 = max(t0, at[p][1] + (0 if e == "t" == at[p][2] else lat[i if back else p]))
                q = busy[e]
                k = len(q)
                while k and q[k - 1][1] > t0:
                    k -= 1
                while k < len(q) and t0 + c > q[k][0]:
                    t0, k = max(t0, q[k][1]), k + 1
                if best is None or t0 + c + pen * (e == "v") < best[0]:
                    best = (t0 + c + pen * (e == "v"), t0, t0 + c, e, k)
            at[i] = best[1:4]
            busy[best[3]].insert(best[4], best[1:3])
        return at

    def end(at):
        return max(x[1] + y for x, y in zip(at, lat))

    at = None
    for pen in PEN:
        key = [-x for x in rank]
        for k in range(NIT):
            a = place(key, alt, False, pen)
            if at is None or end(a) < end(at):
                at = a
            key = [-x[1] for x in place([-x[1] for x in a], alt, True, pen)]
    marks, seed = [i for i in range(n) if "n" in alt[i]], [SEED]

    def pick(xs):
        seed[0] = (seed[0] * 1103515245 + 12345) % 2 ** 31
        return xs[(seed[0] >> 8) % len(xs)]

    def worth(at):
        return end(at) + 0.2 * sum(at[i][1] for i in marks) + 0.05 * sum(x[1] for x in at) / n

    gap = [[(p, 0 if "t" in alt[i] and "t" in alt[p] else lat[p]) for p in pre[i]] for i in range(n)]

    def again(key, one, old, seq0, j0):
        seq = sorted(range(n), key=lambda j: key[j])
        f = 0
        while f < n and seq[f] == seq0[f] != j0:
            f += 1
        busy, at = {e: [] for e in "vatgsn"}, list(old)
        for x in sorted(at[i] for i in seq[:f]):
            busy[x[2]].append(x)
        for i in seq[f:]:
            e, t0 = one[i], 0
            c, q = alt[i][e], busy[e]
            for p, d in gap[i]:
                if at[p][1] + d > t0:
                    t0 = at[p][1] + d
            k = m = len(q)
            while k and q[k - 1][1] > t0:
                k -= 1
            while k < m and t0 + c > q[k][0]:
                if q[k][1] > t0:
                    t0 = q[k][1]
                k += 1
            at[i] = (t0, t0 + c, e)
            q.insert(k, at[i])
        return at, seq

    key, one, kept = [x[0] if i >= NIN else i - 10 ** 9 for i, x in enumerate(at)], [x[2] for x in at], at
    at, seq = again(key, one, at, [-1] * n, -1)
    now, paths = worth(at), {}
    for k in range(NSW):
        if paths.get("at") is not at:
            paths = {"at": at, "before": {x[1:]: j for j, x in enumerate(at)}, "last": max(range(n), key=lambda j: at[j][1] + lat[j])}
        i = pick(marks + [paths["last"]] * 3)
        if i not in paths:
            pairs = paths[i] = []
            while i is not None:
                c = [p for p, d in gap[i] if at[p][1] + d == at[i][0]]
                j = pick(c) if c else paths["before"].get((at[i][0], at[i][2]))
                if not c and j is not None:
                    pairs.append((j, i))
                i = j
        else:
            pairs = paths[i]
        if not pairs:
            continue
        (a, b), how, key2, one2 = pick(pairs), pick((0, 1, 2)), list(key), list(one)
        free, j0 = [j for j in (a, b) if len(alt[j]) > 1], -1
        if how == 0 and free:
            j0 = pick(free)
            one2[j0] = [e for e in alt[j0] if e != one[j0]][0]
        elif a >= NIN:
            d, todo = (-1, [b]) if how < 2 else (1, [a])
            key2[todo[0]] = (min if d < 0 else max)(key[a], key[b]) + d * pick((1, 1, 300, 1000, 3000))
            while todo:
                j = todo.pop()
                for p in (pre[j] if d < 0 else nxt[j]):
                    if d * key2[p] <= d * key2[j]:
                        key2[p] = key2[j] + d * 0.01
                        todo.append(p)
        a, seq2 = again(key2, one2, at, seq, j0)
        w = worth(a)
        if w <= now + pick(range(1 + TOL * (NSW - k) // NSW)):
            at, key, one, now, seq = a, key2, one2, w, seq2
            if end(at) < end(kept):
                kept = at
    return kept


def rank_program(g, core, T, topo):
    r = T.rank_of(core)
    if r is None:
        relay_program(g, core, T, topo)
        return
    N = len(T.cores)
    E = {"v": g.vector, "a": g.scalar, "t": g.tensor, "g": g, "s": g.sync}
    ops, hist, ndma = [], {}, [0]

    def v(n, a=0, b=None, st=1, p0=0, p1=128, ps=1):
        w = _S[n][0] if n in _S else (512 if n in _PS else T[n].shape[1])
        b = w if b is None else b
        nn, o = _PACK.get(n, (n, 0))
        return (nn, a + o, b + o, st, p0, p1, ps)

    def ind(w, o):
        return ("IND", w, o)

    def ap(x):
        if not isinstance(x, tuple):
            return x
        if x[0] == "IND":
            return ap(x[1]).indirect(ap(x[2]))
        n, a, b, st, p0, p1, ps = x
        if ps != 1:
            return T[n][p0:p1:ps, a:b]
        return T[n][p0:p1, a:b] if st == 1 else T[n][p0:p1, a:b:st]

    def regs(xs):
        return [v(y[0]) if y[0] in _WHOLE else y for x in xs if isinstance(x, tuple) for y in (x[1:] if x[0] == "IND" else [x])]

    def width(x):
        return 16 * (x[2][2] - x[2][1]) if x[0] == "IND" else (x[2] - x[1] + x[3] - 1) // x[3]

    def short(x):
        return x[0] not in _PS and SCRATCH[x[0]][2] in (B, U, H16)

    def step(alt, outs, ins, acc=False, sem=None, lat=HOP):
        o, i = regs([x[1] if x[0] == "IND" else x for x in outs]), regs(ins) + [x[2] for x in outs if x[0] == "IND"]
        me, pre, one = len(ops), {}, list(alt)[0] if len(alt) == 1 else None
        for w, xs in ((True, o), (False, i)):
            for x in xs:
                for h in hist.setdefault(x[0], []):
                    y = h[0]
                    if x[0] in _PS:
                        if (acc and w and h[3]) or (not w and not h[1] and one and ops[h[2]]["one"] == one):
                            continue
                    elif y[2] <= x[1] or y[1] >= x[2] or not (w or h[1]) or y[5] <= x[4] or y[4] >= x[5] or (y[3] == x[3] and (y[1] - x[1]) % x[3]):
                        continue
                    pre[h[2]] = True
        for w, xs in ((True, o), (False, i)):
            for x in xs:
                hs = hist[x[0]]
                if w and not acc and (x[0] in _PS or (x[3] == 1 and x[4] == 0 and x[5] == 128)):
                    hs[:] = [h for h in hs if not (x[0] in _PS or (h[0][1] >= x[1] and h[0][2] <= x[2]))]
                hs.append((x, w, me, acc and w))
        ops.append({"alt": alt, "one": one, "pre": [p for p in pre if p != me], "sem": sem, "lat": lat})
        return me

    def cost(o, xs, two=False):
        n = width(o)
        if o[0] == "IND":
            return 60 + SCA * n
        if xs[0][0] == "IND":
            return 60 + GA * n
        n = width(xs[0])
        return 60 + (2 * n if two and not any(x[0] in _PS for x in xs) else (n / 2 if not two and short(o) and all(short(x) for x in xs) else n))

    def on_v(fn, o, xs, c):
        return step({"v": (lambda: [fn()], c)}, [o], xs)

    def tt(o, a, b, op):
        on_v(lambda: g.vector.tensor_tensor(ap(o), ap(a), ap(b), op), o, [a, b], cost(o, [a, b], True))

    def f_ts(o, a, s1, op0, s2=None, op1=None):
        if op1 is None:
            return lambda: g.vector.tensor_scalar(ap(o), ap(a), ap(s1), None, op0)
        return lambda: g.vector.tensor_scalar(ap(o), ap(a), ap(s1), ap(s2), op0, op1)

    def plain(o, a):
        return o[0] != "IND" and all(y[0] in _PS or SCRATCH[y[0]][2] in (F, B) for y in (o, regs([a])[0]))

    def ts(o, a, s1, op0, s2=None, op1=None):
        if plain(o, a) and (op0, op1) in ((OP.mult, None), (OP.add, None), (OP.mult, OP.add)):
            lin(o, a, None if op0 == OP.add else s1, s1 if op0 == OP.add else s2)
        else:
            on_v(f_ts(o, a, s1, op0, s2, op1), o, [a, s1, s2], cost(o, [a]))

    def tc(o, a):
        if plain(o, a):
            lin(o, a)
        else:
            on_v(lambda: g.vector.tensor_copy(ap(o), ap(a)), o, [a], cost(o, [a]))

    def scan(o, a, b, init, op0, op1):
        on_v(lambda: g.vector.tensor_tensor_scan(ap(o), ap(a), ap(b), ap(init), op0, op1), o, [a, b, init], cost(o, [a, b]))

    def ms(o, c):
        on_v(lambda: g.vector.memset(ap(o), c), o, [], cost(o, [o]))

    def c_act(a):
        return 80 + GA * width(a) if a[0] == "IND" else 80 + width(a)

    def act(o, a, f=AF.Copy, bias=0.0, scale=1.0, acc=None):
        step({"a": (lambda: [g.scalar.activation(ap(o), ap(a), f, ap(bias), ap(scale), accum_out=ap(acc))], c_act(a))}, [o] + ([acc] if acc else []), [a, bias, scale])

    def lin(o, a, scale=None, bias=None):
        if scale is None and bias is None:
            fv = lambda: g.vector.tensor_copy(ap(o), ap(a))
        else:
            fv = f_ts(o, a, 1.0 if scale is None else scale, OP.mult, 0.0 if bias is None else bias, OP.add)
        fa = lambda: g.scalar.activation(ap(o), ap(a), AF.Copy if bias is None else AF.Identity, 0.0 if bias is None else ap(bias), 1.0 if scale is None else ap(scale))
        step({"v": (lambda: [fv()], cost(o, [a])), "a": (lambda: [fa()], c_act(a))}, [o], [a, scale, bias])

    def mm(*ms_, acc=False):
        c = sum(max(min(64, width(x[1])), width(x[2])) / 2 + TF for x in ms_)
        step({"t": (lambda: [g.tensor.matmul(ap(o), ap(l), ap(x), s0, s1) for o, l, x, s0, s1 in ms_], c)}, [x[0] for x in ms_], [y for x in ms_ for y in x[1:3]], acc)

    def long(*ms_, n=8):
        for i in range(0, len(ms_), n):
            mm(*ms_[i:i + n])

    def iota(o, pat, base=0, ch=0):
        step({"g": (lambda: [g.iota(ap(o), pat, base, ch, allow_small_or_imprecise_dtypes=True)], GX * (160 + 2 * width(o)))}, [o], [], lat=GL)

    def select(o, a, pat, op, c, base, ch):
        step({"g": (lambda: [g.affine_select(ap(o), ap(a), pat, op, float(c), base, ch)], GX * (210 + 2 * width(o)))}, [o], [a], lat=GL)

    def fill(o, c):
        step({"g": (lambda: [g.iota(ap(o), [[0, width(o)]], c, 0, allow_small_or_imprecise_dtypes=True)], GX * (160 + 2 * width(o))),
              "v": (lambda: [g.vector.memset(ap(o), c)], cost(o, [o]))}, [o], [])

    def dma(q, pairs, lat=DMA):
        ndma[0] += 1
        step({q: (lambda: [E[q].dma_start(ap(o), ap(a)) for o, a in pairs], 60 * len(pairs))}, [o for o, a in pairs], [a for o, a in pairs], sem="d%d" % (ndma[0] - 1), lat=lat)

    direct, rel, off, on = plan(r, T, topo)
    cnt, seg = {"ls": 0}, order(r, T, topo)

    def exchange(ex, x, lands):
        last = onward(ex, r, direct, core, T, topo)
        if ex[0] == "c":
            w = [T["MV" + ex[1]][:, 16 * seg.index(q[0]):16 * seg.index(q[-1]) + 16] for c, q in rel]
            calls = [([RemoteDMATransfer(dst_ids=[dst(topo, c, core)], dma_engine_mask=bits(es), remote_sem=T.sem["r" + ex], src=y, dst=y)
                       for (c, q), y, es in zip(rel, w, parts(on, len(rel)))], x[0], NET - 500), (last, x[1], NET - 1500)]
        else:
            calls = [([RemoteDMATransfer(dst_ids=[dst(topo, c, core) for c, q in rel], dma_engine_mask=bits(on), remote_sem=T.sem["r" + ex], srcs=[ap(x)], dsts=[ap(x) for c in rel])] + last,
                      x, NAB + 3000 * (ex == "a0"))]
        cnt["ls"] += len(on) + len(off)
        s = [step({"g": (lambda tr=tr: [g.remote_dma_fused(tr, local_sem=T.sem.ls)][1:], 400)}, [], [y], lat=lat) for tr, y, lat in calls]
        cnt["y" + ex] = sum(len(engines_to(ex, q, r, T, topo)) for q in range(N) if q != r)
        ops[step({"n": (None, 1)}, lands, [], sem="y" + ex, lat=HOP)]["pre"] += s

    def col(i):
        return v("COL", i, i + 1)

    (P_, M_, G_, G15, C13, K14, K15, UHC, UCC, C16_, CN16, R15, I0, BC, B255, LT8, GE8, MH, RNC, K256, H18, H19, N255, C256_, K7N, CP_, CN_) = range(27)
    TQ, TQB = 32, 40

    def nbs(t):
        return [128, 128, 32 + 16 * t]

    def chunks(a, b, n=CH):
        return [(x, min(b, x + n)) for x in range(a, b, n)]

    def phase(k, fn, xs):
        i, w = len(ops), 0
        for x in xs:
            fn(*x)
        for o in ops[:i - 1:-1]:
            if "t" not in o["alt"]:
                o["more"] = w
                w += min(c for f, c in o["alt"].values()) / k

    dma("s", [(v("POI"), v("post"))])
    dma("a", [(v("ABI", 224, 448), v("absorb", 224, 448))], 1900)
    dma("a", [(v("X0", 0, 1792), v("rec", 0, 1792))], 3800)
    dma("s", [(v("X0", 1792, 3584), v("rec", 1792, 3584))], 3800)
    dma("s", [(v("XB", 0, 3584, 1, 16 * q, 16 * q + 14), v("rec", 0, 3584, 1, 16 * q, 16 * q + 14)) for q in range(8)] + [(v("ABI", 0, 224), v("absorb", 0, 224))], 5500)
    ic = [v("IC", i, i + 1) for i in range(3)]
    iota(ic[0], [[0, 1]], 0, 1)
    iota(v("IOT"), [[1, 256]])
    iota(v("IOS"), [[16, 288]])
    iota(v("G1"), [[1, 8], [0, 16]])
    iota(v("G2"), [[0, 8], [1, 16]])
    iota(v("C15"), [[-1, 16]], 15)
    iota(v("C16k"), [[16, 16]])
    iota(v("C16b"), [[16, 16]])
    iota(v("C256"), [[256, 24]])
    iota(v("SQ"), [[1, 8], [8, 3]])
    iota(v("IOB", 0, 16 * r + 16), [[1, 16 * r + 16]])
    iota(v("IOB", 16 * r, 128), [[1, 128 - 16 * r]], 16 * r + 16)
    iota(v("IOB", 128, 144), [[1, 16]], 16 * r)
    ts(ic[1], ic[0], 15, OP.bitwise_and)
    ts(ic[2], ic[0], 4, OP.arith_shift_right)
    for i in range(3):
        tc(col(i), ic[i])
    ts(col(G15), col(G_), 16, OP.mult, 15, OP.add)
    for c, x, op in ((C13, 14, OP.is_lt), (K14, 14, OP.is_equal), (K15, 15, OP.is_equal), (I0, 0, OP.is_equal), (GE8, 8, OP.is_ge)):
        ts(col(c), col(M_), x, op)
    for c, x, a, b in ((BC, C13, -1, 1), (B255, C13, -255, 255), (N255, C13, 255, -255), (K256, C13, -256, 256), (C256_, C13, 256, 0), (UHC, K14, 256, col(K15)), (UCC, K15, 1 / 256, col(K14)),
                       (RNC, K14, -16, col(K15)), (C16_, C13, 16, 0), (CN16, C13, -16, 0), (R15, M_, 16, 15), (LT8, GE8, -1, 1), (MH, M_, 2, 1), (H18, K14, 18, 0),
                       (H19, K14, 19, 0), (K7N, K14, -7, 0), (CP_, C13, 2048, 0), (CN_, C13, -2048, 0)):
        ts(col(c), col(x), a, OP.mult, b, OP.add)
    ts(v("U1"), v("IOT", 0, 144), col(G15), OP.is_equal)
    for nm, c in (("UH", UHC), ("UC", UCC), ("U16", C16_), ("UN16", CN16)):
        ts(v(nm), v("U1"), col(c), OP.mult)
    tc(v("UF"), v("U1"))
    ts(v("ID"), v("IOT", 0, 128), col(P_), OP.is_equal)
    for nm, w in (("NID", -1), ("IDL", 2 ** 23), ("IDh", 1)):
        ts(v(nm), v("ID"), w, OP.mult)
    ts(v("BO"), v("G1"), col(G_), OP.is_equal)
    for nm, c in (("BOh", 1), ("RN", col(RNC)), ("RC", col(UCC))):
        ts(v(nm), v("BO"), c, OP.mult)
    ts(v("B15"), v("U1", 0, 128), col(M_), OP.mult)
    select(v("TRI"), v("BO"), [[1, 128]], OP.is_ge, 0, 0, -1)
    ts(v("SLOT"), v("IOS"), col(M_), OP.add)
    ts(v("I16"), v("IOT", 0, 16), col(M_), OP.is_equal)
    ts(v("I17"), v("I16"), 2 ** 17, OP.mult)
    for i, (c, w) in enumerate(((CP_, 2), (CN_, 2), (CP_, 1), (CN_, 1), (I0, 1))):
        ts(v("W8", 8 * i, 8 * i + 8), v("BO", 0, 128, 16), col(c), OP.mult, w, OP.mult)
    for i, x in enumerate(MS):
        if x and (i < 2 or x != MS[i - 2]):
            ts(v("CO%d" % i), v("BO"), col(CP_ if i % 2 else CN_), OP.mult)
            select(v("CO%d" % i), v("CO%d" % i), [[0, 8], [-1, 16]], OP.is_gt, 0, x, 0)
    for x, c in ((v("ZER"), 0), (v("ONE"), 1), (v("DN"), -128), (v("D0"), -1), (v("MVV0"), 255), (v("FST"), -2 ** 17), (v("TAB0", 0, 896), 4096)):
        ms(x, c)
    ms(v("DN", 0, 384, 16), 2 ** 14)
    ms(v("D0", 304, 305), 2000)
    select(v("RP"), v("ONE", 0, 128), [[-1, 8], [0, 16]], OP.is_equal, 0, 0, 1)
    select(v("MKU"), v("ONE", 0, 192), [[0, 24], [-16, 8]], OP.is_ge, 0, 0, 1)
    select(v("MKU"), v("MKU"), [[0, 24], [16, 8]], OP.is_ge, 0, 15, -1)

    for x in (v("X0", 3584, 3808), v("X1", 3696, 3808), v("L", 288, 448), v("CE", 288, 320), v("VS", 256, 272), v("VB", 288, 320), v("OHB", 288, 320), v("ZW")):
        fill(x, 0)
    for x in (v("F0", 288, 304), v("F1", 304, 320), v("SF0"), v("SF1"), v("D1"), v("DG")):
        fill(x, 1)
    fill(v("MVV1"), 255)
    ms(v("DG", 0, 384, 16), -2 ** 25)
    ms(v("D1", 7, 128, 8), 0)
    ts(v("ZW", 112, 128), v("I16"), -1, OP.mult)
    ts(v("L8f"), v("SQ", 0, 24, 2), col(LT8), OP.mult)
    ts(v("t24", 0, 12), v("SQ", 1, 24, 2), col(GE8), OP.mult)
    tt(v("L8f"), v("L8f"), v("t24", 0, 12), OP.add)
    tc(v("L8u"), v("L8f"))
    ts(v("K7"), v("IOT", 0, 8), 0, OP.mult, col(M_), OP.add)
    ts(v("K86"), v("K7"), 8, OP.mult, 6, OP.add)
    for i, d in enumerate(seg):
        fill(v("PRa", 16 * i, 16 * i + 16), 16 * d + 16)
    ts(v("COL", TQ, TQ + 8), v("PRa", 0, 128, 16), col(M_), OP.add)
    ts(v("PRa"), v("PRa"), 16 * r + 16, OP.is_le, 32 - r, OP.add)
    ts(v("COL", TQB, TQB + 8), v("COL", TQ, TQ + 8), -1000, OP.mult)
    ts(v("DGO"), v("C16k"), col(M_), OP.add, 3808, OP.add)
    ts(v("DQ"), v("COL", TQ, TQ + 8), 304 - 287, OP.add)
    ts(v("DM"), v("COL", TQ, TQ + 8), 3808 - 1904 - 16, OP.add)
    for x in (v("PIf", 288, 320), v("CPf", 288, 320), v("NEI", 288, 320), v("PIm", 288, 320)):
        fill(x, 0)
    ms(v("PN", 256, 384), 0)
    tc(v("K16"), v("IOT", 0, 16))
    ts(v("PRa"), v("PRa"), col(K14), OP.mult, col(C256_), OP.add)
    ts(v("JK", 0, 128), v("G2"), col(K15), OP.mult)
    tt(v("PR0"), v("PRa"), v("JK", 0, 128), OP.add)
    ts(v("PR1"), v("PR0"), col(K7N), OP.add)
    for t in range(2):
        lin(v("HV%d" % t), v("IOT"), col(K15), col(H18 + t))
        iota(v("ZC%d" % t), [[1, 112]], 3584 + 112 * t - 4096)
        fill(v("PR%d" % t, 112, 128), 2 ** 20)

    def by_row(bank, u, x, a, b):
        mm(*[(v(bank, a, b), v(u, 15 - m, 143 - m), v(x, 16 * a + m, 16 * b, 16), m == 0, m == 15) for m in range(16)], acc=True)

    def full(t, a, b):
        mm((v("PC", a, b), v("BO"), v("L", a, b), True, True))
        act(v("F%d" % t, a, b), v("PC", a, b), AF.Sign, -11.5)

    def count(t, a, b, j, one):
        scan(v("INC", a, b), v("F%d" % t, a, b), v(one, a, b), v("INC", a - 1, a) if a else 0.0, OP.add, OP.add)
        act(v("JK", a, b), v("INC", a, b), AF.Sign, col(MH), -1.0, v("acc", j, j + 1))

    def numbers(t, x, pre):
        P, t1, t2 = 288 + 16 * t, v("t1", 0, 1), v("t1", 1, 2)
        ts(v("pre", 0, 8), v("IOT", 0, 8), 0.0, OP.mult, pre, OP.add)
        ts(v("pre", 8, 9), v("pre", 0, 1), -1, OP.mult, 2 * P, OP.add)
        ts(v("pre", 9, 10), v("pre", 0, 1), 0.5, OP.mult, 320 * r, OP.add)
        ts(v("pk8"), v("pre", 0, 8), x, OP.add, 0.5, OP.mult)
        ts(t1, x, 0.5, OP.mult, v("pre", 9, 10), OP.add)
        ts(t2, x, v("pre", 8, 9), OP.is_ge, 2560 + 16 * r - 320 * r - P, OP.mult)
        ts(v("NO%d" % t, 0, 1), t1, t2, OP.add)
        exchange("a%d" % t, v("NO%d" % t, 0, 1), [v("NL%d" % t, 0, 7)])

    def apart(win, lst, x, out, bank):
        lin(v(x), ind(v(win), v(lst)))
        mm((bank, v("NID"), v("VS", 0, 256), True, False))
        mm((bank, v("ID"), v(x), False, True))
        act(v(out), bank, AF.Abs)

    def split(t):
        P, pk1, bt, pc = 288 + 16 * t, v("pk8", 0, 1), v("BT%d" % t, 16 * r, 16 * r + 16), v("PC", 0, 16)
        tc(v("SPu"), ind(v("PIf"), pk1))
        if t == 0:
            lin(v("VS", 0, 256), ind(v("X1", 0, 3584), v("SPu")))
        else:
            tc(v("CSu"), ind(v("CPf"), pk1))
            lin(v("VSa"), ind(v("X1"), v("SPu")))
            tt(v("VS", 0, 256), ind(v("X1"), v("CSu")), v("VSa"), OP.max)
        tc(v("LS"), ind(v("L", 0, 320), pk1))
        mm((pc, v("TRI"), v("LS"), True, True))
        act(v("Z"), pc, AF.Relu, 1.0, -1.0)
        mm((pc, v("ID"), v("C16b"), True, False), (pc, v("BO"), v("Z"), False, True))
        tc(v("LAu"), pc)
        tt(v("LSE"), ind(v("L", 0, 320), v("pk8")), v("BO"), OP.mult)
        apart("VS", "LAu", "AD", "AA", v("PX", 0, 256))
        mm((pc, v("ID"), v("C15"), True, False), (pc, v("LSE"), v("I17"), False, False))
        mm(*[(pc, v("U16", 15 - k, 143 - k), v("AA", 16 * k, 16 * k + 16), False, k == 15) for k in range(16)])
        on_v(lambda: g.vector.tensor_reduce(ap(v("kx")), ap(pc), AxisListType.X, OP.max), v("kx"), [pc], 64)
        ts(v("kr"), v("kx"), 15, OP.bitwise_and)
        ts(v("obu", 0, 1), v("kr"), -1, OP.mult, col(R15), OP.add)
        tc(bt, ind(v("VS"), v("obu", 0, 1)))
        exchange("b%d" % t, bt, [v("BT%d" % t)])
        tc(ind(v("SF%d" % t), pk1), v("ZER", 0, 16))

    def parted(t):
        pk1, pb = v("pk8", 0, 1), v("PB", 0, 16)
        tc(v("BV"), ind(v("VS"), v("obu", 0, 1)))
        apart("BV", "K16", "BD", "BA", v("PB", 0, 256))
        tc(v("SPf"), ind(v("PIf"), pk1))
        for u, x in (("U16", "AA"), ("UN16", "BA")):
            long(*([(pb, v("IDL"), v("LS"), True, False)][:x == "AA"] + [(pb, v(u, 15 - m, 143 - m), v(x, m, 256, 16), False, x == "BA" and m == 15) for m in range(16)]))
        ts(v("GS"), pb, 2 ** 23, OP.is_gt)
        ts(v("NG"), v("GS"), -1, OP.mult, 1, OP.add)
        mm((pb, v("IDL"), v("GS"), True, False), (pb, v("TRI"), v("NG"), False, True))
        ts(v("RO"), pb, 1, OP.is_equal)
        mm((pb, v("ID"), v("HV%d" % t, 0, 256, 16), True, False), (pb, v("B15"), v("RO"), False, True))
        tc(v("FV"), pb)
        tc(v("MVV%d" % t, 112, 128), v("FV"))
        lin(v("FD"), ind(v("FV"), v("K7", 0, 7)), None, col(N255))
        ts(v("g1"), v("NG"), 8192, OP.mult)
        tt(v("g1"), v("g1"), v("SPf"), OP.add)
        tt(v("GLf"), v("g1"), v("DGO"), OP.min)
        tc(v("GLu"), v("GLf"))
        tc(ind(v("X0"), v("GLu")), v("HV%d" % t))
        if t == 0:
            tt(v("LS"), v("LS"), v("GS"), OP.subtract)
            tc(ind(v("L", 0, 320), pk1), v("LS"))

    def centres():
        pk1 = v("pk8", 0, 1)
        tc(ind(v("CE"), pk1), v("AD", 0, 256, 16))
        tc(v("CE", 288, 304), v("BT0", 16 * r, 16 * r + 16))
        tc(v("NU", 288, 304), ind(v("NEI"), pk1))
        tc(v("CSf"), ind(v("CPf"), pk1))

    def by_posting(xs, w, t):
        mm(*[(v("PG", 128 * b + m, 128 * b + 128, 16, 0, nbs(t)[b]), x, v("W8", 8 * w, 8 * w + 8), False, False) for m, b, x in xs], acc=True)

    def listed(x, first):
        tt(v("Y"), ind(v(x), v("L8u")), v("MKU"), OP.mult)
        for o, x in ([(24, first)] if first else []) + [(0, [])]:
            mm(*(x + [(v("PC", o, o + 24), v("ZW", 112 - 16 * q, 240 - 16 * q), v("Y", 24 * q, 24 * q + 24), q == 0 and not x, q == 7) for q in range(8)]))

    def near(t):
        P, nb, tab = 288 + 16 * t, nbs(t), v("TAB%d" % t)
        tc(ind(tab, v("NO%d" % t, 0, 1)), v("IOB", 128, 144))
        tc(ind(tab, v("NL%d" % t, 0, 7)), v("IOB", 0, 112))
        phase(2, lambda a, b: lin(v("TN", 16 * a, 16 * b), ind(tab, v("NU", a, b))), chunks(0, 256) + chunks(256, P, 16))
        for b in range(3):
            mm(*[(v("PN", 128 * b + m, 128 * b + 128, 16, 0, nb[b]), v("TN", 2048 * b + m, 2048 * b + 16 * nb[b], 16), v("W8", 32, 40), True, True) for m in range(16)], acc=True)
        scan(v("kn"), v("DN"), v("PN", 0, 384), 0.0, OP.add, OP.min)
        ts(v("Ti"), v("kn", 15, 384, 16), 127, OP.bitwise_and)
        listed("Ti", [])
        ts(v("TLu"), v("PC", 0, 24), -1, OP.mult)
        lin(v("BQ", 0, P), ind(v("BT%d" % t), v("TLu", 0, P // 16)))
        ts(v("hs"), v("kn", 15, 384, 16), 128, OP.is_lt)
        ts(v("t24"), v("Ti"), 16, OP.add)
        tt(v("TH"), v("t24"), v("hs"), OP.mult)

    def gains(t, c, out, sign):
        P, nb, V, k = 288 + 16 * t, nbs(t), "VW"[t], MS[2 * t + sign]
        first = [len(ops)][:k]
        if k:
            mm((v("PX", 0, P), v("ID"), v(c, 0, P), True, True))
            mm(*[(v("PG", 128 * b, 128 * b + 128, 1, 0, nb[b]), v(c, 128 * b, 128 * b + nb[b]), v("CO%d" % (sign + 2 * (k != MS[sign]))), False, False) for b in range(3)], acc=True)

        def row(m):
            tt(v(out, 304 * m, 304 * m + P), v(V, m, 16 * P, 16), v("PX", 0, P), OP.max)
            if m >= MS[2 * t + 1 - sign]:
                by_posting([(m, b, v(V, 2048 * b + m, 2048 * b + 16 * nb[b], 16)) for b in range(3)], 3 - sign, t)
            by_posting([(m, b, v(out, 304 * m + 128 * b, 304 * m + 128 * b + nb[b])) for b in range(3)], sign, t)

        def rows(i, b, ms_):
            n, bank, o = nb[b], ("PM0", "PM1", "PA", "PN")[i % (3 + sign)], 2048 * b + nb[b] * ms_[0]
            mm(*[(v(bank, n * j, n * j + n), v("ID"), v(V, 2048 * b + m, 2048 * b + 16 * n, 16), j == 0, False) for j, m in enumerate(ms_)])
            mm(*[(v(bank, n * j, n * j + n), v("NID"), v(c, 128 * b, 128 * b + n), False, m == ms_[-1]) for j, m in enumerate(ms_)])
            ops[-1]["pre"] += first
            act(v(out + "2", o, o + n * len(ms_)), v(bank, 0, n * len(ms_)), AF.Abs)
            by_posting([(m, b, v(out + "2", o + n * j, o + n * j + n)) for j, m in enumerate(ms_)], sign + 2, t)
        phase(1, row, [(m,) for m in range(k)])
        def arow(m):
            o, x, pm = v(out, 304 * m, 304 * m + P), v(V, m, 16 * P, 16), v(("PM0", "PM1", "PA", "PN")[m % (3 + sign)], 0, P)
            mm((pm, v("ID"), x, True, False))
            mm((pm, v("NID"), v(c, 0, P), False, True))
            ops[-1]["pre"] += first
            act(o, pm, AF.Abs)
            by_posting([(m, b, v(out, 304 * m + 128 * b, 304 * m + 128 * b + nb[b])) for b in range(3)], sign + 2, t)
        if QUAD[2 * t + sign]:
            phase(1, rows, [(i, b, range(x, y)) for i, (b, x, y) in enumerate((b, x, y) for b in range(3) for x, y in chunks(k, 16, 512 // nb[b]))])
        else:
            phase(1, arow, [(m,) for m in range(k, 16)])

    def absorb(out, win, lst, x, n, k):
        def part(a, b):
            o, w, y = v(out, 16 * a, 16 * b), ind(win, v(lst, a, b)), v(x, 16 * a, 16 * b)
            if a // 32 in k:
                h, pm = v("H", 16 * a, 16 * b), v("PM%d" % (k.index(a // 32) % 2), 0, 16 * (b - a))
                act(h, w)
                mm((pm, v("ID"), h, True, True))
                tt(o, pm, y, OP.max)
            else:
                tt(o, w, y, OP.max)
        cut = [a for a in range(0, n, 32) if a // 32 in k or a // 32 - 1 in k or a % CH == 0] + [n]
        phase(1, part, zip(cut, cut[1:]))

    def keys_open(t):
        nb = nbs(t)
        mm((v("PG", 0, 384), v("FST"), v("ONE"), True, False))
        for x in ("L", "SF%d" % t):
            mm(*[(v("PG", 128 * b, 128 * b + 128, 1, 0, nb[b]), v(x, 128 * b, 128 * b + nb[b]), v("IDL"), False, False) for b in range(3)], acc=True)

    def turn(x, pa, out, banks, t):
        P, nb = 288 + 16 * t, nbs(t)
        mm(*[(v(pa, 128 * b, 128 * b + nb[b], 1, 0, 8), v(x, 8 * b, 8 * b + 8), v("ID", 0, nb[b]), True, True) for b in range(3)])
        lin(v(out, 0, P, 1, 0, 8), v(pa, 0, P, 1, 0, 8))
        for bank in banks:
            mm((v(bank, 0, P), v("RP", 0, 128, 1, 0, 8), v(out, 0, P, 1, 0, 8), True, True))

    def pick(t):
        P = 288 + 16 * t
        mm((v("PG", 0, 16), v("FST"), v("ZER", 0, 16), False, True))
        scan(v("ki"), v("DG"), v("PG", 0, 384), 0.0, OP.add, OP.max)
        tt(v("X24"), v("ki", 15, 384, 16), v("TH"), OP.min)
        turn("X24", "PA", "T8", ("PM0", "PM1"), t)
        ts(v("lo"), v("ki", 15, 384, 16), 15, OP.bitwise_and)
        listed("lo", [(v("PC", 24, 48), v("ID"), v("C256"), True, False)])
        ts(v("VLu"), v("PC", 24, 48), col(R15), OP.add)
        ts(v("MLu"), v("PC", 0, 24), 15, OP.add)
        lin(v("VB", 0, P), ind(v("VW"[t], 0, 16 * P), v("VLu", 0, P // 16)))
        for q in range(8):
            z = v("ZQ", P * q, P * q + P)
            if q in NACT:
                act(z, v("PM0", 0, P), AF.Abs, col(TQB + q), 1000.0)
            else:
                ts(z, v("PM1", 0, P), col(TQ + q), OP.not_equal, 1000, OP.mult)
        for a, b in SCANS:
            scan(v("SC", P * a, P * b), v("D0", 304 - P, 304 + P), v("ZQ", P * a, P * b), 1000.0, OP.add, OP.min)
        h = N - 1 - len(direct)
        for a, b in ((0, h), (h, N)):
            ts(v("QTu", a, b), v("SC", P * a + P - 1, P * b, P), P - 1, OP.add, 304, OP.min)
            tt(v("MV%d" % t, 16 * a, 16 * b), ind(v("VB"), v("QTu", a, b)), v("PR%d" % t, 16 * a, 16 * b), OP.min)
        exchange("c%d" % t, [v("MV%d" % t, 0, 16 * h), v("MV%d" % t, 16 * h, 128)], [v("XA") if t else v("X1", 3584, 3696)])

    def own(t):
        P = 288 + 16 * t
        last = v("SC", P - 1, 8 * P, P)
        tc(v("OHB", 0, P), ind(v("I16"), v("MLu", 0, P // 16)))
        tc(v("OHm"), ind(v("OHB"), v("QTu")))
        if t == 0:
            tt(v("QLf"), last, v("DQ"), OP.min)
            ts(v("QLu"), v("QLf"), P - 1, OP.add)
            tt(v("LN"), ind(v("L", 0, 320), v("QTu")), v("OHm"), OP.subtract)
            tc(ind(v("L"), v("QLu")), v("LN"))
        lin(v("PIm", 288 * t, P), v("PIf", 288 * t, P), None, -1904.0)
        tt(v("PGh"), ind(v("PIm"), v("QTu")), v("OHm"), OP.mult)
        ts(v("t24", 0, 8), last, 0, OP.is_gt)
        tt(v("DMh"), v("t24", 0, 8), v("DM"), OP.mult)
        mm(*([(v("PB", 0, 8), v("IDh"), v("DMh"), True, False)] + [(v("PB", 0, 8), v("UF", 15 - k, 143 - k), v("PGh", k, 128, 16), False, k == 15) for k in range(16)]))
        ts(v("MVL"), v("PB", 0, 8), 1904, OP.add)
        tc(ind(v("X0"), v("MVL")), v("MVV%d" % t))
        mm((v("PB", 0, 16), v("RC"), v("MV%d" % t, 112, 128), True, True), (v("PB", 16, 32), v("BOh"), v("PGh", 112, 128), True, True))
        a = 16 * t
        act(v("exo"), v("PB", 0, 16), AF.Sign)
        if t == 0:
            act(v("E32", 0, 16), v("PB", 0, 16), AF.Relu, -257.0)
        act(v("E32", 16, 32), v("PB", 16, 32), AF.Identity, 1904.0)
        ts(v("D1", 6, 128, 8), v("exo"), -1, OP.mult, 1, OP.add)
        tt(v("ROo"), v("RO"), v("exo"), OP.mult)
        tt(v("E32", a, 32), v("E32", a, 32), v("CSf", a, 32), OP.subtract)
        tt(v("E32", a, 32), v("E32", a, 32), v("RO", a, 32), OP.mult)
        tt(v("CSo", a, 32), v("E32", a, 32), v("CSf", a, 32), OP.add)
        if t == 0:
            mm(*[(v("PB", 0, 16), v("BO"), v(x), x == "GS", x == "ROo") for x in ("GS", "ROo")],
               *[(v("PB", 16, 32), v(w), v(x), i == 0, i == 3) for i, (w, x) in enumerate((("IDL", "GS"), ("IDL", "RO"), ("ID", "GS"), ("ID", "ROo")))])
            act(v("T3"), v("PB", 0, 16), AF.Identity, -11.0 * 8192, 8192.0)
            act(v("T2"), v("PB", 16, 32), AF.Identity, -2.0 ** 23)
        ms(v("PX", 0, 128), 0)

    def land(t):
        P, n = 288 + 16 * t, v("nn", 6, 128, 8)
        nx, a0 = ("XA", 0) if t else ("X1", 3584)
        mm(*[(v("PX", o, 128, 8), v("RN"), v(nx, a0 + 16 * o, a0 + 16 * o + 16), True, True) for o in range(7)])
        scan(v("nn"), v("PX", 0, 128), v("D1"), 0.0, OP.min, OP.mult)
        if t == 0:
            tt(v("F1", P, P + 16), n, v("T3"), OP.is_lt)
            tt(v("L", P, P + 16), n, v("T2"), OP.is_lt)
        ts(v("iw"), n, 4095, OP.bitwise_and)
        tt(v("xw"), v("iw"), v("RO"), OP.mult)
        tt(v("PIf", P, P + 16), v("xw"), v("SPo"), OP.max)
        if t == 0:
            tt(v("CPf", P, P + 16), v("xw"), v("CSo"), OP.add)
        tt(v("WN"), ind(v("nn"), v("K86", 0, 7)), v("ZC%d" % t), OP.is_equal)
        tt(v("WN"), v("WN"), v("FD"), OP.mult)

    tc(v("PU", 0, 288), v("POI"))
    tc(v("PIf", 0, 288), v("POI"))
    tc(v("ABU"), v("ABI", 0, 224))
    phase(2, lambda a, b: lin(v("H", 16 * a, 16 * b), ind(v("X0", 0, 3584), v("PU", a, b))), chunks(0, 288, CHH))
    for a, b in ((0, 144), (144, 216), (216, 288)):
        by_row("PA", "UH", "H", a, b)
    tt(v("L", 0, 288), v("PA", 0, 288), v("SLOT"), OP.is_equal)
    ts(v("AI"), v("ABI", 224, 448), 8, OP.arith_shift_right)
    ts(v("AJ"), v("ABI", 224, 448), 255, OP.bitwise_and)
    ts(v("A2", 0, 224), v("AI"), 1, OP.add, 256, OP.mult)
    ts(v("A2", 224, 448), v("AJ"), 1, OP.add, 256, OP.mult)
    mm(*[(v("PB", 64 * q + 16 * j, 64 * q + 16 * j + 16, 1, 0, 112), v("A2", j, 448, 4), v("ID", 16 * q, 16 * q + 16), True, True) for q in range(8) for j in range(4)])
    lin(v("S3", 0, 512, 1, 0, 112), v("PB", 0, 512, 1, 0, 112))
    dma("s", [(v("XB", 0, 3584, 1, 16 * q + 14, 16 * q + 16), v("S3", 64 * q, 64 * q + 64, 1, 0, 112)) for q in range(8)], DS3)
    i = len(ops) - 2
    for x in ([(v("CE", 0, 288), v("cen")), (v("NEI", 0, 288), v("near"))], [(v("TAB0", a, b), v("TAB0", 0, 896)) for a, b in chunks(896, 2688, 896)],
              [(v("TAB1", a, b), v("TAB0", 0, 896)) for a, b in chunks(0, 2688, 896)]):
        dma("s", x, 4000)
        ops[-1]["pre"].append(i)
    tc(v("NU", 0, 288), v("NEI", 0, 288))
    full(0, 0, 288)
    count(0, 0, 304, 0, "ONE")
    numbers(0, v("acc", 0, 1), 304.0)
    absorb("X1", v("X0", 0, 3808), "ABU", "XB", 224, KA[0])
    split(0)
    phase(2, lambda a, b: lin(v("V", 16 * a, 16 * b), ind(v("X1", 0, 3584), v("PU", a, b))), chunks(0, 288))
    keys_open(0)
    parted(0)
    gains(0, "CE", "MC", 0)
    near(0)
    gains(0, "BQ", "MB", 1)
    long(*[(v("PN", 0, 288), v("UC", 15 - m, 143 - m), v("V", m, 4608, 16), m == 0, m == 15) for m in range(16)], n=2)
    ts(v("CPf", 0, 288), v("PN", 0, 288), -257, OP.add)
    tc(v("CU", 0, 288), v("CPf", 0, 288))
    centres()
    pick(0)
    own(0)
    full(1, 0, 288)
    count(1, 0, 288, 1, "ONE")
    ts(v("acc", 2, 3), v("acc", 1, 2), 320, OP.add)
    land(0)
    ts(v("X0", 3584, 3696), v("WN"), col(B255), OP.add)
    count(1, 288, 320, 3, "F1")
    numbers(1, v("acc", 3, 4), v("acc", 2, 3))
    tc(v("PU", 288, 304), v("PIf", 288, 304))
    tc(v("CU", 288, 304), v("CPf", 288, 304))
    dma("s", [(v("ypost", 0, 304), v("PIf", 0, 304))])
    dma("s", [(v("ya", 0, 112), v("X1", 3584, 3696))])
    split(1)
    parted(1)
    lin(v("V", 4608, 4864), ind(v("X1"), v("PU", 288, 304)), None, col(K256))
    absorb("W", v("X1"), "CU", "V", 304, KA[1])
    keys_open(1)
    gains(1, "CE", "MC", 0)
    near(1)
    gains(1, "BQ", "MB", 1)
    pick(1)
    own(1)
    dma("s", [(v("yh", 0, 3584, 1, 0, 16, 2), v("X0", 0, 3584, 1, 14, 128, 16))])
    dma("a", [(v("yh", 0, 3584, 1, 1, 16, 2), v("X0", 0, 3584, 1, 15, 128, 16))])
    dma("s", [(v("ya", 0, 112, 1, i, 128, 16), v("X0", 3584, 3696, 1, i, 128, 16)) for i in (14, 15)])
    lin(v("XM"), v("XA"), col(C13), col(B255))
    land(1)
    dma("s", [(v("ypost", 304, 320), v("PIf", 304, 320))])
    tt(v("YA", 112, 224), v("XM"), v("WN"), OP.add)
    dma("a", [(v("ya", 112, 224), v("YA", 112, 224))])

    shape = tuple(tuple(o["pre"]) for o in ops)
    if shape not in _ORDER:
        _ORDER[shape] = arrange([o["pre"] for o in ops], [o["lat"] for o in ops], [{e: c for e, (f, c) in o["alt"].items()} for o in ops], [o.get("more", 0) for o in ops])
    for o, x in zip(ops, _ORDER[shape]):
        o["start"], o["eng"] = x[0], x[2]
    know = {e: {} for e in E}

    def waits(e, need):
        for s, n, k in sorted(need, key=lambda z: -len(z[2])):
            if know[e].get(s, 0) < n:
                E[e].wait_ge(T.sem[s], n)
                for a, b in list(k.items()) + [(s, n)]:
                    know[e][a] = max(know[e].get(a, 0), b)

    for o in sorted(ops, key=lambda z: z["start"]):
        e = o["eng"]
        if e == "n":
            o["done"] = (o["sem"], cnt[o["sem"]], {})
            continue
        waits(e, [ops[p]["done"] for p in o["pre"] if not e == "t" == ops[p]["eng"]])
        s = o["sem"] or "c" + e
        for x in o["alt"][e][0]():
            x.then_inc(T.sem[s], 16 if o["sem"] else 1)
            cnt[s] = cnt.get(s, 0) + (16 if o["sem"] else 1)
        o["done"] = (s, cnt.get(s, 0), dict(know[e]))
    waits("g", [(s, n, {}) for s, n in cnt.items() if n])
